import numpy as np
import ml_dtypes


def mxq(x, axis, fmt="e4m3"):
    dtype, down = {"e4m3": (ml_dtypes.float8_e4m3fn, 7), "e5m2": (ml_dtypes.float8_e5m2, 14)}[fmt]
    v = np.moveaxis(np.asarray(x, np.float32).astype(ml_dtypes.bfloat16).astype(np.float64), axis, -1)
    blocks = v.reshape(v.shape[:-1] + (-1, 32))
    amax = np.abs(blocks).max(-1, keepdims=True)
    byte = np.maximum(np.where(amax > 0, np.frexp(amax)[1] - 1 + 127, 0) - down, 1)
    scale = np.exp2(byte - 127.0)
    codes = (blocks / scale).astype(np.float32).astype(dtype).astype(np.float64)
    return np.moveaxis((codes * scale).reshape(v.shape), -1, axis)


WIDE = False


def mx_kscale(k):
    if not WIDE:
        return np.ones(k)
    levels = np.array([10, -10, 5, -5, 0])
    if k % 512:
        return np.exp2(np.random.permutation(np.resize(levels, k // 32))).repeat(32)
    a = np.empty((k // 512, 16))
    for p in range(k // 512):
        a[p, :8] = np.random.permutation(np.resize(levels, 8))
        for g in range(8):
            far = levels[np.abs(levels - a[p, g]) >= 10]
            a[p, g + 8] = far[np.random.randint(len(far))]
    return np.exp2(a.ravel()).repeat(32)


def f64(x):
    return np.asarray(x).astype(np.float64)


def striped(idx):
    return np.tile(np.asarray(idx).reshape(-1, 16).T, (8, 1)).astype(np.uint16)


def unstriped(offs):
    return offs[:16].T.reshape(-1).astype(np.int64)


B, N, T, D, DV, NQ = 2, 512, 2048, 512, 512, 128
PAGE = 64


def setup_inputs():
    n = np.random.standard_normal
    pages = np.random.permutation(T // PAGE)[:B * N // PAGE]
    idx = (pages[:, None] * PAGE + np.arange(PAGE)[None, :]).reshape(-1)
    s = mx_kscale(D)[:, None]
    u = np.ones(T)
    u[idx] = mx_kscale(B * N)
    r = np.random.uniform(0.5, 2.0, T)
    raw = n((D, T)) / s / (u * r)
    return {
        "qT": (n((B, D, NQ)) * s * (1.00 / np.sqrt(D))).astype(np.float32),
        "cT": raw.astype(np.float32),
        "ts": np.tile(u * r, (128, 1)).astype(np.float32),
        "sink": (2.0 + 3.0 * n((B, NQ, 1))).astype(np.float32),
        "ch": np.tile(s[:, 0] * np.random.uniform(0.5, 2.0, D), (128, 1)).astype(np.float32),
        "offs": striped(idx),
    }


def reference(qT, cT, ts, sink, ch, offs):
    idx = unstriped(offs)
    c = f64(cT)
    pick = lambda x: x[:, idx].reshape(x.shape[0], B, N).transpose(1, 0, 2)
    q = f64(qT)
    score = mxq(q, 1, "e4m3").transpose(0, 2, 1) @ mxq(pick(c), 1, "e4m3")
    score = score * pick(f64(ts))[:, :1, :]
    m = np.maximum(score.max(-1, keepdims=True), f64(sink))
    p = np.exp(score - m)
    total = p.sum(-1, keepdims=True) + np.exp(f64(sink) - m)
    w = p * pick(f64(ts))[:, :1, :]
    y = mxq(w, 2, "e4m3") @ mxq(pick(c).transpose(0, 2, 1), 1, "e4m3")
    y = y / total
    y = y * f64(ch)[:1]
    return y

@@ -1,0 +1,299 @@
+from contextlib import ExitStack
+
+import concourse.mybir as mybir
+from concourse.masks import make_identity
+
+B, N, T, D, NQ = 2, 512, 2048, 512, 128
+P = 128
+H = N // 2
+FLOPS = 4 * B * N * D * NQ
+
+F32 = mybir.dt.float32
+BF16 = mybir.dt.bfloat16
+U32 = mybir.dt.uint32
+U16 = mybir.dt.uint16
+U8 = mybir.dt.uint8
+FP8X4 = mybir.dt.float8_e4m3fn_x4
+MULT = mybir.AluOpType.mult
+ADD = mybir.AluOpType.add
+MIN = mybir.AluOpType.min
+EXP = mybir.ActivationFunctionType.Exp
+AX = mybir.AxisListType.X
+
+
+def tile_attend_x_mla_sink_kernel(tc, qT, cT, ts, sink, ch, offs, out):
+    nc = tc.nc
+    with ExitStack() as ctx:
+        lists = ctx.enter_context(tc.tile_pool(name="lists", bufs=1))
+        keep = ctx.enter_context(tc.tile_pool(name="keep", bufs=1))
+        psum = ctx.enter_context(tc.psum_pool(name="psum", bufs=1))
+
+        def sb(shape, dtype, name):
+            return keep.tile(shape, dtype, name=name, align_bytes=64)
+
+        def slot(shape, name, k):
+            return keep.tile(shape, F32, name=name, tag=f"r{k}", bufs=1, align_bytes=64)
+
+        def bank(name):
+            return psum.tile([P, 512], F32, name=name, tag="x", bufs=4)
+
+        def half_bank(name, b, h):
+            return psum.tile([P, 512], F32, name=name, tag=f"s{b}{h}", bufs=1)
+
+        offsets = lists.tile([P, B * N // 16], U16, name="offsets")
+        nc.sync.dma_start(offsets[:], offs)
+        ident = sb([P, P], F32, "ident")
+        make_identity(nc, ident[:])
+        sink_sb = sb([P, B], F32, "sink_sb")
+        nc.scalar.dma_start(out=sink_sb[:], in_=sink.rearrange("b q o -> q (b o)"))
+
+        cv = cT.rearrange("(p t) c -> p t c", t=4)
+        planes = []
+        for t in range(4):
+            pl = slot([P, T], f"plane{t}", t)
+            nc.sync.dma_start(out=pl[:], in_=cv[:, t, :])
+            planes.append(pl)
+
+        warm = sb([P, 1], F32, "warm")
+        nc.gpsimd.memset(warm[:], 0.0)
+        nc.scalar.activation(out=warm[:], in_=warm[:], func=EXP)
+
+        na = [sb([P, 516], F32, f"na{b}") for b in range(B)]
+        for b in range(B):
+            nc.gpsimd.memset(na[b][:, 512:516], 2.0 ** 126)
+            nc.gpsimd.tensor_scalar(out=na[b][:, 512:513], in0=sink_sb[:, b:b + 1], scalar1=-1.0, scalar2=0.0, op0=MULT, op1=ADD)
+        nm = [sb([P, 1], F32, f"nm{b}") for b in range(B)]
+        l2 = [sb([P, 2], F32, f"l2_{b}") for b in range(B)]
+        rl = [sb([P, 1], F32, f"rl{b}") for b in range(B)]
+        g = sb([P, 4, B * N], F32, "g")
+        vb = [sb([P, B * N], BF16, f"vb{t}") for t in range(4)]
+        vt = [sb([P, 2, 4, 64, 4], BF16, f"vt{b}") for b in range(B)]
+        vtw = [v[:].rearrange("m h t p s -> m (h t p s)").bitcast(F32).rearrange("m (h t p u) -> m h t p u", h=2, t=4, u=2) for v in vt]
+        vq = [sb([P, D], U32, f"vq{b}") for b in range(B)]
+        vs = [sb([P, D], U8, f"vs{b}") for b in range(B)]
+        tsg = sb([P, B * N], F32, "tsg")
+        ts4 = [sb([P, 4], F32, f"ts4_{b}") for b in range(B)]
+        qi = [sb([P, NQ, 4], BF16, f"qi{b}") for b in range(B)]
+        qq = [sb([P, NQ], U32, f"qq{b}") for b in range(B)]
+        qs = [sb([P, NQ], U8, f"qs{b}") for b in range(B)]
+        ki = [[sb([P, H, 4], BF16, f"ki{b}_{h}") for h in range(2)] for b in range(B)]
+        kq = [sb([P, N], U32, f"kq{b}") for b in range(B)]
+        ks = [sb([P, N], U8, f"ks{b}") for b in range(B)]
+        p = [sb([P, 4, 129], F32, f"p{b}") for b in range(B)]
+        wi = [sb([P, NQ, 4], BF16, f"wi{b}") for b in range(B)]
+        wq = [sb([P, NQ], U32, f"wq{b}") for b in range(B)]
+        ws = [sb([P, NQ], U8, f"ws{b}") for b in range(B)]
+        o = [sb([P, D], F32, f"o{b}") for b in range(B)]
+        qraw = [None, None]
+        tile = {}
+
+        def copy(eng, out, in_):
+            if eng == "A":
+                nc.scalar.copy(out=out, in_=in_)
+            elif eng == "D":
+                nc.vector.tensor_copy(out=out, in_=in_)
+            else:
+                nc.gpsimd.tensor_scalar(out=out, in0=in_, scalar1=1.0, scalar2=0.0, op0=MULT, op1=ADD)
+
+        def load_q(b, k):
+            qraw[b] = slot([P, 4, NQ], f"qraw{b}", k)
+            nc.sync.dma_start(out=qraw[b][:], in_=qT[b].rearrange("(p t) q -> p t q", t=4))
+
+        def load_ch():
+            tile["ch"] = slot([P, D], "ch_sb", 3)
+            nc.sync.dma_start(out=tile["ch"][:], in_=ch)
+
+        def load_ts(k):
+            tile["ts"] = slot([P, T], "tsw", k)
+            nc.sync.dma_start(out=tile["ts"][:], in_=ts)
+
+        def ts_gather(b):
+            nc.vector.tensor_copy(tsg[:, b * N:(b + 1) * N], tile["ts"][:].indirect(offsets[:, b * 32:(b + 1) * 32]))
+
+        def ts4_turn(b):
+            tile["t4", b] = bank("tps")
+            for s in range(4):
+                nc.tensor.transpose(tile["t4", b][:, s * P:(s + 1) * P], tsg[:, b * N + s:(b + 1) * N:4], ident[:])
+
+        def ts4_out(b):
+            nc.scalar.copy(out=ts4[b][:], in_=tile["t4", b][:, 0:512:P])
+
+        def gather(t):
+            nc.vector.tensor_copy(g[:, t, :], planes[t][:].indirect(offsets[:]))
+
+        def gather3(b, h):
+            k = 2 * b + h
+            nc.vector.tensor_copy(g[:, 3, k * H:(k + 1) * H], planes[3][:].indirect(offsets[:, k * 16:(k + 1) * 16]))
+
+        def cast(t, eng):
+            copy(eng, vb[t][:], g[:, t, :])
+
+        def turn(t):
+            words = vb[t][:].bitcast(F32)
+            tile["v", t] = bank("vps")
+            for b in range(B):
+                for u in range(2):
+                    k = 2 * b + u
+                    nc.tensor.transpose(tile["v", t][:, k * P:(k + 1) * P], words[:, b * H + u:(b + 1) * H:2], ident[:])
+
+        def values(t, b):
+            nc.scalar.copy(out=vtw[b][:, :, t, :, :],
+                           in_=tile["v", t][:, b * 2 * P:(b + 1) * 2 * P].rearrange("m (u h p) -> m h p u", u=2, h=2))
+
+        def quant_values(h, b):
+            cols = slice(h * H, (h + 1) * H)
+            nc.vector.quantize_mx(out=vq[b][:, cols].bitcast(FP8X4), scales=vs[b][:, cols],
+                                  in_=vt[b][:, h].rearrange("m t p s -> m (t p s)"))
+
+        def query(b, eng):
+            copy(eng, qi[b][:], qraw[b][:].rearrange("p t q -> p q t"))
+
+        def quant_query(b):
+            nc.vector.quantize_mx(out=qq[b][:].bitcast(FP8X4), scales=qs[b][:], in_=qi[b][:].rearrange("p q t -> p (q t)"))
+
+        def keys(b, h, eng):
+            lo = b * N + h * H
+            copy(eng, ki[b][h][:], g[:, :, lo:lo + H].rearrange("p t s -> p s t"))
+
+        def quant_keys(b, h):
+            hc = slice(h * H, (h + 1) * H)
+            nc.vector.quantize_mx(out=kq[b][:, hc].bitcast(FP8X4), scales=ks[b][:, hc],
+                                  in_=ki[b][h][:].rearrange("p s t -> p (s t)"))
+
+        def scores(b, h):
+            hc = slice(h * H, (h + 1) * H)
+            tile["s", b, h] = half_bank(f"sps{b}{h}", b, h)
+            nc.tensor.matmul_mx(tile["s", b, h][:, 0:H], lhsT=qq[b][:].bitcast(FP8X4), lhsT_scale=qs[b][:],
+                                rhs=kq[b][:, hc].bitcast(FP8X4), rhs_scale=ks[b][:, hc], start=True, stop=True)
+
+        def scaled(b, h):
+            hc = slice(h * H, (h + 1) * H)
+            nc.vector.scalar_tensor_tensor(out=na[b][:, hc], in0=tile["s", b, h][:, 0:H], scalar=-1.0,
+                                           in1=tsg[:, b * N + h * H:b * N + (h + 1) * H], op0=MULT, op1=MULT)
+
+        def row_min(b):
+            nc.vector.tensor_reduce(out=nm[b][:], in_=na[b][:, 0:N + 1], axis=AX, op=MIN)
+
+        def expo(b, i):
+            nc.scalar.activation(out=p[b][:, 2 * i:2 * i + 2, :].rearrange("q s m -> q m s"),
+                                 in_=na[b][:].rearrange("q (m s) -> q m s", s=4)[:, :, 2 * i:2 * i + 2],
+                                 func=EXP, bias=nm[b][:], scale=-1.0, accum_out=l2[b][:, i:i + 1])
+
+        def turn_p(b, i):
+            if ("p", b) not in tile:
+                tile["p", b] = bank("pps")
+            for s in (2 * i, 2 * i + 1):
+                nc.tensor.transpose(tile["p", b][:, s * P:(s + 1) * P], p[b][:, s, 0:P], ident[:])
+
+        def weights(b):
+            nc.vector.tensor_tensor(out=wi[b][:], in0=tile["p", b][:].rearrange("m (s q) -> m q s", s=4),
+                                    in1=ts4[b][:].unsqueeze(1).to_broadcast([P, NQ, 4]), op=MULT)
+
+        def quant_weights(b):
+            nc.vector.quantize_mx(out=wq[b][:].bitcast(FP8X4), scales=ws[b][:], in_=wi[b][:].rearrange("m q s -> m (q s)"))
+
+        def recip(b):
+            nc.vector.tensor_tensor(out=rl[b][:], in0=l2[b][:, 0:1], in1=l2[b][:, 1:2], op=ADD)
+            nc.vector.reciprocal(out=rl[b][:], in_=rl[b][:])
+
+        def product(b, h):
+            cols = slice(h * H, (h + 1) * H)
+            tile["y", b, h] = half_bank(f"yps{b}{h}", b, h)
+            nc.tensor.matmul_mx(tile["y", b, h][:, 0:H], lhsT=wq[b][:].bitcast(FP8X4), lhsT_scale=ws[b][:],
+                                rhs=vq[b][:, cols].bitcast(FP8X4), rhs_scale=vs[b][:, cols], start=True, stop=True)
+
+        def epilogue(b, h):
+            cols = slice(h * H, (h + 1) * H)
+            nc.vector.scalar_tensor_tensor(
+                out=o[b][:, cols].rearrange("q (p t) -> q p t", t=4), in0=tile["y", b, h][:, 0:H].rearrange("q (t p) -> q p t", t=4),
+                scalar=rl[b][:], in1=tile["ch"][:, cols].rearrange("q (p t) -> q p t", t=4), op0=MULT, op1=MULT)
+
+        def store(b, h):
+            cols = slice(h * H, (h + 1) * H)
+            nc.sync.dma_start(out=out[b][:, cols], in_=o[b][:, cols])
+
+        gather(0)
+        gather(1)
+        gather(2)
+        gather3(0, 0)
+        load_q(0, 0)
+        cast(1, "A")
+        load_q(1, 1)
+        gather3(0, 1)
+        query(0, "D")
+        cast(0, "A")
+        turn(0)
+        keys(0, 0, "A")
+        gather3(1, 0)
+        load_ts(2)
+        query(1, "D")
+        keys(0, 1, "A")
+        gather3(1, 1)
+        quant_keys(0, 0)
+        quant_query(0)
+        cast(2, "A")
+        keys(1, 1, "D")
+        keys(1, 0, "A")
+        quant_keys(0, 1)
+        ts_gather(0)
+        quant_keys(1, 1)
+        scores(0, 1)
+        quant_keys(1, 0)
+        quant_query(1)
+        scores(0, 0)
+        turn(1)
+        scaled(0, 1)
+        load_ch()
+        scores(1, 0)
+        turn(2)
+        ts4_turn(0)
+        scores(1, 1)
+        scaled(0, 0)
+        ts_gather(1)
+        values(0, 0)
+        scaled(1, 0)
+        scaled(1, 1)
+        row_min(0)
+        expo(0, 0)
+        cast(3, "A")
+        values(2, 0)
+        row_min(1)
+        values(1, 1)
+        turn(3)
+        values(1, 0)
+        ts4_turn(1)
+        values(3, 0)
+        quant_values(1, 0)
+        expo(1, 1)
+        ts4_out(0)
+        quant_values(0, 0)
+        turn_p(0, 0)
+        values(0, 1)
+        values(2, 1)
+        turn_p(1, 1)
+        expo(0, 1)
+        values(3, 1)
+        expo(1, 0)
+        ts4_out(1)
+        turn_p(0, 1)
+        recip(1)
+        quant_values(0, 1)
+        weights(0)
+        quant_weights(0)
+        turn_p(1, 0)
+        quant_values(1, 1)
+        weights(1)
+        quant_weights(1)
+        product(1, 0)
+        product(0, 0)
+        product(1, 1)
+        epilogue(1, 1)
+        epilogue(1, 0)
+        store(1, 1)
+        product(0, 1)
+        store(1, 0)
+        recip(0)
+        epilogue(0, 0)
+        store(0, 0)
+        epilogue(0, 1)
+        store(0, 1)

@@ -15,8 +15,7 @@ U16 = mybir.dt.uint16
 U8 = mybir.dt.uint8
 FP8X4 = mybir.dt.float8_e4m3fn_x4
 MULT = mybir.AluOpType.mult
-ADD = mybir.AluOpType.add
-MIN = mybir.AluOpType.min
+MAX = mybir.AluOpType.max
 EXP = mybir.ActivationFunctionType.Exp
 AX = mybir.AxisListType.X
 
@@ -37,15 +36,14 @@ def tile_attend_x_mla_sink_kernel(tc, qT, cT, ts, sink, ch, offs, out):
         def bank(name):
             return psum.tile([P, 512], F32, name=name, tag="x", bufs=4)
 
-        def half_bank(name, b, h):
-            return psum.tile([P, 512], F32, name=name, tag=f"s{b}{h}", bufs=1)
+        def seq_bank(name, b):
+            return psum.tile([P, 512], F32, name=name, tag=f"s{b}", bufs=2)
 
         offsets = lists.tile([P, B * N // 16], U16, name="offsets")
         nc.sync.dma_start(offsets[:], offs)
-        ident = sb([P, P], F32, "ident")
-        make_identity(nc, ident[:])
-        sink_sb = sb([P, B], F32, "sink_sb")
-        nc.scalar.dma_start(out=sink_sb[:], in_=sink.rearrange("b q o -> q (b o)"))
+        tsw = sb([P, T], F32, "tsw")
+        nc.sync.dma_start(out=tsw[P - 1:P, :], in_=ts[0:1, :])
+        nc.vector.memset(tsw[0:P - 1, :], 0.0)
 
         cv = cT.rearrange("(p t) c -> p t c", t=4)
         planes = []
@@ -54,136 +52,128 @@ def tile_attend_x_mla_sink_kernel(tc, qT, cT, ts, sink, ch, offs, out):
             nc.sync.dma_start(out=pl[:], in_=cv[:, t, :])
             planes.append(pl)
 
+        a = sb([P, B, 520], F32, "a")
+        nc.sync.dma_start(out=a[:, :, N:N + 1], in_=sink.rearrange("b q o -> q b o"))
+
+        ident = sb([P, P], F32, "ident")
+        make_identity(nc, ident[:])
         warm = sb([P, 1], F32, "warm")
         nc.gpsimd.memset(warm[:], 0.0)
         nc.scalar.activation(out=warm[:], in_=warm[:], func=EXP)
 
-        na = [sb([P, 516], F32, f"na{b}") for b in range(B)]
-        for b in range(B):
-            nc.gpsimd.memset(na[b][:, 512:516], 2.0 ** 126)
-            nc.gpsimd.tensor_scalar(out=na[b][:, 512:513], in0=sink_sb[:, b:b + 1], scalar1=-1.0, scalar2=0.0, op0=MULT, op1=ADD)
         nm = [sb([P, 1], F32, f"nm{b}") for b in range(B)]
-        l2 = [sb([P, 2], F32, f"l2_{b}") for b in range(B)]
+        lsum = [sb([P, 1], F32, f"lsum{b}") for b in range(B)]
         rl = [sb([P, 1], F32, f"rl{b}") for b in range(B)]
-        g = sb([P, 4, B * N], F32, "g")
-        vb = [sb([P, B * N], BF16, f"vb{t}") for t in range(4)]
-        vt = [sb([P, 2, 4, 64, 4], BF16, f"vt{b}") for b in range(B)]
-        vtw = [v[:].rearrange("m h t p s -> m (h t p s)").bitcast(F32).rearrange("m (h t p u) -> m h t p u", h=2, t=4, u=2) for v in vt]
+        g = sb([P, 4 * B * N], BF16, "g")
+        vt23 = sb([P, 2 * B * N], BF16, "vt23")
         vq = [sb([P, D], U32, f"vq{b}") for b in range(B)]
         vs = [sb([P, D], U8, f"vs{b}") for b in range(B)]
         tsg = sb([P, B * N], F32, "tsg")
         ts4 = [sb([P, 4], F32, f"ts4_{b}") for b in range(B)]
+        tsb = [sb([P, N], F32, f"tsb{b}") for b in range(B)]
         qi = [sb([P, NQ, 4], BF16, f"qi{b}") for b in range(B)]
         qq = [sb([P, NQ], U32, f"qq{b}") for b in range(B)]
         qs = [sb([P, NQ], U8, f"qs{b}") for b in range(B)]
         ki = [[sb([P, H, 4], BF16, f"ki{b}_{h}") for h in range(2)] for b in range(B)]
         kq = [sb([P, N], U32, f"kq{b}") for b in range(B)]
         ks = [sb([P, N], U8, f"ks{b}") for b in range(B)]
-        p = [sb([P, 4, 129], F32, f"p{b}") for b in range(B)]
+        p = [sb([P, N + 1], F32, f"p{b}") for b in range(B)]
         wi = [sb([P, NQ, 4], BF16, f"wi{b}") for b in range(B)]
         wq = [sb([P, NQ], U32, f"wq{b}") for b in range(B)]
         ws = [sb([P, NQ], U8, f"ws{b}") for b in range(B)]
         o = [sb([P, D], F32, f"o{b}") for b in range(B)]
-        qraw = [None, None]
         tile = {}
 
-        def copy(eng, out, in_):
-            if eng == "A":
-                nc.scalar.copy(out=out, in_=in_)
-            elif eng == "D":
-                nc.vector.tensor_copy(out=out, in_=in_)
-            else:
-                nc.gpsimd.tensor_scalar(out=out, in0=in_, scalar1=1.0, scalar2=0.0, op0=MULT, op1=ADD)
+        def plane_cols(t):
+            return g[:, t * B * N:(t + 1) * B * N]
 
-        def load_q(b, k):
-            qraw[b] = slot([P, 4, NQ], f"qraw{b}", k)
-            nc.sync.dma_start(out=qraw[b][:], in_=qT[b].rearrange("(p t) q -> p t q", t=4))
+        def vt(t):
+            return plane_cols(t + 2) if t < 2 else vt23[:, (t - 2) * B * N:(t - 1) * B * N]
+
+        def interleave(eng, dst, src):
+            copy = nc.scalar.copy if eng == "A" else nc.vector.tensor_copy
+            copy(out=dst.rearrange("p (c i) t -> p c t i", i=4), in_=src.rearrange("p t (c i) -> p c t i", i=4))
+
+        def load_q():
+            tile["q"] = slot([P, B, 4, NQ], "qraw", 1)
+            for b in range(B):
+                nc.sync.dma_start(out=tile["q"][:, b], in_=qT[b].rearrange("(p t) q -> p t q", t=4))
 
         def load_ch():
             tile["ch"] = slot([P, D], "ch_sb", 3)
             nc.sync.dma_start(out=tile["ch"][:], in_=ch)
 
-        def load_ts(k):
-            tile["ts"] = slot([P, T], "tsw", k)
-            nc.sync.dma_start(out=tile["ts"][:], in_=ts)
-
-        def ts_gather(b):
-            nc.vector.tensor_copy(tsg[:, b * N:(b + 1) * N], tile["ts"][:].indirect(offsets[:, b * 32:(b + 1) * 32]))
-
-        def ts4_turn(b):
-            tile["t4", b] = bank("tps")
-            for s in range(4):
-                nc.tensor.transpose(tile["t4", b][:, s * P:(s + 1) * P], tsg[:, b * N + s:(b + 1) * N:4], ident[:])
-
-        def ts4_out(b):
-            nc.scalar.copy(out=ts4[b][:], in_=tile["t4", b][:, 0:512:P])
+        def ts_road():
+            nc.vector.tensor_copy(tsg[:], tsw[:].indirect(offsets[:]))
+            for b in range(B):
+                cols = bank("tps")
+                for s in range(4):
+                    nc.tensor.transpose(cols[:, s * P:(s + 1) * P], tsg[:, b * N + s:(b + 1) * N:4], ident[:])
+                nc.scalar.copy(out=ts4[b][:], in_=cols[:, P - 1:512:P])
+            for b in range(B):
+                rows = bank("tbs")
+                for s in range(4):
+                    nc.tensor.transpose(rows[:, s * P:(s + 1) * P], ts4[b][:, s:s + 1].to_broadcast([P, P]), ident[:])
+                nc.scalar.copy(out=tsb[b][:], in_=rows[:])
 
         def gather(t):
-            nc.vector.tensor_copy(g[:, t, :], planes[t][:].indirect(offsets[:]))
+            nc.vector.tensor_copy(plane_cols(t), planes[t][:].indirect(offsets[:]))
 
-        def gather3(b, h):
-            k = 2 * b + h
-            nc.vector.tensor_copy(g[:, 3, k * H:(k + 1) * H], planes[3][:].indirect(offsets[:, k * 16:(k + 1) * 16]))
-
-        def cast(t, eng):
-            copy(eng, vb[t][:], g[:, t, :])
+        def gather_seq(t, b):
+            nc.vector.tensor_copy(plane_cols(t)[:, b * N:(b + 1) * N], planes[t][:].indirect(offsets[:, b * 32:(b + 1) * 32]))
 
         def turn(t):
-            words = vb[t][:].bitcast(F32)
+            words = plane_cols(t).bitcast(F32)
             tile["v", t] = bank("vps")
             for b in range(B):
                 for u in range(2):
                     k = 2 * b + u
                     nc.tensor.transpose(tile["v", t][:, k * P:(k + 1) * P], words[:, b * H + u:(b + 1) * H:2], ident[:])
 
-        def values(t, b):
-            nc.scalar.copy(out=vtw[b][:, :, t, :, :],
-                           in_=tile["v", t][:, b * 2 * P:(b + 1) * 2 * P].rearrange("m (u h p) -> m h p u", u=2, h=2))
+        def values(t):
+            nc.scalar.copy(out=vt(t).bitcast(F32).rearrange("m (b p u) -> m b p u", b=B, u=2),
+                           in_=tile["v", t][:].rearrange("m (b u p) -> m b p u", b=B, u=2))
 
-        def quant_values(h, b):
-            cols = slice(h * H, (h + 1) * H)
-            nc.vector.quantize_mx(out=vq[b][:, cols].bitcast(FP8X4), scales=vs[b][:, cols],
-                                  in_=vt[b][:, h].rearrange("m t p s -> m (t p s)"))
+        def quant_values(t):
+            cols = slice(t * P, (t + 1) * P)
+            for b in range(B):
+                nc.vector.quantize_mx(out=vq[b][:, cols].bitcast(FP8X4), scales=vs[b][:, cols], in_=vt(t)[:, b * N:(b + 1) * N])
 
         def query(b, eng):
-            copy(eng, qi[b][:], qraw[b][:].rearrange("p t q -> p q t"))
+            interleave(eng, qi[b][:], tile["q"][:, b])
 
         def quant_query(b):
             nc.vector.quantize_mx(out=qq[b][:].bitcast(FP8X4), scales=qs[b][:], in_=qi[b][:].rearrange("p q t -> p (q t)"))
 
         def keys(b, h, eng):
             lo = b * N + h * H
-            copy(eng, ki[b][h][:], g[:, :, lo:lo + H].rearrange("p t s -> p s t"))
+            interleave(eng, ki[b][h][:], g[:].rearrange("p (t s) -> p t s", t=4)[:, :, lo:lo + H])
 
         def quant_keys(b, h):
             hc = slice(h * H, (h + 1) * H)
             nc.vector.quantize_mx(out=kq[b][:, hc].bitcast(FP8X4), scales=ks[b][:, hc],
                                   in_=ki[b][h][:].rearrange("p s t -> p (s t)"))
 
-        def scores(b, h):
-            hc = slice(h * H, (h + 1) * H)
-            tile["s", b, h] = half_bank(f"sps{b}{h}", b, h)
-            nc.tensor.matmul_mx(tile["s", b, h][:, 0:H], lhsT=qq[b][:].bitcast(FP8X4), lhsT_scale=qs[b][:],
-                                rhs=kq[b][:, hc].bitcast(FP8X4), rhs_scale=ks[b][:, hc], start=True, stop=True)
+        def scores(b):
+            tile["s", b] = seq_bank("sps", b)
+            nc.tensor.matmul_mx(tile["s", b][:], lhsT=qq[b][:].bitcast(FP8X4), lhsT_scale=qs[b][:],
+                                rhs=kq[b][:].bitcast(FP8X4), rhs_scale=ks[b][:], start=True, stop=True)
 
-        def scaled(b, h):
-            hc = slice(h * H, (h + 1) * H)
-            nc.vector.scalar_tensor_tensor(out=na[b][:, hc], in0=tile["s", b, h][:, 0:H], scalar=-1.0,
-                                           in1=tsg[:, b * N + h * H:b * N + (h + 1) * H], op0=MULT, op1=MULT)
+        def scaled(b):
+            nc.vector.tensor_tensor(out=a[:, b, 0:N].rearrange("q (s m) -> q s m", s=4),
+                                    in0=tile["s", b][:].rearrange("q (m s) -> q s m", s=4),
+                                    in1=tsb[b][:].rearrange("q (s m) -> q s m", s=4), op=MULT)
 
-        def row_min(b):
-            nc.vector.tensor_reduce(out=nm[b][:], in_=na[b][:, 0:N + 1], axis=AX, op=MIN)
+        def row_max(b):
+            nc.vector.tensor_reduce(out=nm[b][:], in_=a[:, b, 0:N + 1], axis=AX, op=MAX, negate=True)
 
-        def expo(b, i):
-            nc.scalar.activation(out=p[b][:, 2 * i:2 * i + 2, :].rearrange("q s m -> q m s"),
-                                 in_=na[b][:].rearrange("q (m s) -> q m s", s=4)[:, :, 2 * i:2 * i + 2],
-                                 func=EXP, bias=nm[b][:], scale=-1.0, accum_out=l2[b][:, i:i + 1])
+        def expo(b):
+            nc.scalar.activation(out=p[b][:], in_=a[:, b, 0:N + 1], func=EXP, bias=nm[b][:], scale=1.0, accum_out=lsum[b][:])
 
-        def turn_p(b, i):
-            if ("p", b) not in tile:
-                tile["p", b] = bank("pps")
-            for s in (2 * i, 2 * i + 1):
-                nc.tensor.transpose(tile["p", b][:, s * P:(s + 1) * P], p[b][:, s, 0:P], ident[:])
+        def turn_p(b):
+            tile["p", b] = bank("pps")
+            for s in range(4):
+                nc.tensor.transpose(tile["p", b][:, s * P:(s + 1) * P], p[b][:, s * P:(s + 1) * P], ident[:])
 
         def weights(b):
             nc.vector.tensor_tensor(out=wi[b][:], in0=tile["p", b][:].rearrange("m (s q) -> m q s", s=4),
@@ -193,107 +183,68 @@ def tile_attend_x_mla_sink_kernel(tc, qT, cT, ts, sink, ch, offs, out):
             nc.vector.quantize_mx(out=wq[b][:].bitcast(FP8X4), scales=ws[b][:], in_=wi[b][:].rearrange("m q s -> m (q s)"))
 
         def recip(b):
-            nc.vector.tensor_tensor(out=rl[b][:], in0=l2[b][:, 0:1], in1=l2[b][:, 1:2], op=ADD)
-            nc.vector.reciprocal(out=rl[b][:], in_=rl[b][:])
+            nc.vector.reciprocal(out=rl[b][:], in_=lsum[b][:])
 
-        def product(b, h):
-            cols = slice(h * H, (h + 1) * H)
-            tile["y", b, h] = half_bank(f"yps{b}{h}", b, h)
-            nc.tensor.matmul_mx(tile["y", b, h][:, 0:H], lhsT=wq[b][:].bitcast(FP8X4), lhsT_scale=ws[b][:],
-                                rhs=vq[b][:, cols].bitcast(FP8X4), rhs_scale=vs[b][:, cols], start=True, stop=True)
+        def product(b):
+            tile["y", b] = seq_bank("yps", b)
+            nc.tensor.matmul_mx(tile["y", b][:], lhsT=wq[b][:].bitcast(FP8X4), lhsT_scale=ws[b][:],
+                                rhs=vq[b][:].bitcast(FP8X4), rhs_scale=vs[b][:], start=True, stop=True)
 
-        def epilogue(b, h):
-            cols = slice(h * H, (h + 1) * H)
+        def epilogue(b):
             nc.vector.scalar_tensor_tensor(
-                out=o[b][:, cols].rearrange("q (p t) -> q p t", t=4), in0=tile["y", b, h][:, 0:H].rearrange("q (t p) -> q p t", t=4),
-                scalar=rl[b][:], in1=tile["ch"][:, cols].rearrange("q (p t) -> q p t", t=4), op0=MULT, op1=MULT)
+                out=o[b][:].rearrange("q (p t) -> q p t", t=4), in0=tile["y", b][:].rearrange("q (t p) -> q p t", t=4),
+                scalar=rl[b][:], in1=tile["ch"][:].rearrange("q (p t) -> q p t", t=4), op0=MULT, op1=MULT)
+            nc.sync.dma_start(out=out[b], in_=o[b][:])
 
-        def store(b, h):
-            cols = slice(h * H, (h + 1) * H)
-            nc.sync.dma_start(out=out[b][:, cols], in_=o[b][:, cols])
-
+        ts_road()
         gather(0)
-        gather(1)
-        gather(2)
-        gather3(0, 0)
-        load_q(0, 0)
-        cast(1, "A")
-        load_q(1, 1)
-        gather3(0, 1)
-        query(0, "D")
-        cast(0, "A")
         turn(0)
+        values(0)
+        gather(1)
+        load_q()
+        turn(1)
+        quant_values(0)
+        gather(2)
+        values(1)
+        turn(2)
+        quant_values(1)
+        gather_seq(3, 0)
+        gather_seq(3, 1)
+        load_ch()
+        values(2)
         keys(0, 0, "A")
-        gather3(1, 0)
-        load_ts(2)
-        query(1, "D")
-        keys(0, 1, "A")
-        gather3(1, 1)
+        keys(0, 1, "D")
+        query(0, "D")
         quant_keys(0, 0)
         quant_query(0)
-        cast(2, "A")
-        keys(1, 1, "D")
-        keys(1, 0, "A")
         quant_keys(0, 1)
-        ts_gather(0)
-        quant_keys(1, 1)
-        scores(0, 1)
-        quant_keys(1, 0)
-        quant_query(1)
-        scores(0, 0)
-        turn(1)
-        scaled(0, 1)
-        load_ch()
-        scores(1, 0)
-        turn(2)
-        ts4_turn(0)
-        scores(1, 1)
-        scaled(0, 0)
-        ts_gather(1)
-        values(0, 0)
-        scaled(1, 0)
-        scaled(1, 1)
-        row_min(0)
-        expo(0, 0)
-        cast(3, "A")
-        values(2, 0)
-        row_min(1)
-        values(1, 1)
+        scores(0)
+        keys(1, 0, "A")
+        keys(1, 1, "A")
+        query(1, "A")
         turn(3)
-        values(1, 0)
-        ts4_turn(1)
-        values(3, 0)
-        quant_values(1, 0)
-        expo(1, 1)
-        ts4_out(0)
-        quant_values(0, 0)
-        turn_p(0, 0)
-        values(0, 1)
-        values(2, 1)
-        turn_p(1, 1)
-        expo(0, 1)
-        values(3, 1)
-        expo(1, 0)
-        ts4_out(1)
-        turn_p(0, 1)
-        recip(1)
-        quant_values(0, 1)
+        quant_values(2)
+        scaled(0)
+        row_max(0)
+        expo(0)
+        quant_keys(1, 0)
+        quant_keys(1, 1)
+        quant_query(1)
+        scores(1)
+        values(3)
+        turn_p(0)
+        scaled(1)
         weights(0)
+        row_max(1)
+        expo(1)
         quant_weights(0)
-        turn_p(1, 0)
-        quant_values(1, 1)
-        weights(1)
-        quant_weights(1)
-        product(1, 0)
-        product(0, 0)
-        product(1, 1)
-        epilogue(1, 1)
-        epilogue(1, 0)
-        store(1, 1)
-        product(0, 1)
-        store(1, 0)
+        quant_values(3)
         recip(0)
-        epilogue(0, 0)
-        store(0, 0)
-        epilogue(0, 1)
-        store(0, 1)
+        product(0)
+        turn_p(1)
+        epilogue(0)
+        weights(1)
+        recip(1)
+        quant_weights(1)
+        product(1)
+        epilogue(1)

@@ -15,6 +15,7 @@ U16 = mybir.dt.uint16
 U8 = mybir.dt.uint8
 FP8X4 = mybir.dt.float8_e4m3fn_x4
 MULT = mybir.AluOpType.mult
+ADD = mybir.AluOpType.add
 MAX = mybir.AluOpType.max
 EXP = mybir.ActivationFunctionType.Exp
 AX = mybir.AxisListType.X
@@ -30,8 +31,8 @@ def tile_attend_x_mla_sink_kernel(tc, qT, cT, ts, sink, ch, offs, out):
         def sb(shape, dtype, name):
             return keep.tile(shape, dtype, name=name, align_bytes=64)
 
-        def slot(shape, name, k):
-            return keep.tile(shape, F32, name=name, tag=f"r{k}", bufs=1, align_bytes=64)
+        def slot(shape, name, k, dtype=F32):
+            return keep.tile(shape, dtype, name=name, tag=f"r{k}", bufs=1, align_bytes=64)
 
         def bank(name):
             return psum.tile([P, 512], F32, name=name, tag="x", bufs=4)
@@ -62,19 +63,18 @@ def tile_attend_x_mla_sink_kernel(tc, qT, cT, ts, sink, ch, offs, out):
         nc.scalar.activation(out=warm[:], in_=warm[:], func=EXP)
 
         nm = [sb([P, 1], F32, f"nm{b}") for b in range(B)]
-        lsum = [sb([P, 1], F32, f"lsum{b}") for b in range(B)]
+        lsum = [sb([P, 2], F32, f"lsum{b}") for b in range(B)]
+        total = [sb([P, 1], F32, f"total{b}") for b in range(B)]
         rl = [sb([P, 1], F32, f"rl{b}") for b in range(B)]
         g = sb([P, 4 * B * N], BF16, "g")
-        vt23 = sb([P, 2 * B * N], BF16, "vt23")
         vq = [sb([P, D], U32, f"vq{b}") for b in range(B)]
         vs = [sb([P, D], U8, f"vs{b}") for b in range(B)]
         tsg = sb([P, B * N], F32, "tsg")
         ts4 = [sb([P, 4], F32, f"ts4_{b}") for b in range(B)]
         tsb = [sb([P, N], F32, f"tsb{b}") for b in range(B)]
-        qi = [sb([P, NQ, 4], BF16, f"qi{b}") for b in range(B)]
         qq = [sb([P, NQ], U32, f"qq{b}") for b in range(B)]
         qs = [sb([P, NQ], U8, f"qs{b}") for b in range(B)]
-        ki = [[sb([P, H, 4], BF16, f"ki{b}_{h}") for h in range(2)] for b in range(B)]
+        ki = [sb([P, 4 * N], BF16, f"ki{b}") for b in range(B)]
         kq = [sb([P, N], U32, f"kq{b}") for b in range(B)]
         ks = [sb([P, N], U8, f"ks{b}") for b in range(B)]
         p = [sb([P, N + 1], F32, f"p{b}") for b in range(B)]
@@ -87,8 +87,6 @@ def tile_attend_x_mla_sink_kernel(tc, qT, cT, ts, sink, ch, offs, out):
         def plane_cols(t):
             return g[:, t * B * N:(t + 1) * B * N]
 
-        def vt(t):
-            return plane_cols(t + 2) if t < 2 else vt23[:, (t - 2) * B * N:(t - 1) * B * N]
 
         def interleave(eng, dst, src):
             copy = nc.scalar.copy if eng == "A" else nc.vector.tensor_copy
@@ -100,7 +98,7 @@ def tile_attend_x_mla_sink_kernel(tc, qT, cT, ts, sink, ch, offs, out):
                 nc.sync.dma_start(out=tile["q"][:, b], in_=qT[b].rearrange("(p t) q -> p t q", t=4))
 
         def load_ch():
-            tile["ch"] = slot([P, D], "ch_sb", 3)
+            tile["ch"] = slot([P, D], "ch_sb", 2)
             nc.sync.dma_start(out=tile["ch"][:], in_=ch)
 
         def ts_road():
@@ -119,8 +117,8 @@ def tile_attend_x_mla_sink_kernel(tc, qT, cT, ts, sink, ch, offs, out):
         def gather(t):
             nc.vector.tensor_copy(plane_cols(t), planes[t][:].indirect(offsets[:]))
 
-        def gather_seq(t, b):
-            nc.vector.tensor_copy(plane_cols(t)[:, b * N:(b + 1) * N], planes[t][:].indirect(offsets[:, b * 32:(b + 1) * 32]))
+        def gather_part(t, lo, hi):
+            nc.vector.tensor_copy(plane_cols(t)[:, lo:hi], planes[t][:].indirect(offsets[:, lo // 16:hi // 16]))
 
         def turn(t):
             words = plane_cols(t).bitcast(F32)
@@ -131,28 +129,40 @@ def tile_attend_x_mla_sink_kernel(tc, qT, cT, ts, sink, ch, offs, out):
                     nc.tensor.transpose(tile["v", t][:, k * P:(k + 1) * P], words[:, b * H + u:(b + 1) * H:2], ident[:])
 
         def values(t):
-            nc.scalar.copy(out=vt(t).bitcast(F32).rearrange("m (b p u) -> m b p u", b=B, u=2),
-                           in_=tile["v", t][:].rearrange("m (b u p) -> m b p u", b=B, u=2))
+            src = tile["v", t][:].rearrange("m (b u p) -> m b p u", b=B, u=2)
+            if t < 2:
+                nc.scalar.copy(out=plane_cols(t + 2).bitcast(F32).rearrange("m (b p u) -> m b p u", b=B, u=2), in_=src)
+            else:
+                nc.scalar.copy(out=ki[0][:].bitcast(F32).rearrange("m (b h t p u) -> m b h t p u", b=B, h=2, t=2, u=2)[:, :, :, t - 2],
+                               in_=src.rearrange("m b (h p) u -> m b h p u", h=2))
 
         def quant_values(t):
-            cols = slice(t * P, (t + 1) * P)
             for b in range(B):
-                nc.vector.quantize_mx(out=vq[b][:, cols].bitcast(FP8X4), scales=vs[b][:, cols], in_=vt(t)[:, b * N:(b + 1) * N])
+                for h in range(2):
+                    cols = slice(h * H + t * 64, h * H + (t + 1) * 64)
+                    nc.vector.quantize_mx(out=vq[b][:, cols].bitcast(FP8X4), scales=vs[b][:, cols],
+                                          in_=plane_cols(t + 2)[:, b * N + h * H:b * N + (h + 1) * H])
 
-        def query(b, eng):
-            interleave(eng, qi[b][:], tile["q"][:, b])
+        def quant_late_values(b):
+            for h in range(2):
+                cols = slice(h * H + P, (h + 1) * H)
+                nc.vector.quantize_mx(out=vq[b][:, cols].bitcast(FP8X4), scales=vs[b][:, cols],
+                                      in_=ki[0][:, (2 * b + h) * N:(2 * b + h + 1) * N])
+
+        def query(b):
+            if b == 0:
+                tile["qi"] = slot([P, B * NQ * 4], "qi", 3, BF16)
+            interleave("A", tile["qi"][:, b * N:(b + 1) * N].rearrange("p (q t) -> p q t", t=4), tile["q"][:, b])
 
         def quant_query(b):
-            nc.vector.quantize_mx(out=qq[b][:].bitcast(FP8X4), scales=qs[b][:], in_=qi[b][:].rearrange("p q t -> p (q t)"))
+            nc.vector.quantize_mx(out=qq[b][:].bitcast(FP8X4), scales=qs[b][:], in_=tile["qi"][:, b * N:(b + 1) * N])
 
         def keys(b, h, eng):
             lo = b * N + h * H
-            interleave(eng, ki[b][h][:], g[:].rearrange("p (t s) -> p t s", t=4)[:, :, lo:lo + H])
+            interleave(eng, ki[b][:, h * 4 * H:(h + 1) * 4 * H].rearrange("p (s t) -> p s t", t=4), g[:].rearrange("p (t s) -> p t s", t=4)[:, :, lo:lo + H])
 
-        def quant_keys(b, h):
-            hc = slice(h * H, (h + 1) * H)
-            nc.vector.quantize_mx(out=kq[b][:, hc].bitcast(FP8X4), scales=ks[b][:, hc],
-                                  in_=ki[b][h][:].rearrange("p s t -> p (s t)"))
+        def quant_keys(b):
+            nc.vector.quantize_mx(out=kq[b][:].bitcast(FP8X4), scales=ks[b][:], in_=ki[b][:])
 
         def scores(b):
             tile["s", b] = seq_bank("sps", b)
@@ -168,7 +178,9 @@ def tile_attend_x_mla_sink_kernel(tc, qT, cT, ts, sink, ch, offs, out):
             nc.vector.tensor_reduce(out=nm[b][:], in_=a[:, b, 0:N + 1], axis=AX, op=MAX, negate=True)
 
         def expo(b):
-            nc.scalar.activation(out=p[b][:], in_=a[:, b, 0:N + 1], func=EXP, bias=nm[b][:], scale=1.0, accum_out=lsum[b][:])
+            for i, (lo, hi) in enumerate(((0, H), (H, N + 1))):
+                nc.scalar.activation(out=p[b][:, lo:hi], in_=a[:, b, lo:hi], func=EXP, bias=nm[b][:], scale=1.0,
+                                     accum_out=lsum[b][:, i:i + 1])
 
         def turn_p(b):
             tile["p", b] = bank("pps")
@@ -183,18 +195,23 @@ def tile_attend_x_mla_sink_kernel(tc, qT, cT, ts, sink, ch, offs, out):
             nc.vector.quantize_mx(out=wq[b][:].bitcast(FP8X4), scales=ws[b][:], in_=wi[b][:].rearrange("m q s -> m (q s)"))
 
         def recip(b):
-            nc.vector.reciprocal(out=rl[b][:], in_=lsum[b][:])
+            nc.vector.tensor_reduce(out=total[b][:], in_=lsum[b][:], axis=AX, op=ADD)
+            nc.vector.reciprocal(out=rl[b][:], in_=total[b][:])
 
         def product(b):
-            tile["y", b] = seq_bank("yps", b)
-            nc.tensor.matmul_mx(tile["y", b][:], lhsT=wq[b][:].bitcast(FP8X4), lhsT_scale=ws[b][:],
-                                rhs=vq[b][:].bitcast(FP8X4), rhs_scale=vs[b][:], start=True, stop=True)
+            for h in range(2):
+                cols = slice(h * H, (h + 1) * H)
+                tile["y", b, h] = seq_bank("yps", h)
+                nc.tensor.matmul_mx(tile["y", b, h][:, 0:H], lhsT=wq[b][:].bitcast(FP8X4), lhsT_scale=ws[b][:],
+                                    rhs=vq[b][:, cols].bitcast(FP8X4), rhs_scale=vs[b][:, cols], start=True, stop=True)
 
-        def epilogue(b):
+        def epilogue(b, h, queue):
+            cols = slice(h * H, (h + 1) * H)
             nc.vector.scalar_tensor_tensor(
-                out=o[b][:].rearrange("q (p t) -> q p t", t=4), in0=tile["y", b][:].rearrange("q (t p) -> q p t", t=4),
-                scalar=rl[b][:], in1=tile["ch"][:].rearrange("q (p t) -> q p t", t=4), op0=MULT, op1=MULT)
-            nc.sync.dma_start(out=out[b], in_=o[b][:])
+                out=o[b][:, cols].rearrange("q (p t) -> q p t", t=4),
+                in0=tile["y", b, h][:, 0:H].rearrange("q (t p) -> q p t", t=4),
+                scalar=rl[b][:], in1=tile["ch"][:, cols].rearrange("q (p t) -> q p t", t=4), op0=MULT, op1=MULT)
+            queue.dma_start(out=out[b][:, cols], in_=o[b][:, cols])
 
         ts_road()
         gather(0)
@@ -208,43 +225,42 @@ def tile_attend_x_mla_sink_kernel(tc, qT, cT, ts, sink, ch, offs, out):
         values(1)
         turn(2)
         quant_values(1)
-        gather_seq(3, 0)
-        gather_seq(3, 1)
+        gather_part(3, 0, H)
+        gather_part(3, H, B * N)
         load_ch()
-        values(2)
         keys(0, 0, "A")
         keys(0, 1, "D")
-        query(0, "D")
-        quant_keys(0, 0)
-        quant_query(0)
-        quant_keys(0, 1)
-        scores(0)
+        query(0)
+        keys(1, 1, "D")
         keys(1, 0, "A")
-        keys(1, 1, "A")
-        query(1, "A")
+        query(1)
         turn(3)
-        quant_values(2)
+        quant_keys(0)
+        quant_query(0)
+        scores(0)
+        quant_keys(1)
+        quant_query(1)
+        scores(1)
+        values(2)
+        values(3)
         scaled(0)
         row_max(0)
         expo(0)
-        quant_keys(1, 0)
-        quant_keys(1, 1)
-        quant_query(1)
-        scores(1)
-        values(3)
-        turn_p(0)
         scaled(1)
-        weights(0)
         row_max(1)
         expo(1)
-        quant_weights(0)
-        quant_values(3)
-        recip(0)
-        product(0)
+        turn_p(0)
         turn_p(1)
-        epilogue(0)
+        quant_late_values(0)
+        quant_late_values(1)
+        weights(0)
+        recip(0)
+        quant_weights(0)
+        product(0)
         weights(1)
         recip(1)
         quant_weights(1)
         product(1)
-        epilogue(1)
+        for b in range(B):
+            epilogue(b, 0, nc.scalar)
+            epilogue(b, 1, nc.sync)

@@ -6,6 +6,7 @@ from concourse.masks import make_identity
 B, N, T, D, NQ = 2, 512, 2048, 512, 128
 P = 128
 H = N // 2
+PLANE = 4 * T
 FLOPS = 4 * B * N * D * NQ
 
 F32 = mybir.dt.float32
@@ -15,8 +16,9 @@ U16 = mybir.dt.uint16
 U8 = mybir.dt.uint8
 FP8X4 = mybir.dt.float8_e4m3fn_x4
 MULT = mybir.AluOpType.mult
-ADD = mybir.AluOpType.add
 MAX = mybir.AluOpType.max
+IDENTITY = mybir.ActivationFunctionType.Identity
+COPY = mybir.ActivationFunctionType.Copy
 EXP = mybir.ActivationFunctionType.Exp
 AX = mybir.AxisListType.X
 
@@ -26,13 +28,14 @@ def tile_attend_x_mla_sink_kernel(tc, qT, cT, ts, sink, ch, offs, out):
     with ExitStack() as ctx:
         lists = ctx.enter_context(tc.tile_pool(name="lists", bufs=1))
         keep = ctx.enter_context(tc.tile_pool(name="keep", bufs=1))
+        ring = ctx.enter_context(tc.tile_pool(name="ring", bufs=1))
         psum = ctx.enter_context(tc.psum_pool(name="psum", bufs=1))
 
         def sb(shape, dtype, name):
             return keep.tile(shape, dtype, name=name, align_bytes=64)
 
-        def slot(shape, name, k, dtype=F32):
-            return keep.tile(shape, dtype, name=name, tag=f"r{k}", bufs=1, align_bytes=64)
+        def placed(shape, dtype, name, offset):
+            return ring.tile(shape, dtype, name=name, offset=offset, align_bytes=64)
 
         def bank(name):
             return psum.tile([P, 512], F32, name=name, tag="x", bufs=4)
@@ -49,7 +52,7 @@ def tile_attend_x_mla_sink_kernel(tc, qT, cT, ts, sink, ch, offs, out):
         cv = cT.rearrange("(p t) c -> p t c", t=4)
         planes = []
         for t in range(4):
-            pl = slot([P, T], f"plane{t}", t)
+            pl = placed([P, T], F32, f"plane{t}", t * PLANE)
             nc.sync.dma_start(out=pl[:], in_=cv[:, t, :])
             planes.append(pl)
 
@@ -64,13 +67,14 @@ def tile_attend_x_mla_sink_kernel(tc, qT, cT, ts, sink, ch, offs, out):
 
         nm = [sb([P, 1], F32, f"nm{b}") for b in range(B)]
         lsum = [sb([P, 2], F32, f"lsum{b}") for b in range(B)]
-        total = [sb([P, 1], F32, f"total{b}") for b in range(B)]
-        rl = [sb([P, 1], F32, f"rl{b}") for b in range(B)]
+        total = sb([P, B], F32, "total")
+        rl = sb([P, B], F32, "rl")
         g = sb([P, 4 * B * N], BF16, "g")
-        vq = [sb([P, D], U32, f"vq{b}") for b in range(B)]
+        vt01 = sb([P, 4 * N], BF16, "vt01")
+        vq = [placed([P, D], U32, f"vq{b}", 3 * PLANE + (b + 1) * 4 * D) for b in range(B)]
         vs = [sb([P, D], U8, f"vs{b}") for b in range(B)]
         tsg = sb([P, B * N], F32, "tsg")
-        ts4 = [sb([P, 4], F32, f"ts4_{b}") for b in range(B)]
+        ts4 = [placed([P, 4], F32, f"ts4_{b}", 4 * PLANE + 64 * b) for b in range(B)]
         tsb = [sb([P, N], F32, f"tsb{b}") for b in range(B)]
         qq = [sb([P, NQ], U32, f"qq{b}") for b in range(B)]
         qs = [sb([P, NQ], U8, f"qs{b}") for b in range(B)]
@@ -93,21 +97,24 @@ def tile_attend_x_mla_sink_kernel(tc, qT, cT, ts, sink, ch, offs, out):
             copy(out=dst.rearrange("p (c i) t -> p c t i", i=4), in_=src.rearrange("p t (c i) -> p c t i", i=4))
 
         def load_q():
-            tile["q"] = slot([P, B, 4, NQ], "qraw", 1)
+            tile["q"] = placed([P, B, 4, NQ], F32, "qraw", PLANE)
             for b in range(B):
                 nc.sync.dma_start(out=tile["q"][:, b], in_=qT[b].rearrange("(p t) q -> p t q", t=4))
 
         def load_ch():
-            tile["ch"] = slot([P, D], "ch_sb", 2)
+            tile["ch"] = placed([P, D], F32, "ch_sb", 2 * PLANE)
             nc.sync.dma_start(out=tile["ch"][:], in_=ch)
 
-        def ts_road():
+        def ts_gather():
             nc.vector.tensor_copy(tsg[:], tsw[:].indirect(offsets[:]))
             for b in range(B):
-                cols = bank("tps")
+                tile["t", b] = bank("tps")
                 for s in range(4):
-                    nc.tensor.transpose(cols[:, s * P:(s + 1) * P], tsg[:, b * N + s:(b + 1) * N:4], ident[:])
-                nc.scalar.copy(out=ts4[b][:], in_=cols[:, P - 1:512:P])
+                    nc.tensor.transpose(tile["t", b][:, s * P:(s + 1) * P], tsg[:, b * N + s:(b + 1) * N:4], ident[:])
+
+        def ts_spread():
+            for b in range(B):
+                nc.scalar.copy(out=ts4[b][:], in_=tile["t", b][:, P - 1:512:P])
             for b in range(B):
                 rows = bank("tbs")
                 for s in range(4):
@@ -116,6 +123,11 @@ def tile_attend_x_mla_sink_kernel(tc, qT, cT, ts, sink, ch, offs, out):
 
         def gather(t):
             nc.vector.tensor_copy(plane_cols(t), planes[t][:].indirect(offsets[:]))
+
+        def gather_on_scalar(t):
+            half = placed([P, T], BF16, "half", 4 * PLANE)
+            nc.vector.tensor_copy(out=half[:], in_=planes[t][:])
+            nc.scalar.activation(plane_cols(t), half[:].indirect(offsets[:]), COPY)
 
         def gather_part(t, lo, hi):
             nc.vector.tensor_copy(plane_cols(t)[:, lo:hi], planes[t][:].indirect(offsets[:, lo // 16:hi // 16]))
@@ -129,29 +141,20 @@ def tile_attend_x_mla_sink_kernel(tc, qT, cT, ts, sink, ch, offs, out):
                     nc.tensor.transpose(tile["v", t][:, k * P:(k + 1) * P], words[:, b * H + u:(b + 1) * H:2], ident[:])
 
         def values(t):
-            src = tile["v", t][:].rearrange("m (b u p) -> m b p u", b=B, u=2)
-            if t < 2:
-                nc.scalar.copy(out=plane_cols(t + 2).bitcast(F32).rearrange("m (b p u) -> m b p u", b=B, u=2), in_=src)
-            else:
-                nc.scalar.copy(out=ki[0][:].bitcast(F32).rearrange("m (b h t p u) -> m b h t p u", b=B, h=2, t=2, u=2)[:, :, :, t - 2],
-                               in_=src.rearrange("m b (h p) u -> m b h p u", h=2))
+            src = tile["v", t][:].rearrange("m (b u h p) -> m b h p u", b=B, u=2, h=2)
+            stage = vt01 if t < 2 else ki[0]
+            nc.scalar.copy(out=stage[:].bitcast(F32).rearrange("m (b h t p u) -> m b h t p u", b=B, h=2, t=2, u=2)[:, :, :, t % 2], in_=src)
 
-        def quant_values(t):
-            for b in range(B):
-                for h in range(2):
-                    cols = slice(h * H + t * 64, h * H + (t + 1) * 64)
-                    nc.vector.quantize_mx(out=vq[b][:, cols].bitcast(FP8X4), scales=vs[b][:, cols],
-                                          in_=plane_cols(t + 2)[:, b * N + h * H:b * N + (h + 1) * H])
-
-        def quant_late_values(b):
+        def quant_values(b, pair):
+            stage = vt01 if pair == 0 else ki[0]
             for h in range(2):
-                cols = slice(h * H + P, (h + 1) * H)
+                cols = slice(h * H + pair * P, h * H + (pair + 1) * P)
                 nc.vector.quantize_mx(out=vq[b][:, cols].bitcast(FP8X4), scales=vs[b][:, cols],
-                                      in_=ki[0][:, (2 * b + h) * N:(2 * b + h + 1) * N])
+                                      in_=stage[:, (2 * b + h) * N:(2 * b + h + 1) * N])
 
         def query(b):
             if b == 0:
-                tile["qi"] = slot([P, B * NQ * 4], "qi", 3, BF16)
+                tile["qi"] = placed([P, B * NQ * 4], BF16, "qi", 3 * PLANE)
             interleave("A", tile["qi"][:, b * N:(b + 1) * N].rearrange("p (q t) -> p q t", t=4), tile["q"][:, b])
 
         def quant_query(b):
@@ -181,6 +184,7 @@ def tile_attend_x_mla_sink_kernel(tc, qT, cT, ts, sink, ch, offs, out):
             for i, (lo, hi) in enumerate(((0, H), (H, N + 1))):
                 nc.scalar.activation(out=p[b][:, lo:hi], in_=a[:, b, lo:hi], func=EXP, bias=nm[b][:], scale=1.0,
                                      accum_out=lsum[b][:, i:i + 1])
+            nc.scalar.activation(out=total[:, b:b + 1], in_=lsum[b][:, 0:1], func=IDENTITY, bias=lsum[b][:, 1:2], scale=1.0)
 
         def turn_p(b):
             tile["p", b] = bank("pps")
@@ -194,10 +198,6 @@ def tile_attend_x_mla_sink_kernel(tc, qT, cT, ts, sink, ch, offs, out):
         def quant_weights(b):
             nc.vector.quantize_mx(out=wq[b][:].bitcast(FP8X4), scales=ws[b][:], in_=wi[b][:].rearrange("m q s -> m (q s)"))
 
-        def recip(b):
-            nc.vector.tensor_reduce(out=total[b][:], in_=lsum[b][:], axis=AX, op=ADD)
-            nc.vector.reciprocal(out=rl[b][:], in_=total[b][:])
-
         def product(b):
             for h in range(2):
                 cols = slice(h * H, (h + 1) * H)
@@ -210,21 +210,20 @@ def tile_attend_x_mla_sink_kernel(tc, qT, cT, ts, sink, ch, offs, out):
             nc.vector.scalar_tensor_tensor(
                 out=o[b][:, cols].rearrange("q (p t) -> q p t", t=4),
                 in0=tile["y", b, h][:, 0:H].rearrange("q (t p) -> q p t", t=4),
-                scalar=rl[b][:], in1=tile["ch"][:, cols].rearrange("q (p t) -> q p t", t=4), op0=MULT, op1=MULT)
+                scalar=rl[:, b:b + 1], in1=tile["ch"][:, cols].rearrange("q (p t) -> q p t", t=4), op0=MULT, op1=MULT)
             queue.dma_start(out=out[b][:, cols], in_=o[b][:, cols])
 
-        ts_road()
-        gather(0)
-        turn(0)
-        values(0)
+        ts_gather()
+        gather_on_scalar(0)
+        ts_spread()
         gather(1)
         load_q()
-        turn(1)
-        quant_values(0)
         gather(2)
+        turn(0)
+        values(0)
+        turn(1)
         values(1)
         turn(2)
-        quant_values(1)
         gather_part(3, 0, H)
         gather_part(3, H, B * N)
         load_ch()
@@ -251,14 +250,14 @@ def tile_attend_x_mla_sink_kernel(tc, qT, cT, ts, sink, ch, offs, out):
         expo(1)
         turn_p(0)
         turn_p(1)
-        quant_late_values(0)
-        quant_late_values(1)
+        for b in range(B):
+            quant_values(b, 0)
+            quant_values(b, 1)
         weights(0)
-        recip(0)
         quant_weights(0)
         product(0)
         weights(1)
-        recip(1)
+        nc.vector.reciprocal(out=rl[:], in_=total[:])
         quant_weights(1)
         product(1)
         for b in range(B):

@@ -18,7 +18,6 @@ FP8X4 = mybir.dt.float8_e4m3fn_x4
 MULT = mybir.AluOpType.mult
 MAX = mybir.AluOpType.max
 IDENTITY = mybir.ActivationFunctionType.Identity
-COPY = mybir.ActivationFunctionType.Copy
 EXP = mybir.ActivationFunctionType.Exp
 AX = mybir.AxisListType.X
 
@@ -56,8 +55,6 @@ def tile_attend_x_mla_sink_kernel(tc, qT, cT, ts, sink, ch, offs, out):
             nc.sync.dma_start(out=pl[:], in_=cv[:, t, :])
             planes.append(pl)
 
-        a = sb([P, B, 520], F32, "a")
-        nc.sync.dma_start(out=a[:, :, N:N + 1], in_=sink.rearrange("b q o -> q b o"))
 
         ident = sb([P, P], F32, "ident")
         make_identity(nc, ident[:])
@@ -69,12 +66,11 @@ def tile_attend_x_mla_sink_kernel(tc, qT, cT, ts, sink, ch, offs, out):
         lsum = [sb([P, 2], F32, f"lsum{b}") for b in range(B)]
         total = sb([P, B], F32, "total")
         rl = sb([P, B], F32, "rl")
-        g = sb([P, 4 * B * N], BF16, "g")
-        vt01 = sb([P, 4 * N], BF16, "vt01")
-        vq = [placed([P, D], U32, f"vq{b}", 3 * PLANE + (b + 1) * 4 * D) for b in range(B)]
+        g = sb([P, 5 * B * N], BF16, "g")
+        vq = [placed([P, D], U32, f"vq{b}", 2 * PLANE + (b + 1) * 4 * D) for b in range(B)]
         vs = [sb([P, D], U8, f"vs{b}") for b in range(B)]
         tsg = sb([P, B * N], F32, "tsg")
-        ts4 = [placed([P, 4], F32, f"ts4_{b}", 4 * PLANE + 64 * b) for b in range(B)]
+        ts4 = [sb([P, 4], F32, f"ts4_{b}") for b in range(B)]
         tsb = [sb([P, N], F32, f"tsb{b}") for b in range(B)]
         qq = [sb([P, NQ], U32, f"qq{b}") for b in range(B)]
         qs = [sb([P, NQ], U8, f"qs{b}") for b in range(B)]
@@ -86,6 +82,7 @@ def tile_attend_x_mla_sink_kernel(tc, qT, cT, ts, sink, ch, offs, out):
         wq = [sb([P, NQ], U32, f"wq{b}") for b in range(B)]
         ws = [sb([P, NQ], U8, f"ws{b}") for b in range(B)]
         o = [sb([P, D], F32, f"o{b}") for b in range(B)]
+        a = placed([P, B, 520], F32, "a", PLANE // 2 + PLANE)
         tile = {}
 
         def plane_cols(t):
@@ -102,7 +99,8 @@ def tile_attend_x_mla_sink_kernel(tc, qT, cT, ts, sink, ch, offs, out):
                 nc.sync.dma_start(out=tile["q"][:, b], in_=qT[b].rearrange("(p t) q -> p t q", t=4))
 
         def load_ch():
-            tile["ch"] = placed([P, D], F32, "ch_sb", 2 * PLANE)
+            nc.sync.dma_start(out=a[:, :, N:N + 1], in_=sink.rearrange("b q o -> q b o"))
+            tile["ch"] = placed([P, D], F32, "ch_sb", 2 * PLANE + 3 * 4 * D)
             nc.sync.dma_start(out=tile["ch"][:], in_=ch)
 
         def ts_gather():
@@ -124,11 +122,6 @@ def tile_attend_x_mla_sink_kernel(tc, qT, cT, ts, sink, ch, offs, out):
         def gather(t):
             nc.vector.tensor_copy(plane_cols(t), planes[t][:].indirect(offsets[:]))
 
-        def gather_on_scalar(t):
-            half = placed([P, T], BF16, "half", 4 * PLANE)
-            nc.vector.tensor_copy(out=half[:], in_=planes[t][:])
-            nc.scalar.activation(plane_cols(t), half[:].indirect(offsets[:]), COPY)
-
         def gather_part(t, lo, hi):
             nc.vector.tensor_copy(plane_cols(t)[:, lo:hi], planes[t][:].indirect(offsets[:, lo // 16:hi // 16]))
 
@@ -142,27 +135,31 @@ def tile_attend_x_mla_sink_kernel(tc, qT, cT, ts, sink, ch, offs, out):
 
         def values(t):
             src = tile["v", t][:].rearrange("m (b u h p) -> m b h p u", b=B, u=2, h=2)
-            stage = vt01 if t < 2 else ki[0]
-            nc.scalar.copy(out=stage[:].bitcast(F32).rearrange("m (b h t p u) -> m b h t p u", b=B, h=2, t=2, u=2)[:, :, :, t % 2], in_=src)
+            stage = g[:, 3 * B * N:] if t < 2 else ki[0][:]
+            nc.scalar.copy(out=stage.bitcast(F32).rearrange("m (b h t p u) -> m b h t p u", b=B, h=2, t=2, u=2)[:, :, :, t % 2], in_=src)
 
         def quant_values(b, pair):
-            stage = vt01 if pair == 0 else ki[0]
-            for h in range(2):
+            stage = g[:, 3 * B * N:] if pair == 0 else ki[0][:]
+            for h in (1, 0):
                 cols = slice(h * H + pair * P, h * H + (pair + 1) * P)
                 nc.vector.quantize_mx(out=vq[b][:, cols].bitcast(FP8X4), scales=vs[b][:, cols],
                                       in_=stage[:, (2 * b + h) * N:(2 * b + h + 1) * N])
 
         def query(b):
             if b == 0:
-                tile["qi"] = placed([P, B * NQ * 4], BF16, "qi", 3 * PLANE)
-            interleave("A", tile["qi"][:, b * N:(b + 1) * N].rearrange("p (q t) -> p q t", t=4), tile["q"][:, b])
+                tile["qi", b] = placed([P, NQ * 4], BF16, "qi", 3 * PLANE)[:]
+            else:
+                tile["qi", b] = a[:, 0, 0:H].bitcast(BF16)
+            interleave("A", tile["qi", b].rearrange("p (q t) -> p q t", t=4), tile["q"][:, b])
 
         def quant_query(b):
-            nc.vector.quantize_mx(out=qq[b][:].bitcast(FP8X4), scales=qs[b][:], in_=tile["qi"][:, b * N:(b + 1) * N])
+            nc.vector.quantize_mx(out=qq[b][:].bitcast(FP8X4), scales=qs[b][:], in_=tile["qi", b])
 
-        def keys(b, h, eng):
+        def keys(b, h, pair, eng):
             lo = b * N + h * H
-            interleave(eng, ki[b][:, h * 4 * H:(h + 1) * 4 * H].rearrange("p (s t) -> p s t", t=4), g[:].rearrange("p (t s) -> p t s", t=4)[:, :, lo:lo + H])
+            copy = nc.scalar.copy if eng == "A" else nc.vector.tensor_copy
+            copy(out=ki[b][:, h * 4 * H:(h + 1) * 4 * H].rearrange("p (s t) -> p s t", t=4)[:, :, 2 * pair:2 * pair + 2],
+                 in_=g[:, 2 * pair * B * N:(2 * pair + 2) * B * N].rearrange("p (t s) -> p s t", t=2)[:, lo:lo + H])
 
         def quant_keys(b):
             nc.vector.quantize_mx(out=kq[b][:].bitcast(FP8X4), scales=ks[b][:], in_=ki[b][:])
@@ -214,24 +211,30 @@ def tile_attend_x_mla_sink_kernel(tc, qT, cT, ts, sink, ch, offs, out):
             queue.dma_start(out=out[b][:, cols], in_=o[b][:, cols])
 
         ts_gather()
-        gather_on_scalar(0)
         ts_spread()
-        gather(1)
-        load_q()
-        gather(2)
+        gather(0)
         turn(0)
         values(0)
+        gather(1)
+        load_q()
         turn(1)
         values(1)
+        keys(1, 1, 0, "D")
+        keys(0, 0, 0, "A")
+        keys(0, 1, 0, "A")
+        keys(1, 0, 0, "A")
+        gather(2)
         turn(2)
+        quant_values(1, 0)
+        quant_values(0, 0)
         gather_part(3, 0, H)
         gather_part(3, H, B * N)
         load_ch()
-        keys(0, 0, "A")
-        keys(0, 1, "D")
+        keys(0, 0, 1, "A")
+        keys(0, 1, 1, "D")
         query(0)
-        keys(1, 1, "D")
-        keys(1, 0, "A")
+        keys(1, 1, 1, "D")
+        keys(1, 0, 1, "A")
         query(1)
         turn(3)
         quant_keys(0)
@@ -251,7 +254,6 @@ def tile_attend_x_mla_sink_kernel(tc, qT, cT, ts, sink, ch, offs, out):
         turn_p(0)
         turn_p(1)
         for b in range(B):
-            quant_values(b, 0)
             quant_values(b, 1)
         weights(0)
         quant_weights(0)

@@ -6,7 +6,7 @@ from concourse.masks import make_identity
 B, N, T, D, NQ = 2, 512, 2048, 512, 128
 P = 128
 H = N // 2
-PLANE = 4 * T
+PLANE = 4 * T + 256
 FLOPS = 4 * B * N * D * NQ
 
 F32 = mybir.dt.float32
@@ -67,14 +67,15 @@ def tile_attend_x_mla_sink_kernel(tc, qT, cT, ts, sink, ch, offs, out):
         total = sb([P, B], F32, "total")
         rl = sb([P, B], F32, "rl")
         g = sb([P, 5 * B * N], BF16, "g")
-        vq = [placed([P, D], U32, f"vq{b}", 2 * PLANE + (b + 1) * 4 * D) for b in range(B)]
+        vq = [placed([P, D], U32, f"vq{b}", 2 * PLANE + 4160 + b * 4 * D) for b in range(B)]
         vs = [sb([P, D], U8, f"vs{b}") for b in range(B)]
         tsg = sb([P, B * N], F32, "tsg")
         ts4 = [sb([P, 4], F32, f"ts4_{b}") for b in range(B)]
+        tsc = [placed([P, 4], F32, f"tsc{b}", 4 * PLANE + 64 * b) for b in range(B)]
         tsb = [sb([P, N], F32, f"tsb{b}") for b in range(B)]
         qq = [sb([P, NQ], U32, f"qq{b}") for b in range(B)]
         qs = [sb([P, NQ], U8, f"qs{b}") for b in range(B)]
-        ki = [sb([P, 4 * N], BF16, f"ki{b}") for b in range(B)]
+        ki = [placed([P, 4 * N], BF16, "ki0", 4 * PLANE), placed([P, 4 * N], BF16, "ki1", 2 * PLANE + 64)]
         kq = [sb([P, N], U32, f"kq{b}") for b in range(B)]
         ks = [sb([P, N], U8, f"ks{b}") for b in range(B)]
         p = [sb([P, N + 1], F32, f"p{b}") for b in range(B)]
@@ -82,7 +83,7 @@ def tile_attend_x_mla_sink_kernel(tc, qT, cT, ts, sink, ch, offs, out):
         wq = [sb([P, NQ], U32, f"wq{b}") for b in range(B)]
         ws = [sb([P, NQ], U8, f"ws{b}") for b in range(B)]
         o = [sb([P, D], F32, f"o{b}") for b in range(B)]
-        a = placed([P, B, 520], F32, "a", PLANE // 2 + PLANE)
+        a = placed([P, B, 520], F32, "a", 2 * PLANE - 4096)
         tile = {}
 
         def plane_cols(t):
@@ -99,8 +100,7 @@ def tile_attend_x_mla_sink_kernel(tc, qT, cT, ts, sink, ch, offs, out):
                 nc.sync.dma_start(out=tile["q"][:, b], in_=qT[b].rearrange("(p t) q -> p t q", t=4))
 
         def load_ch():
-            nc.sync.dma_start(out=a[:, :, N:N + 1], in_=sink.rearrange("b q o -> q b o"))
-            tile["ch"] = placed([P, D], F32, "ch_sb", 2 * PLANE + 3 * 4 * D)
+            tile["ch"] = placed([P, D], F32, "ch_sb", 3 * PLANE + 2048)
             nc.sync.dma_start(out=tile["ch"][:], in_=ch)
 
         def ts_gather():
@@ -112,11 +112,12 @@ def tile_attend_x_mla_sink_kernel(tc, qT, cT, ts, sink, ch, offs, out):
 
         def ts_spread():
             for b in range(B):
+                nc.scalar.copy(out=tsc[b][:], in_=tile["t", b][:, P - 1:512:P])
                 nc.scalar.copy(out=ts4[b][:], in_=tile["t", b][:, P - 1:512:P])
             for b in range(B):
                 rows = bank("tbs")
                 for s in range(4):
-                    nc.tensor.transpose(rows[:, s * P:(s + 1) * P], ts4[b][:, s:s + 1].to_broadcast([P, P]), ident[:])
+                    nc.tensor.transpose(rows[:, s * P:(s + 1) * P], tsc[b][:, s:s + 1].to_broadcast([P, P]), ident[:])
                 nc.scalar.copy(out=tsb[b][:], in_=rows[:])
 
         def gather(t):
@@ -155,11 +156,10 @@ def tile_attend_x_mla_sink_kernel(tc, qT, cT, ts, sink, ch, offs, out):
         def quant_query(b):
             nc.vector.quantize_mx(out=qq[b][:].bitcast(FP8X4), scales=qs[b][:], in_=tile["qi", b])
 
-        def keys(b, h, pair, eng):
-            lo = b * N + h * H
+        def keys(b, lo, hi, pair, eng):
             copy = nc.scalar.copy if eng == "A" else nc.vector.tensor_copy
-            copy(out=ki[b][:, h * 4 * H:(h + 1) * 4 * H].rearrange("p (s t) -> p s t", t=4)[:, :, 2 * pair:2 * pair + 2],
-                 in_=g[:, 2 * pair * B * N:(2 * pair + 2) * B * N].rearrange("p (t s) -> p s t", t=2)[:, lo:lo + H])
+            copy(out=ki[b][:].rearrange("p (s t) -> p s t", t=4)[:, lo:hi, 2 * pair:2 * pair + 2],
+                 in_=g[:, 2 * pair * B * N:(2 * pair + 2) * B * N].rearrange("p (t s) -> p s t", t=2)[:, b * N + lo:b * N + hi])
 
         def quant_keys(b):
             nc.vector.quantize_mx(out=kq[b][:].bitcast(FP8X4), scales=ks[b][:], in_=ki[b][:])
@@ -211,30 +211,30 @@ def tile_attend_x_mla_sink_kernel(tc, qT, cT, ts, sink, ch, offs, out):
             queue.dma_start(out=out[b][:, cols], in_=o[b][:, cols])
 
         ts_gather()
-        ts_spread()
         gather(0)
         turn(0)
         values(0)
+        ts_spread()
         gather(1)
         load_q()
         turn(1)
         values(1)
-        keys(1, 1, 0, "D")
-        keys(0, 0, 0, "A")
-        keys(0, 1, 0, "A")
-        keys(1, 0, 0, "A")
+        keys(0, 0, H, 0, "A")
+        keys(0, H, N, 0, "A")
         gather(2)
+        nc.sync.dma_start(out=a[:, :, N:N + 1], in_=sink.rearrange("b q o -> q b o"))
+        keys(1, 0, N, 0, "A")
         turn(2)
         quant_values(1, 0)
         quant_values(0, 0)
         gather_part(3, 0, H)
         gather_part(3, H, B * N)
         load_ch()
-        keys(0, 0, 1, "A")
-        keys(0, 1, 1, "D")
+        keys(0, 0, H, 1, "A")
+        keys(0, H, N, 1, "D")
         query(0)
-        keys(1, 1, 1, "D")
-        keys(1, 0, 1, "A")
+        keys(1, H, N, 1, "D")
+        keys(1, 0, H, 1, "A")
         query(1)
         turn(3)
         quant_keys(0)
@@ -253,15 +253,16 @@ def tile_attend_x_mla_sink_kernel(tc, qT, cT, ts, sink, ch, offs, out):
         expo(1)
         turn_p(0)
         turn_p(1)
-        for b in range(B):
-            quant_values(b, 1)
+        quant_values(0, 1)
         weights(0)
+        quant_values(1, 1)
         quant_weights(0)
         product(0)
-        weights(1)
         nc.vector.reciprocal(out=rl[:], in_=total[:])
+        weights(1)
+        epilogue(0, 0, nc.scalar)
         quant_weights(1)
         product(1)
-        for b in range(B):
-            epilogue(b, 0, nc.scalar)
-            epilogue(b, 1, nc.sync)
+        epilogue(0, 1, nc.sync)
+        epilogue(1, 0, nc.scalar)
+        epilogue(1, 1, nc.sync)

@@ -66,7 +66,8 @@ def tile_attend_x_mla_sink_kernel(tc, qT, cT, ts, sink, ch, offs, out):
         lsum = [sb([P, 2], F32, f"lsum{b}") for b in range(B)]
         total = sb([P, B], F32, "total")
         rl = sb([P, B], F32, "rl")
-        g = sb([P, 5 * B * N], BF16, "g")
+        g = sb([P, 4 * B * N], BF16, "g")
+        early1 = placed([P, 2 * N], BF16, "early1", 4 * PLANE + 8 * N)
         vq = [placed([P, D], U32, f"vq{b}", 2 * PLANE + 4160 + b * 4 * D) for b in range(B)]
         vs = [sb([P, D], U8, f"vs{b}") for b in range(B)]
         tsg = sb([P, B * N], F32, "tsg")
@@ -75,8 +76,8 @@ def tile_attend_x_mla_sink_kernel(tc, qT, cT, ts, sink, ch, offs, out):
         tsb = [sb([P, N], F32, f"tsb{b}") for b in range(B)]
         qq = [sb([P, NQ], U32, f"qq{b}") for b in range(B)]
         qs = [sb([P, NQ], U8, f"qs{b}") for b in range(B)]
-        ki = [placed([P, 4 * N], BF16, "ki0", 4 * PLANE), placed([P, 4 * N], BF16, "ki1", 2 * PLANE + 64)]
-        kq = [sb([P, N], U32, f"kq{b}") for b in range(B)]
+        ki = [placed([P, 4 * N], BF16, "ki0", 4 * PLANE), sb([P, 4 * N], BF16, "ki1")]
+        kq = [placed([P, N], U32, "kq0", PLANE), sb([P, N], U32, "kq1")]
         ks = [sb([P, N], U8, f"ks{b}") for b in range(B)]
         p = [sb([P, N + 1], F32, f"p{b}") for b in range(B)]
         wi = [sb([P, NQ, 4], BF16, f"wi{b}") for b in range(B)]
@@ -95,9 +96,9 @@ def tile_attend_x_mla_sink_kernel(tc, qT, cT, ts, sink, ch, offs, out):
             copy(out=dst.rearrange("p (c i) t -> p c t i", i=4), in_=src.rearrange("p t (c i) -> p c t i", i=4))
 
         def load_q():
-            tile["q"] = placed([P, B, 4, NQ], F32, "qraw", PLANE)
             for b in range(B):
-                nc.sync.dma_start(out=tile["q"][:, b], in_=qT[b].rearrange("(p t) q -> p t q", t=4))
+                tile["q", b] = placed([P, 4, NQ], F32, f"qraw{b}", PLANE + 16 * NQ * b)
+                nc.sync.dma_start(out=tile["q", b][:], in_=qT[b].rearrange("(p t) q -> p t q", t=4))
 
         def load_ch():
             tile["ch"] = placed([P, D], F32, "ch_sb", 3 * PLANE + 2048)
@@ -134,24 +135,27 @@ def tile_attend_x_mla_sink_kernel(tc, qT, cT, ts, sink, ch, offs, out):
                     k = 2 * b + u
                     nc.tensor.transpose(tile["v", t][:, k * P:(k + 1) * P], words[:, b * H + u:(b + 1) * H:2], ident[:])
 
-        def values(t):
-            src = tile["v", t][:].rearrange("m (b u h p) -> m b h p u", b=B, u=2, h=2)
-            stage = g[:, 3 * B * N:] if t < 2 else ki[0][:]
-            nc.scalar.copy(out=stage.bitcast(F32).rearrange("m (b h t p u) -> m b h t p u", b=B, h=2, t=2, u=2)[:, :, :, t % 2], in_=src)
+        def values(t, b):
+            src = tile["v", t][:, b * H:(b + 1) * H].rearrange("m (u h p) -> m h p u", u=2, h=2)
+            nc.scalar.copy(out=stage(t // 2, b).bitcast(F32).rearrange("m (h t p u) -> m h t p u", h=2, t=2, u=2)[:, :, t % 2], in_=src)
 
-        def quant_values(b, pair):
-            stage = g[:, 3 * B * N:] if pair == 0 else ki[0][:]
-            for h in (1, 0):
+        def stage(pair, b):
+            if pair == 1:
+                return ki[0][:, 2 * b * N:2 * (b + 1) * N]
+            return early1[:] if b == 1 else g[:, 3 * B * N:]
+
+        def quant_values(b, pair, halves=range(2)):
+            for h in halves:
                 cols = slice(h * H + pair * P, h * H + (pair + 1) * P)
                 nc.vector.quantize_mx(out=vq[b][:, cols].bitcast(FP8X4), scales=vs[b][:, cols],
-                                      in_=stage[:, (2 * b + h) * N:(2 * b + h + 1) * N])
+                                      in_=stage(pair, b)[:, h * N:(h + 1) * N])
 
         def query(b):
             if b == 0:
-                tile["qi", b] = placed([P, NQ * 4], BF16, "qi", 3 * PLANE)[:]
+                tile["qi", b] = placed([P, NQ * 4], BF16, "qi", 4 * PLANE + 8 * N)[:]
             else:
-                tile["qi", b] = a[:, 0, 0:H].bitcast(BF16)
-            interleave("A", tile["qi", b].rearrange("p (q t) -> p q t", t=4), tile["q"][:, b])
+                tile["qi", b] = placed([P, NQ * 4], BF16, "qi1", 4 * PLANE + 10 * N)[:]
+            interleave("A", tile["qi", b].rearrange("p (q t) -> p q t", t=4), tile["q", b][:])
 
         def quant_query(b):
             nc.vector.quantize_mx(out=qq[b][:].bitcast(FP8X4), scales=qs[b][:], in_=tile["qi", b])
@@ -161,13 +165,14 @@ def tile_attend_x_mla_sink_kernel(tc, qT, cT, ts, sink, ch, offs, out):
             copy(out=ki[b][:].rearrange("p (s t) -> p s t", t=4)[:, lo:hi, 2 * pair:2 * pair + 2],
                  in_=g[:, 2 * pair * B * N:(2 * pair + 2) * B * N].rearrange("p (t s) -> p s t", t=2)[:, b * N + lo:b * N + hi])
 
-        def quant_keys(b):
-            nc.vector.quantize_mx(out=kq[b][:].bitcast(FP8X4), scales=ks[b][:], in_=ki[b][:])
+        def quant_keys(b, lo, hi):
+            nc.vector.quantize_mx(out=kq[b][:, lo:hi].bitcast(FP8X4), scales=ks[b][:, lo:hi], in_=ki[b][:, 4 * lo:4 * hi])
 
-        def scores(b):
-            tile["s", b] = seq_bank("sps", b)
-            nc.tensor.matmul_mx(tile["s", b][:], lhsT=qq[b][:].bitcast(FP8X4), lhsT_scale=qs[b][:],
-                                rhs=kq[b][:].bitcast(FP8X4), rhs_scale=ks[b][:], start=True, stop=True)
+        def scores(b, lo, hi):
+            if lo == 0:
+                tile["s", b] = seq_bank("sps", b)
+            nc.tensor.matmul_mx(tile["s", b][:, lo:hi], lhsT=qq[b][:].bitcast(FP8X4), lhsT_scale=qs[b][:],
+                                rhs=kq[b][:, lo:hi].bitcast(FP8X4), rhs_scale=ks[b][:, lo:hi], start=True, stop=True)
 
         def scaled(b):
             nc.vector.tensor_tensor(out=a[:, b, 0:N].rearrange("q (s m) -> q s m", s=4),
@@ -213,22 +218,27 @@ def tile_attend_x_mla_sink_kernel(tc, qT, cT, ts, sink, ch, offs, out):
         ts_gather()
         gather(0)
         turn(0)
-        values(0)
+        values(0, 0)
+        values(0, 1)
         ts_spread()
-        gather(1)
+        gather_part(1, N, B * N)
+        gather_part(1, 0, N)
+        keys(1, 0, N, 0, "D")
         load_q()
         turn(1)
-        values(1)
+        values(1, 0)
+        values(1, 1)
         keys(0, 0, H, 0, "A")
         keys(0, H, N, 0, "A")
         gather(2)
         nc.sync.dma_start(out=a[:, :, N:N + 1], in_=sink.rearrange("b q o -> q b o"))
-        keys(1, 0, N, 0, "A")
         turn(2)
-        quant_values(1, 0)
         quant_values(0, 0)
+        quant_values(1, 0, [0])
         gather_part(3, 0, H)
-        gather_part(3, H, B * N)
+        quant_values(1, 0, [1])
+        gather_part(3, H, N + H)
+        gather_part(3, N + H, B * N)
         load_ch()
         keys(0, 0, H, 1, "A")
         keys(0, H, N, 1, "D")
@@ -237,23 +247,27 @@ def tile_attend_x_mla_sink_kernel(tc, qT, cT, ts, sink, ch, offs, out):
         keys(1, 0, H, 1, "A")
         query(1)
         turn(3)
-        quant_keys(0)
         quant_query(0)
-        scores(0)
-        quant_keys(1)
+        quant_keys(0, 0, H)
+        scores(0, 0, H)
+        quant_keys(0, H, N)
+        scores(0, H, N)
+        quant_keys(1, 0, N)
         quant_query(1)
-        scores(1)
-        values(2)
-        values(3)
+        scores(1, 0, N)
+        values(2, 0)
+        values(3, 0)
+        values(2, 1)
+        values(3, 1)
         scaled(0)
         row_max(0)
         expo(0)
+        quant_values(0, 1)
         scaled(1)
         row_max(1)
         expo(1)
         turn_p(0)
         turn_p(1)
-        quant_values(0, 1)
         weights(0)
         quant_values(1, 1)
         quant_weights(0)

@@ -71,7 +71,7 @@ def tile_attend_x_mla_sink_kernel(tc, qT, cT, ts, sink, ch, offs, out):
         vq = [placed([P, D], U32, f"vq{b}", 2 * PLANE + 4160 + b * 4 * D) for b in range(B)]
         vs = [sb([P, D], U8, f"vs{b}") for b in range(B)]
         tsg = sb([P, B * N], F32, "tsg")
-        ts4 = [sb([P, 4], F32, f"ts4_{b}") for b in range(B)]
+        ts4 = [sb([P, 4], F32, "ts4_0"), placed([P, 4], F32, "ts4_1", 4 * PLANE + 12 * N)]
         tsc = [placed([P, 4], F32, f"tsc{b}", 4 * PLANE + 64 * b) for b in range(B)]
         tsb = [sb([P, N], F32, f"tsb{b}") for b in range(B)]
         qq = [sb([P, NQ], U32, f"qq{b}") for b in range(B)]
@@ -83,7 +83,7 @@ def tile_attend_x_mla_sink_kernel(tc, qT, cT, ts, sink, ch, offs, out):
         wi = [sb([P, NQ, 4], BF16, f"wi{b}") for b in range(B)]
         wq = [sb([P, NQ], U32, f"wq{b}") for b in range(B)]
         ws = [sb([P, NQ], U8, f"ws{b}") for b in range(B)]
-        o = [sb([P, D], F32, f"o{b}") for b in range(B)]
+        o = [placed([P, D], F32, "o0", 4 * PLANE + 12 * N), sb([P, D], F32, "o1")]
         a = placed([P, B, 520], F32, "a", 2 * PLANE - 4096)
         tile = {}
 
@@ -221,8 +221,9 @@ def tile_attend_x_mla_sink_kernel(tc, qT, cT, ts, sink, ch, offs, out):
         values(0, 0)
         values(0, 1)
         ts_spread()
+        gather_part(1, 0, H)
         gather_part(1, N, B * N)
-        gather_part(1, 0, N)
+        gather_part(1, H, N)
         keys(1, 0, N, 0, "D")
         load_q()
         turn(1)
@@ -274,9 +275,9 @@ def tile_attend_x_mla_sink_kernel(tc, qT, cT, ts, sink, ch, offs, out):
         product(0)
         nc.vector.reciprocal(out=rl[:], in_=total[:])
         weights(1)
-        epilogue(0, 0, nc.scalar)
         quant_weights(1)
         product(1)
+        epilogue(0, 0, nc.scalar)
         epilogue(0, 1, nc.sync)
         epilogue(1, 0, nc.scalar)
         epilogue(1, 1, nc.sync)

@@ -127,16 +127,17 @@ def tile_attend_x_mla_sink_kernel(tc, qT, cT, ts, sink, ch, offs, out):
         def gather_part(t, lo, hi):
             nc.vector.tensor_copy(plane_cols(t)[:, lo:hi], planes[t][:].indirect(offsets[:, lo // 16:hi // 16]))
 
-        def turn(t):
+        def turn(t, seqs):
             words = plane_cols(t).bitcast(F32)
-            tile["v", t] = bank("vps")
-            for b in range(B):
+            rows = bank("vps")
+            for b in seqs:
+                tile["v", t, b] = rows
                 for u in range(2):
                     k = 2 * b + u
-                    nc.tensor.transpose(tile["v", t][:, k * P:(k + 1) * P], words[:, b * H + u:(b + 1) * H:2], ident[:])
+                    nc.tensor.transpose(rows[:, k * P:(k + 1) * P], words[:, b * H + u:(b + 1) * H:2], ident[:])
 
         def values(t, b):
-            src = tile["v", t][:, b * H:(b + 1) * H].rearrange("m (u h p) -> m h p u", u=2, h=2)
+            src = tile["v", t, b][:, b * H:(b + 1) * H].rearrange("m (u h p) -> m h p u", u=2, h=2)
             nc.scalar.copy(out=stage(t // 2, b).bitcast(F32).rearrange("m (h t p u) -> m h t p u", h=2, t=2, u=2)[:, :, t % 2], in_=src)
 
         def stage(pair, b):
@@ -217,7 +218,7 @@ def tile_attend_x_mla_sink_kernel(tc, qT, cT, ts, sink, ch, offs, out):
 
         ts_gather()
         gather(0)
-        turn(0)
+        turn(0, (0, 1))
         values(0, 0)
         values(0, 1)
         ts_spread()
@@ -226,14 +227,15 @@ def tile_attend_x_mla_sink_kernel(tc, qT, cT, ts, sink, ch, offs, out):
         gather_part(1, H, N)
         keys(1, 0, N, 0, "D")
         load_q()
-        turn(1)
-        values(1, 0)
+        turn(1, (1,))
         values(1, 1)
+        turn(1, (0,))
+        values(1, 0)
         keys(0, 0, H, 0, "A")
         keys(0, H, N, 0, "A")
         gather(2)
         nc.sync.dma_start(out=a[:, :, N:N + 1], in_=sink.rearrange("b q o -> q b o"))
-        turn(2)
+        turn(2, (0, 1))
         quant_values(0, 0)
         quant_values(1, 0, [0])
         gather_part(3, 0, H)
@@ -247,7 +249,7 @@ def tile_attend_x_mla_sink_kernel(tc, qT, cT, ts, sink, ch, offs, out):
         keys(1, H, N, 1, "D")
         keys(1, 0, H, 1, "A")
         query(1)
-        turn(3)
+        turn(3, (0, 1))
         quant_query(0)
         quant_keys(0, 0, H)
         scores(0, 0, H)

@@ -7,6 +7,7 @@ B, N, T, D, NQ = 2, 512, 2048, 512, 128
 P = 128
 H = N // 2
 PLANE = 4 * T + 256
+ROW = N + 8
 FLOPS = 4 * B * N * D * NQ
 
 F32 = mybir.dt.float32
@@ -45,7 +46,7 @@ def tile_attend_x_mla_sink_kernel(tc, qT, cT, ts, sink, ch, offs, out):
         offsets = lists.tile([P, B * N // 16], U16, name="offsets")
         nc.sync.dma_start(offsets[:], offs)
         tsw = sb([P, T], F32, "tsw")
-        nc.sync.dma_start(out=tsw[P - 1:P, :], in_=ts[0:1, :])
+        nc.scalar.dma_start(out=tsw[P - 1:P, :], in_=ts[0:1, :])
         nc.vector.memset(tsw[0:P - 1, :], 0.0)
 
         cv = cT.rearrange("(p t) c -> p t c", t=4)
@@ -55,6 +56,13 @@ def tile_attend_x_mla_sink_kernel(tc, qT, cT, ts, sink, ch, offs, out):
             nc.sync.dma_start(out=pl[:], in_=cv[:, t, :])
             planes.append(pl)
 
+        qraw = [sb([P, 4, NQ], F32, f"qraw{b}") for b in range(B)]
+        for b in range(B):
+            nc.sync.dma_start(out=qraw[b][:], in_=qT[b].rearrange("(p t) q -> p t q", t=4))
+        a = sb([P, B * ROW], F32, "a")
+        nc.sync.dma_start(out=a[:].rearrange("q (b c) -> q b c", b=B)[:, :, N:N + 1], in_=sink.rearrange("b q o -> q b o"))
+        chs = sb([P, D], F32, "chs")
+        nc.sync.dma_start(out=chs[:], in_=ch)
 
         ident = sb([P, P], F32, "ident")
         make_identity(nc, ident[:])
@@ -76,15 +84,15 @@ def tile_attend_x_mla_sink_kernel(tc, qT, cT, ts, sink, ch, offs, out):
         tsb = [sb([P, N], F32, f"tsb{b}") for b in range(B)]
         qq = [sb([P, NQ], U32, f"qq{b}") for b in range(B)]
         qs = [sb([P, NQ], U8, f"qs{b}") for b in range(B)]
-        ki = [placed([P, 4 * N], BF16, "ki0", 4 * PLANE), sb([P, 4 * N], BF16, "ki1")]
-        kq = [placed([P, N], U32, "kq0", PLANE), sb([P, N], U32, "kq1")]
+        ki0 = placed([P, 4 * N], BF16, "ki0", 4 * PLANE)
+        ki = {(0, 0): ki0[:, 0:4 * H], (0, H): ki0[:, 4 * H:], (1, 0): sb([P, 4 * H], BF16, "ki1")[:], (1, H): a[:, 0:N].bitcast(BF16)}
+        kq = [sb([P, N], U32, f"kq{b}") for b in range(B)]
         ks = [sb([P, N], U8, f"ks{b}") for b in range(B)]
         p = [sb([P, N + 1], F32, f"p{b}") for b in range(B)]
         wi = [sb([P, NQ, 4], BF16, f"wi{b}") for b in range(B)]
         wq = [sb([P, NQ], U32, f"wq{b}") for b in range(B)]
         ws = [sb([P, NQ], U8, f"ws{b}") for b in range(B)]
         o = [placed([P, D], F32, "o0", 4 * PLANE + 12 * N), sb([P, D], F32, "o1")]
-        a = placed([P, B, 520], F32, "a", 2 * PLANE - 4096)
         tile = {}
 
         def plane_cols(t):
@@ -94,15 +102,6 @@ def tile_attend_x_mla_sink_kernel(tc, qT, cT, ts, sink, ch, offs, out):
         def interleave(eng, dst, src):
             copy = nc.scalar.copy if eng == "A" else nc.vector.tensor_copy
             copy(out=dst.rearrange("p (c i) t -> p c t i", i=4), in_=src.rearrange("p t (c i) -> p c t i", i=4))
-
-        def load_q():
-            for b in range(B):
-                tile["q", b] = placed([P, 4, NQ], F32, f"qraw{b}", PLANE + 16 * NQ * b)
-                nc.sync.dma_start(out=tile["q", b][:], in_=qT[b].rearrange("(p t) q -> p t q", t=4))
-
-        def load_ch():
-            tile["ch"] = placed([P, D], F32, "ch_sb", 3 * PLANE + 2048)
-            nc.sync.dma_start(out=tile["ch"][:], in_=ch)
 
         def ts_gather():
             nc.vector.tensor_copy(tsg[:], tsw[:].indirect(offsets[:]))
@@ -121,10 +120,7 @@ def tile_attend_x_mla_sink_kernel(tc, qT, cT, ts, sink, ch, offs, out):
                     nc.tensor.transpose(rows[:, s * P:(s + 1) * P], tsc[b][:, s:s + 1].to_broadcast([P, P]), ident[:])
                 nc.scalar.copy(out=tsb[b][:], in_=rows[:])
 
-        def gather(t):
-            nc.vector.tensor_copy(plane_cols(t), planes[t][:].indirect(offsets[:]))
-
-        def gather_part(t, lo, hi):
+        def gather_v(t, lo, hi):
             nc.vector.tensor_copy(plane_cols(t)[:, lo:hi], planes[t][:].indirect(offsets[:, lo // 16:hi // 16]))
 
         def turn(t, seqs):
@@ -142,7 +138,7 @@ def tile_attend_x_mla_sink_kernel(tc, qT, cT, ts, sink, ch, offs, out):
 
         def stage(pair, b):
             if pair == 1:
-                return ki[0][:, 2 * b * N:2 * (b + 1) * N]
+                return ki0[:, 2 * b * N:2 * (b + 1) * N]
             return early1[:] if b == 1 else g[:, 3 * B * N:]
 
         def quant_values(b, pair, halves=range(2)):
@@ -156,36 +152,35 @@ def tile_attend_x_mla_sink_kernel(tc, qT, cT, ts, sink, ch, offs, out):
                 tile["qi", b] = placed([P, NQ * 4], BF16, "qi", 4 * PLANE + 8 * N)[:]
             else:
                 tile["qi", b] = placed([P, NQ * 4], BF16, "qi1", 4 * PLANE + 10 * N)[:]
-            interleave("A", tile["qi", b].rearrange("p (q t) -> p q t", t=4), tile["q", b][:])
+            interleave("A", tile["qi", b].rearrange("p (q t) -> p q t", t=4), qraw[b][:])
 
         def quant_query(b):
             nc.vector.quantize_mx(out=qq[b][:].bitcast(FP8X4), scales=qs[b][:], in_=tile["qi", b])
 
-        def keys(b, lo, hi, pair, eng):
+        def keys(b, lo, pair, eng):
             copy = nc.scalar.copy if eng == "A" else nc.vector.tensor_copy
-            copy(out=ki[b][:].rearrange("p (s t) -> p s t", t=4)[:, lo:hi, 2 * pair:2 * pair + 2],
-                 in_=g[:, 2 * pair * B * N:(2 * pair + 2) * B * N].rearrange("p (t s) -> p s t", t=2)[:, b * N + lo:b * N + hi])
+            copy(out=ki[b, lo].rearrange("p (s t) -> p s t", t=4)[:, :, 2 * pair:2 * pair + 2],
+                 in_=g[:, 2 * pair * B * N:(2 * pair + 2) * B * N].rearrange("p (t s) -> p s t", t=2)[:, b * N + lo:b * N + lo + H])
 
-        def quant_keys(b, lo, hi):
-            nc.vector.quantize_mx(out=kq[b][:, lo:hi].bitcast(FP8X4), scales=ks[b][:, lo:hi], in_=ki[b][:, 4 * lo:4 * hi])
+        def quant_keys(b, lo):
+            nc.vector.quantize_mx(out=kq[b][:, lo:lo + H].bitcast(FP8X4), scales=ks[b][:, lo:lo + H], in_=ki[b, lo])
 
-        def scores(b, lo, hi):
-            if lo == 0:
-                tile["s", b] = seq_bank("sps", b)
-            nc.tensor.matmul_mx(tile["s", b][:, lo:hi], lhsT=qq[b][:].bitcast(FP8X4), lhsT_scale=qs[b][:],
-                                rhs=kq[b][:, lo:hi].bitcast(FP8X4), rhs_scale=ks[b][:, lo:hi], start=True, stop=True)
+        def scores(b, lo, rows):
+            tile["s", b, lo] = rows
+            nc.tensor.matmul_mx(rows[:, lo:lo + H], lhsT=qq[b][:].bitcast(FP8X4), lhsT_scale=qs[b][:],
+                                rhs=kq[b][:, lo:lo + H].bitcast(FP8X4), rhs_scale=ks[b][:, lo:lo + H], start=True, stop=True)
 
-        def scaled(b):
-            nc.vector.tensor_tensor(out=a[:, b, 0:N].rearrange("q (s m) -> q s m", s=4),
-                                    in0=tile["s", b][:].rearrange("q (m s) -> q s m", s=4),
-                                    in1=tsb[b][:].rearrange("q (s m) -> q s m", s=4), op=MULT)
+        def scaled(b, lo, hi):
+            nc.vector.tensor_tensor(out=a[:, b * ROW:b * ROW + N].rearrange("q (s m) -> q s m", s=4)[:, :, lo // 4:hi // 4],
+                                    in0=tile["s", b, lo][:, lo:hi].rearrange("q (m s) -> q s m", s=4),
+                                    in1=tsb[b][:].rearrange("q (s m) -> q s m", s=4)[:, :, lo // 4:hi // 4], op=MULT)
 
         def row_max(b):
-            nc.vector.tensor_reduce(out=nm[b][:], in_=a[:, b, 0:N + 1], axis=AX, op=MAX, negate=True)
+            nc.vector.tensor_reduce(out=nm[b][:], in_=a[:, b * ROW:b * ROW + N + 1], axis=AX, op=MAX, negate=True)
 
         def expo(b):
             for i, (lo, hi) in enumerate(((0, H), (H, N + 1))):
-                nc.scalar.activation(out=p[b][:, lo:hi], in_=a[:, b, lo:hi], func=EXP, bias=nm[b][:], scale=1.0,
+                nc.scalar.activation(out=p[b][:, lo:hi], in_=a[:, b * ROW + lo:b * ROW + hi], func=EXP, bias=nm[b][:], scale=1.0,
                                      accum_out=lsum[b][:, i:i + 1])
             nc.scalar.activation(out=total[:, b:b + 1], in_=lsum[b][:, 0:1], func=IDENTITY, bias=lsum[b][:, 1:2], scale=1.0)
 
@@ -213,69 +208,70 @@ def tile_attend_x_mla_sink_kernel(tc, qT, cT, ts, sink, ch, offs, out):
             nc.vector.scalar_tensor_tensor(
                 out=o[b][:, cols].rearrange("q (p t) -> q p t", t=4),
                 in0=tile["y", b, h][:, 0:H].rearrange("q (t p) -> q p t", t=4),
-                scalar=rl[:, b:b + 1], in1=tile["ch"][:, cols].rearrange("q (p t) -> q p t", t=4), op0=MULT, op1=MULT)
+                scalar=rl[:, b:b + 1], in1=chs[:, cols].rearrange("q (p t) -> q p t", t=4), op0=MULT, op1=MULT)
             queue.dma_start(out=out[b][:, cols], in_=o[b][:, cols])
 
         ts_gather()
-        gather(0)
+        gather_v(0, 0, B * N)
         turn(0, (0, 1))
         values(0, 0)
         values(0, 1)
         ts_spread()
-        gather_part(1, 0, H)
-        gather_part(1, N, B * N)
-        gather_part(1, H, N)
-        keys(1, 0, N, 0, "D")
-        load_q()
+        gather_v(1, 0, H)
+        gather_v(1, N, B * N)
+        gather_v(1, H, N)
+        keys(1, 0, 0, "D")
+        keys(1, H, 0, "D")
         turn(1, (1,))
         values(1, 1)
         turn(1, (0,))
         values(1, 0)
-        keys(0, 0, H, 0, "A")
-        keys(0, H, N, 0, "A")
-        gather(2)
-        nc.sync.dma_start(out=a[:, :, N:N + 1], in_=sink.rearrange("b q o -> q b o"))
+        keys(0, 0, 0, "A")
+        keys(0, H, 0, "A")
+        gather_v(2, 0, B * N)
         turn(2, (0, 1))
         quant_values(0, 0)
-        quant_values(1, 0, [0])
-        gather_part(3, 0, H)
-        quant_values(1, 0, [1])
-        gather_part(3, H, N + H)
-        gather_part(3, N + H, B * N)
-        load_ch()
-        keys(0, 0, H, 1, "A")
-        keys(0, H, N, 1, "D")
+        quant_values(1, 0)
+        gather_v(3, 0, H)
+        gather_v(3, H, N + H)
         query(0)
-        keys(1, H, N, 1, "D")
-        keys(1, 0, H, 1, "A")
+        keys(0, 0, 1, "A")
+        keys(0, H, 1, "D")
+        gather_v(3, N + H, B * N)
         query(1)
+        keys(1, 0, 1, "A")
         turn(3, (0, 1))
         quant_query(0)
-        quant_keys(0, 0, H)
-        scores(0, 0, H)
-        quant_keys(0, H, N)
-        scores(0, H, N)
-        quant_keys(1, 0, N)
+        quant_keys(0, H)
+        first = seq_bank("sps", 0)
+        scores(0, H, first)
+        quant_keys(0, 0)
+        scores(0, 0, first)
+        keys(1, H, 1, "D")
         quant_query(1)
-        scores(1, 0, N)
+        quant_keys(1, H)
+        scores(1, H, seq_bank("sps", 1))
         values(2, 0)
         values(3, 0)
         values(2, 1)
         values(3, 1)
-        scaled(0)
+        scaled(0, 0, N)
+        quant_keys(1, 0)
+        scores(1, 0, seq_bank("sps", 0))
         row_max(0)
         expo(0)
-        quant_values(0, 1)
-        scaled(1)
+        scaled(1, H, N)
+        scaled(1, 0, H)
         row_max(1)
+        quant_values(0, 1)
         expo(1)
         turn_p(0)
         turn_p(1)
-        weights(0)
         quant_values(1, 1)
+        weights(0)
+        nc.vector.reciprocal(out=rl[:], in_=total[:])
         quant_weights(0)
         product(0)
-        nc.vector.reciprocal(out=rl[:], in_=total[:])
         weights(1)
         quant_weights(1)
         product(1)

@@ -8,6 +8,7 @@ P = 128
 H = N // 2
 PLANE = 4 * T + 256
 ROW = N + 8
+Q = N // 4
 FLOPS = 4 * B * N * D * NQ
 
 F32 = mybir.dt.float32
@@ -46,7 +47,7 @@ def tile_attend_x_mla_sink_kernel(tc, qT, cT, ts, sink, ch, offs, out):
         offsets = lists.tile([P, B * N // 16], U16, name="offsets")
         nc.sync.dma_start(offsets[:], offs)
         tsw = sb([P, T], F32, "tsw")
-        nc.scalar.dma_start(out=tsw[P - 1:P, :], in_=ts[0:1, :])
+        nc.sync.dma_start(out=tsw[P - 1:P, :], in_=ts[0:1, :])
         nc.vector.memset(tsw[0:P - 1, :], 0.0)
 
         cv = cT.rearrange("(p t) c -> p t c", t=4)
@@ -56,20 +57,15 @@ def tile_attend_x_mla_sink_kernel(tc, qT, cT, ts, sink, ch, offs, out):
             nc.sync.dma_start(out=pl[:], in_=cv[:, t, :])
             planes.append(pl)
 
-        qraw = [sb([P, 4, NQ], F32, f"qraw{b}") for b in range(B)]
-        for b in range(B):
-            nc.sync.dma_start(out=qraw[b][:], in_=qT[b].rearrange("(p t) q -> p t q", t=4))
-        a = sb([P, B * ROW], F32, "a")
-        nc.sync.dma_start(out=a[:].rearrange("q (b c) -> q b c", b=B)[:, :, N:N + 1], in_=sink.rearrange("b q o -> q b o"))
-        chs = sb([P, D], F32, "chs")
-        nc.sync.dma_start(out=chs[:], in_=ch)
-
         ident = sb([P, P], F32, "ident")
         make_identity(nc, ident[:])
         warm = sb([P, 1], F32, "warm")
         nc.gpsimd.memset(warm[:], 0.0)
         nc.scalar.activation(out=warm[:], in_=warm[:], func=EXP)
 
+        qraw = [placed([P, 4, NQ], F32, f"qraw{b}", PLANE + 16 * NQ * b) for b in range(B)]
+        a = placed([P, B * ROW], F32, "a", PLANE + 32 * NQ)
+        chs = placed([P, D], F32, "chs", 3 * PLANE + 2048)
         nm = [sb([P, 1], F32, f"nm{b}") for b in range(B)]
         lsum = [sb([P, 2], F32, f"lsum{b}") for b in range(B)]
         total = sb([P, B], F32, "total")
@@ -86,7 +82,7 @@ def tile_attend_x_mla_sink_kernel(tc, qT, cT, ts, sink, ch, offs, out):
         qs = [sb([P, NQ], U8, f"qs{b}") for b in range(B)]
         ki0 = placed([P, 4 * N], BF16, "ki0", 4 * PLANE)
         ki = {(0, 0): ki0[:, 0:4 * H], (0, H): ki0[:, 4 * H:], (1, 0): sb([P, 4 * H], BF16, "ki1")[:], (1, H): a[:, 0:N].bitcast(BF16)}
-        kq = [sb([P, N], U32, f"kq{b}") for b in range(B)]
+        kq = [placed([P, N], U32, "kq0", PLANE), sb([P, N], U32, "kq1")]
         ks = [sb([P, N], U8, f"ks{b}") for b in range(B)]
         p = [sb([P, N + 1], F32, f"p{b}") for b in range(B)]
         wi = [sb([P, NQ, 4], BF16, f"wi{b}") for b in range(B)]
@@ -102,6 +98,11 @@ def tile_attend_x_mla_sink_kernel(tc, qT, cT, ts, sink, ch, offs, out):
         def interleave(eng, dst, src):
             copy = nc.scalar.copy if eng == "A" else nc.vector.tensor_copy
             copy(out=dst.rearrange("p (c i) t -> p c t i", i=4), in_=src.rearrange("p t (c i) -> p c t i", i=4))
+
+        def load_q():
+            for b in range(B):
+                nc.sync.dma_start(out=qraw[b][:], in_=qT[b].rearrange("(p t) q -> p t q", t=4))
+            nc.sync.dma_start(out=a[:].rearrange("q (b c) -> q b c", b=B)[:, :, N:N + 1], in_=sink.rearrange("b q o -> q b o"))
 
         def ts_gather():
             nc.vector.tensor_copy(tsg[:], tsw[:].indirect(offsets[:]))
@@ -157,10 +158,12 @@ def tile_attend_x_mla_sink_kernel(tc, qT, cT, ts, sink, ch, offs, out):
         def quant_query(b):
             nc.vector.quantize_mx(out=qq[b][:].bitcast(FP8X4), scales=qs[b][:], in_=tile["qi", b])
 
-        def keys(b, lo, pair, eng):
+        def keys(b, lo, hi, pair, eng):
+            first = 0 if b == 0 else lo // H * H
+            dst = ki0[:] if b == 0 else ki[b, first]
             copy = nc.scalar.copy if eng == "A" else nc.vector.tensor_copy
-            copy(out=ki[b, lo].rearrange("p (s t) -> p s t", t=4)[:, :, 2 * pair:2 * pair + 2],
-                 in_=g[:, 2 * pair * B * N:(2 * pair + 2) * B * N].rearrange("p (t s) -> p s t", t=2)[:, b * N + lo:b * N + lo + H])
+            copy(out=dst.rearrange("p (s t) -> p s t", t=4)[:, lo - first:hi - first, 2 * pair:2 * pair + 2],
+                 in_=g[:, 2 * pair * B * N:(2 * pair + 2) * B * N].rearrange("p (t s) -> p s t", t=2)[:, b * N + lo:b * N + hi])
 
         def quant_keys(b, lo):
             nc.vector.quantize_mx(out=kq[b][:, lo:lo + H].bitcast(FP8X4), scales=ks[b][:, lo:lo + H], in_=ki[b, lo])
@@ -220,26 +223,29 @@ def tile_attend_x_mla_sink_kernel(tc, qT, cT, ts, sink, ch, offs, out):
         gather_v(1, 0, H)
         gather_v(1, N, B * N)
         gather_v(1, H, N)
-        keys(1, 0, 0, "D")
-        keys(1, H, 0, "D")
+        load_q()
+        keys(1, 0, H, 0, "D")
+        keys(1, H, N, 0, "D")
         turn(1, (1,))
         values(1, 1)
         turn(1, (0,))
         values(1, 0)
-        keys(0, 0, 0, "A")
-        keys(0, H, 0, "A")
+        keys(0, 0, H, 0, "A")
+        keys(0, H, N, 0, "A")
         gather_v(2, 0, B * N)
         turn(2, (0, 1))
         quant_values(0, 0)
         quant_values(1, 0)
         gather_v(3, 0, H)
-        gather_v(3, H, N + H)
+        gather_v(3, H, N)
         query(0)
-        keys(0, 0, 1, "A")
-        keys(0, H, 1, "D")
-        gather_v(3, N + H, B * N)
+        keys(0, 0, Q, 1, "A")
+        gather_v(3, N, B * N)
+        keys(0, Q, N, 1, "D")
+        nc.sync.dma_start(out=chs[:], in_=ch)
         query(1)
-        keys(1, 0, 1, "A")
+        keys(1, H, N, 1, "A")
+        keys(1, 0, H, 1, "A")
         turn(3, (0, 1))
         quant_query(0)
         quant_keys(0, H)
@@ -247,7 +253,6 @@ def tile_attend_x_mla_sink_kernel(tc, qT, cT, ts, sink, ch, offs, out):
         scores(0, H, first)
         quant_keys(0, 0)
         scores(0, 0, first)
-        keys(1, H, 1, "D")
         quant_query(1)
         quant_keys(1, H)
         scores(1, H, seq_bank("sps", 1))

@@ -20,6 +20,7 @@ FP8X4 = mybir.dt.float8_e4m3fn_x4
 MULT = mybir.AluOpType.mult
 MAX = mybir.AluOpType.max
 IDENTITY = mybir.ActivationFunctionType.Identity
+COPY = mybir.ActivationFunctionType.Copy
 EXP = mybir.ActivationFunctionType.Exp
 AX = mybir.AxisListType.X
 
@@ -63,17 +64,18 @@ def tile_attend_x_mla_sink_kernel(tc, qT, cT, ts, sink, ch, offs, out):
         nc.gpsimd.memset(warm[:], 0.0)
         nc.scalar.activation(out=warm[:], in_=warm[:], func=EXP)
 
-        qraw = [placed([P, 4, NQ], F32, f"qraw{b}", PLANE + 16 * NQ * b) for b in range(B)]
-        a = placed([P, B * ROW], F32, "a", PLANE + 32 * NQ)
+        qraw = [placed([P, 4, NQ], F32, f"qraw{b}", PLANE + 4224 + 16 * NQ * b) for b in range(B)]
+        a = placed([P, B * ROW], F32, "a", PLANE)
         chs = placed([P, D], F32, "chs", 3 * PLANE + 2048)
         nm = [sb([P, 1], F32, f"nm{b}") for b in range(B)]
         lsum = [sb([P, 2], F32, f"lsum{b}") for b in range(B)]
         total = sb([P, B], F32, "total")
         rl = sb([P, B], F32, "rl")
-        g = sb([P, 4 * B * N], BF16, "g")
-        early1 = placed([P, 2 * N], BF16, "early1", 4 * PLANE + 8 * N)
+        g = sb([P, 4 * B * N + N], BF16, "g")
+        early1 = sb([P, 2 * N], BF16, "early1")
         vq = [placed([P, D], U32, f"vq{b}", 2 * PLANE + 4160 + b * 4 * D) for b in range(B)]
         vs = [sb([P, D], U8, f"vs{b}") for b in range(B)]
+        late = [placed([P, 2 * N], BF16, f"late{b}", PLANE + 4224 + 8 * NQ + 4 * N * b) for b in range(B)]
         tsg = sb([P, B * N], F32, "tsg")
         ts4 = [sb([P, 4], F32, "ts4_0"), placed([P, 4], F32, "ts4_1", 4 * PLANE + 12 * N)]
         tsc = [placed([P, 4], F32, f"tsc{b}", 4 * PLANE + 64 * b) for b in range(B)]
@@ -81,8 +83,8 @@ def tile_attend_x_mla_sink_kernel(tc, qT, cT, ts, sink, ch, offs, out):
         qq = [sb([P, NQ], U32, f"qq{b}") for b in range(B)]
         qs = [sb([P, NQ], U8, f"qs{b}") for b in range(B)]
         ki0 = placed([P, 4 * N], BF16, "ki0", 4 * PLANE)
-        ki = {(0, 0): ki0[:, 0:4 * H], (0, H): ki0[:, 4 * H:], (1, 0): sb([P, 4 * H], BF16, "ki1")[:], (1, H): a[:, 0:N].bitcast(BF16)}
-        kq = [placed([P, N], U32, "kq0", PLANE), sb([P, N], U32, "kq1")]
+        ki = {(0, 0): ki0[:, 0:4 * H], (0, H): ki0[:, 4 * H:], (1, 0): a[:, 0:N].bitcast(BF16), (1, H): sb([P, 4 * H], BF16, "ki1")[:]}
+        kq = [sb([P, N], U32, f"kq{b}") for b in range(B)]
         ks = [sb([P, N], U8, f"ks{b}") for b in range(B)]
         p = [sb([P, N + 1], F32, f"p{b}") for b in range(B)]
         wi = [sb([P, NQ, 4], BF16, f"wi{b}") for b in range(B)]
@@ -124,6 +126,9 @@ def tile_attend_x_mla_sink_kernel(tc, qT, cT, ts, sink, ch, offs, out):
         def gather_v(t, lo, hi):
             nc.vector.tensor_copy(plane_cols(t)[:, lo:hi], planes[t][:].indirect(offsets[:, lo // 16:hi // 16]))
 
+        def gather_s(t, lo, hi):
+            nc.scalar.activation(plane_cols(t)[:, lo:hi], planes[t][:].indirect(offsets[:, lo // 16:hi // 16]), COPY)
+
         def turn(t, seqs):
             words = plane_cols(t).bitcast(F32)
             rows = bank("vps")
@@ -139,8 +144,8 @@ def tile_attend_x_mla_sink_kernel(tc, qT, cT, ts, sink, ch, offs, out):
 
         def stage(pair, b):
             if pair == 1:
-                return ki0[:, 2 * b * N:2 * (b + 1) * N]
-            return early1[:] if b == 1 else g[:, 3 * B * N:]
+                return late[b][:]
+            return early1[:] if b == 1 else g[:, 3 * B * N:4 * B * N]
 
         def quant_values(b, pair, halves=range(2)):
             for h in halves:
@@ -148,12 +153,10 @@ def tile_attend_x_mla_sink_kernel(tc, qT, cT, ts, sink, ch, offs, out):
                 nc.vector.quantize_mx(out=vq[b][:, cols].bitcast(FP8X4), scales=vs[b][:, cols],
                                       in_=stage(pair, b)[:, h * N:(h + 1) * N])
 
-        def query(b):
-            if b == 0:
-                tile["qi", b] = placed([P, NQ * 4], BF16, "qi", 4 * PLANE + 8 * N)[:]
-            else:
-                tile["qi", b] = placed([P, NQ * 4], BF16, "qi1", 4 * PLANE + 10 * N)[:]
-            interleave("A", tile["qi", b].rearrange("p (q t) -> p q t", t=4), qraw[b][:])
+        def query(b, eng):
+            first = 4 * B * N - H + b * H
+            tile["qi", b] = g[:, first:first + 4 * NQ]
+            interleave(eng, tile["qi", b].rearrange("p (q t) -> p q t", t=4), qraw[b][:])
 
         def quant_query(b):
             nc.vector.quantize_mx(out=qq[b][:].bitcast(FP8X4), scales=qs[b][:], in_=tile["qi", b])
@@ -234,39 +237,42 @@ def tile_attend_x_mla_sink_kernel(tc, qT, cT, ts, sink, ch, offs, out):
         keys(0, H, N, 0, "A")
         gather_v(2, 0, B * N)
         turn(2, (0, 1))
-        quant_values(0, 0)
         quant_values(1, 0)
+        quant_values(0, 0)
         gather_v(3, 0, H)
+        gather_s(3, N, N + H)
         gather_v(3, H, N)
-        query(0)
         keys(0, 0, Q, 1, "A")
-        gather_v(3, N, B * N)
-        keys(0, Q, N, 1, "D")
-        nc.sync.dma_start(out=chs[:], in_=ch)
-        query(1)
-        keys(1, H, N, 1, "A")
+        keys(0, Q, H, 1, "D")
+        keys(0, H, N, 1, "D")
+        query(0, "A")
         keys(1, 0, H, 1, "A")
-        turn(3, (0, 1))
-        quant_query(0)
-        quant_keys(0, H)
-        first = seq_bank("sps", 0)
-        scores(0, H, first)
+        turn(3, (0,))
         quant_keys(0, 0)
+        quant_keys(0, H)
+        quant_query(0)
+        first = seq_bank("sps", 0)
         scores(0, 0, first)
+        scores(0, H, first)
+        gather_v(3, N + H, B * N)
+        nc.sync.dma_start(out=chs[:], in_=ch)
+        keys(1, H, N, 1, "A")
+        turn(3, (1,))
+        query(1, "D")
+        quant_keys(1, 0)
         quant_query(1)
-        quant_keys(1, H)
-        scores(1, H, seq_bank("sps", 1))
+        scores(1, 0, seq_bank("sps", 1))
         values(2, 0)
         values(3, 0)
         values(2, 1)
         values(3, 1)
         scaled(0, 0, N)
-        quant_keys(1, 0)
-        scores(1, 0, seq_bank("sps", 0))
+        quant_keys(1, H)
+        scores(1, H, seq_bank("sps", 0))
         row_max(0)
         expo(0)
-        scaled(1, H, N)
         scaled(1, 0, H)
+        scaled(1, H, N)
         row_max(1)
         quant_values(0, 1)
         expo(1)

@@ -5,11 +5,18 @@ from concourse.masks import make_identity
 
 B, N, T, D, NQ = 2, 512, 2048, 512, 128
 P = 128
-H = N // 2
-PLANE = 4 * T + 256
+HALF = N // 2
+QUARTER = N // 4
 ROW = N + 8
-Q = N // 4
 FLOPS = 4 * B * N * D * NQ
+
+PLANE = 4 * T + 256
+QUERIES_AT = PLANE + 33 * 128
+LATE_VALUES_AT = QUERIES_AT + 8 * NQ
+VALUE_CODES_AT = 2 * PLANE + 65 * 64
+CHANNELS_AT = 3 * PLANE + 4 * D
+FIRST_KEYS_AT = 4 * PLANE
+FIRST_RESULT_AT = FIRST_KEYS_AT + 12 * N
 
 F32 = mybir.dt.float32
 BF16 = mybir.dt.bfloat16
@@ -27,266 +34,269 @@ AX = mybir.AxisListType.X
 
 def tile_attend_x_mla_sink_kernel(tc, qT, cT, ts, sink, ch, offs, out):
     nc = tc.nc
+    on_scalar, on_vector = nc.scalar.copy, nc.vector.tensor_copy
     with ExitStack() as ctx:
         lists = ctx.enter_context(tc.tile_pool(name="lists", bufs=1))
         keep = ctx.enter_context(tc.tile_pool(name="keep", bufs=1))
-        ring = ctx.enter_context(tc.tile_pool(name="ring", bufs=1))
+        shared = ctx.enter_context(tc.tile_pool(name="shared", bufs=1))
         psum = ctx.enter_context(tc.psum_pool(name="psum", bufs=1))
 
-        def sb(shape, dtype, name):
+        def own(shape, dtype, name):
             return keep.tile(shape, dtype, name=name, align_bytes=64)
 
         def placed(shape, dtype, name, offset):
-            return ring.tile(shape, dtype, name=name, offset=offset, align_bytes=64)
+            return shared.tile(shape, dtype, name=name, offset=offset, align_bytes=64)
 
-        def bank(name):
-            return psum.tile([P, 512], F32, name=name, tag="x", bufs=4)
+        def turn_bank(name):
+            return psum.tile([P, 512], F32, name=name, tag="turn", bufs=4)
 
-        def seq_bank(name, b):
-            return psum.tile([P, 512], F32, name=name, tag=f"s{b}", bufs=2)
+        def product_bank(name, pair):
+            return psum.tile([P, 512], F32, name=name, tag=f"product{pair}", bufs=2)
 
         offsets = lists.tile([P, B * N // 16], U16, name="offsets")
         nc.sync.dma_start(offsets[:], offs)
-        tsw = sb([P, T], F32, "tsw")
-        nc.sync.dma_start(out=tsw[P - 1:P, :], in_=ts[0:1, :])
-        nc.vector.memset(tsw[0:P - 1, :], 0.0)
+        ts_window = own([P, T], F32, "ts_window")
+        nc.sync.dma_start(out=ts_window[P - 1:P, :], in_=ts[0:1, :])
+        nc.vector.memset(ts_window[0:P - 1, :], 0.0)
 
-        cv = cT.rearrange("(p t) c -> p t c", t=4)
+        pool_rows = cT.rearrange("(r t) c -> r t c", t=4)
         planes = []
         for t in range(4):
-            pl = placed([P, T], F32, f"plane{t}", t * PLANE)
-            nc.sync.dma_start(out=pl[:], in_=cv[:, t, :])
-            planes.append(pl)
+            plane = placed([P, T], F32, f"plane{t}", t * PLANE)
+            nc.sync.dma_start(out=plane[:], in_=pool_rows[:, t, :])
+            planes.append(plane)
 
-        ident = sb([P, P], F32, "ident")
+        ident = own([P, P], F32, "ident")
         make_identity(nc, ident[:])
-        warm = sb([P, 1], F32, "warm")
+        warm = own([P, 1], F32, "warm")
         nc.gpsimd.memset(warm[:], 0.0)
         nc.scalar.activation(out=warm[:], in_=warm[:], func=EXP)
 
-        qraw = [placed([P, 4, NQ], F32, f"qraw{b}", PLANE + 4224 + 16 * NQ * b) for b in range(B)]
-        a = placed([P, B * ROW], F32, "a", PLANE)
-        chs = placed([P, D], F32, "chs", 3 * PLANE + 2048)
-        nm = [sb([P, 1], F32, f"nm{b}") for b in range(B)]
-        lsum = [sb([P, 2], F32, f"lsum{b}") for b in range(B)]
-        total = sb([P, B], F32, "total")
-        rl = sb([P, B], F32, "rl")
-        g = sb([P, 4 * B * N + N], BF16, "g")
-        early1 = sb([P, 2 * N], BF16, "early1")
-        vq = [placed([P, D], U32, f"vq{b}", 2 * PLANE + 4160 + b * 4 * D) for b in range(B)]
-        vs = [sb([P, D], U8, f"vs{b}") for b in range(B)]
-        late = [placed([P, 2 * N], BF16, f"late{b}", PLANE + 4224 + 8 * NQ + 4 * N * b) for b in range(B)]
-        tsg = sb([P, B * N], F32, "tsg")
-        ts4 = [sb([P, 4], F32, "ts4_0"), placed([P, 4], F32, "ts4_1", 4 * PLANE + 12 * N)]
-        tsc = [placed([P, 4], F32, f"tsc{b}", 4 * PLANE + 64 * b) for b in range(B)]
-        tsb = [sb([P, N], F32, f"tsb{b}") for b in range(B)]
-        qq = [sb([P, NQ], U32, f"qq{b}") for b in range(B)]
-        qs = [sb([P, NQ], U8, f"qs{b}") for b in range(B)]
-        ki0 = placed([P, 4 * N], BF16, "ki0", 4 * PLANE)
-        ki = {(0, 0): ki0[:, 0:4 * H], (0, H): ki0[:, 4 * H:], (1, 0): a[:, 0:N].bitcast(BF16), (1, H): sb([P, 4 * H], BF16, "ki1")[:]}
-        kq = [sb([P, N], U32, f"kq{b}") for b in range(B)]
-        ks = [sb([P, N], U8, f"ks{b}") for b in range(B)]
-        p = [sb([P, N + 1], F32, f"p{b}") for b in range(B)]
-        wi = [sb([P, NQ, 4], BF16, f"wi{b}") for b in range(B)]
-        wq = [sb([P, NQ], U32, f"wq{b}") for b in range(B)]
-        ws = [sb([P, NQ], U8, f"ws{b}") for b in range(B)]
-        o = [placed([P, D], F32, "o0", 4 * PLANE + 12 * N), sb([P, D], F32, "o1")]
-        tile = {}
+        raw_query = [placed([P, 4, NQ], F32, f"raw_query{b}", QUERIES_AT + 16 * NQ * b) for b in range(B)]
+        scaled = placed([P, B * ROW], F32, "scaled", PLANE)
+        channels = placed([P, D], F32, "channels", CHANNELS_AT)
+        neg_max = [own([P, 1], F32, f"neg_max{b}") for b in range(B)]
+        part_sum = [own([P, 2], F32, f"part_sum{b}") for b in range(B)]
+        row_sum = own([P, B], F32, "row_sum")
+        inv_sum = own([P, B], F32, "inv_sum")
+        gathered = own([P, 4 * B * N + N], BF16, "gathered")
+        early_values1 = own([P, 2 * N], BF16, "early_values1")
+        value_codes = [placed([P, D], U32, f"value_codes{b}", VALUE_CODES_AT + b * 4 * D) for b in range(B)]
+        value_scales = [own([P, D], U8, f"value_scales{b}") for b in range(B)]
+        late_values = [placed([P, 2 * N], BF16, f"late_values{b}", LATE_VALUES_AT + 4 * N * b) for b in range(B)]
+        staged_values = {(0, 0): gathered[:, 3 * B * N:4 * B * N], (0, 1): early_values1[:],
+                         (1, 0): late_values[0][:], (1, 1): late_values[1][:]}
+        ts_row = own([P, B * N], F32, "ts_row")
+        ts_cols = [own([P, 4], F32, "ts_cols0"), placed([P, 4], F32, "ts_cols1", FIRST_RESULT_AT)]
+        ts_source = [placed([P, 4], F32, f"ts_source{b}", FIRST_KEYS_AT + 64 * b) for b in range(B)]
+        ts_spread = [own([P, N], F32, f"ts_spread{b}") for b in range(B)]
+        query_codes = [own([P, NQ], U32, f"query_codes{b}") for b in range(B)]
+        query_scales = [own([P, NQ], U8, f"query_scales{b}") for b in range(B)]
+        first_keys = placed([P, 4 * N], BF16, "first_keys", FIRST_KEYS_AT)
+        key_halves = {(0, 0): first_keys[:, 0:4 * HALF], (0, HALF): first_keys[:, 4 * HALF:],
+                      (1, 0): scaled[:, 0:N].bitcast(BF16), (1, HALF): own([P, 4 * HALF], BF16, "last_keys")[:]}
+        key_codes = [own([P, N], U32, f"key_codes{b}") for b in range(B)]
+        key_scales = [own([P, N], U8, f"key_scales{b}") for b in range(B)]
+        p = [own([P, N + 1], F32, f"p{b}") for b in range(B)]
+        w = [own([P, NQ, 4], BF16, f"w{b}") for b in range(B)]
+        w_codes = [own([P, NQ], U32, f"w_codes{b}") for b in range(B)]
+        w_scales = [own([P, NQ], U8, f"w_scales{b}") for b in range(B)]
+        result = [placed([P, D], F32, "result0", FIRST_RESULT_AT), own([P, D], F32, "result1")]
+        banks = {}
 
         def plane_cols(t):
-            return g[:, t * B * N:(t + 1) * B * N]
+            return gathered[:, t * B * N:(t + 1) * B * N]
 
+        def staged_query(b):
+            first = 4 * B * N - HALF + b * HALF
+            return gathered[:, first:first + 4 * NQ]
 
-        def interleave(eng, dst, src):
-            copy = nc.scalar.copy if eng == "A" else nc.vector.tensor_copy
-            copy(out=dst.rearrange("p (c i) t -> p c t i", i=4), in_=src.rearrange("p t (c i) -> p c t i", i=4))
-
-        def load_q():
+        def load_queries_and_sinks():
             for b in range(B):
-                nc.sync.dma_start(out=qraw[b][:], in_=qT[b].rearrange("(p t) q -> p t q", t=4))
-            nc.sync.dma_start(out=a[:].rearrange("q (b c) -> q b c", b=B)[:, :, N:N + 1], in_=sink.rearrange("b q o -> q b o"))
+                nc.sync.dma_start(out=raw_query[b][:], in_=qT[b].rearrange("(r t) q -> r t q", t=4))
+            nc.sync.dma_start(out=scaled[:].rearrange("q (b c) -> q b c", b=B)[:, :, N:N + 1], in_=sink.rearrange("b q o -> q b o"))
 
-        def ts_gather():
-            nc.vector.tensor_copy(tsg[:], tsw[:].indirect(offsets[:]))
+        def gather_ts():
+            nc.vector.tensor_copy(ts_row[:], ts_window[:].indirect(offsets[:]))
             for b in range(B):
-                tile["t", b] = bank("tps")
+                banks["ts", b] = turn_bank("ts_turned")
                 for s in range(4):
-                    nc.tensor.transpose(tile["t", b][:, s * P:(s + 1) * P], tsg[:, b * N + s:(b + 1) * N:4], ident[:])
+                    nc.tensor.transpose(banks["ts", b][:, s * P:(s + 1) * P], ts_row[:, b * N + s:(b + 1) * N:4], ident[:])
 
-        def ts_spread():
+        def spread_ts():
             for b in range(B):
-                nc.scalar.copy(out=tsc[b][:], in_=tile["t", b][:, P - 1:512:P])
-                nc.scalar.copy(out=ts4[b][:], in_=tile["t", b][:, P - 1:512:P])
+                nc.scalar.copy(out=ts_source[b][:], in_=banks["ts", b][:, P - 1:512:P])
+                nc.scalar.copy(out=ts_cols[b][:], in_=banks["ts", b][:, P - 1:512:P])
             for b in range(B):
-                rows = bank("tbs")
+                rows = turn_bank("ts_rows")
                 for s in range(4):
-                    nc.tensor.transpose(rows[:, s * P:(s + 1) * P], tsc[b][:, s:s + 1].to_broadcast([P, P]), ident[:])
-                nc.scalar.copy(out=tsb[b][:], in_=rows[:])
+                    nc.tensor.transpose(rows[:, s * P:(s + 1) * P], ts_source[b][:, s:s + 1].to_broadcast([P, P]), ident[:])
+                nc.scalar.copy(out=ts_spread[b][:], in_=rows[:])
 
-        def gather_v(t, lo, hi):
+        def gather_on_vector(t, lo, hi):
             nc.vector.tensor_copy(plane_cols(t)[:, lo:hi], planes[t][:].indirect(offsets[:, lo // 16:hi // 16]))
 
-        def gather_s(t, lo, hi):
+        def gather_on_scalar(t, lo, hi):
             nc.scalar.activation(plane_cols(t)[:, lo:hi], planes[t][:].indirect(offsets[:, lo // 16:hi // 16]), COPY)
 
-        def turn(t, seqs):
+        def turn_values(t, seqs):
             words = plane_cols(t).bitcast(F32)
-            rows = bank("vps")
+            rows = turn_bank("values_turned")
             for b in seqs:
-                tile["v", t, b] = rows
+                banks["values", t, b] = rows
                 for u in range(2):
                     k = 2 * b + u
-                    nc.tensor.transpose(rows[:, k * P:(k + 1) * P], words[:, b * H + u:(b + 1) * H:2], ident[:])
+                    nc.tensor.transpose(rows[:, k * P:(k + 1) * P], words[:, b * HALF + u:(b + 1) * HALF:2], ident[:])
 
-        def values(t, b):
-            src = tile["v", t, b][:, b * H:(b + 1) * H].rearrange("m (u h p) -> m h p u", u=2, h=2)
-            nc.scalar.copy(out=stage(t // 2, b).bitcast(F32).rearrange("m (h t p u) -> m h t p u", h=2, t=2, u=2)[:, :, t % 2], in_=src)
+        def copy_values(t, b):
+            src = banks["values", t, b][:, b * HALF:(b + 1) * HALF].rearrange("m (u h r) -> m h r u", u=2, h=2)
+            dst = staged_values[t // 2, b].bitcast(F32).rearrange("m (h t r u) -> m h t r u", h=2, t=2, u=2)
+            nc.scalar.copy(out=dst[:, :, t % 2], in_=src)
 
-        def stage(pair, b):
-            if pair == 1:
-                return late[b][:]
-            return early1[:] if b == 1 else g[:, 3 * B * N:4 * B * N]
-
-        def quant_values(b, pair, halves=range(2)):
+        def quantise_values(b, pair, halves=range(2)):
             for h in halves:
-                cols = slice(h * H + pair * P, h * H + (pair + 1) * P)
-                nc.vector.quantize_mx(out=vq[b][:, cols].bitcast(FP8X4), scales=vs[b][:, cols],
-                                      in_=stage(pair, b)[:, h * N:(h + 1) * N])
+                cols = slice(h * HALF + pair * P, h * HALF + (pair + 1) * P)
+                nc.vector.quantize_mx(out=value_codes[b][:, cols].bitcast(FP8X4), scales=value_scales[b][:, cols],
+                                      in_=staged_values[pair, b][:, h * N:(h + 1) * N])
 
-        def query(b, eng):
-            first = 4 * B * N - H + b * H
-            tile["qi", b] = g[:, first:first + 4 * NQ]
-            interleave(eng, tile["qi", b].rearrange("p (q t) -> p q t", t=4), qraw[b][:])
+        def copy_query(b, copy):
+            dst = staged_query(b).rearrange("r (q t) -> r q t", t=4)
+            copy(out=dst.rearrange("r (c i) t -> r c t i", i=4), in_=raw_query[b][:].rearrange("r t (c i) -> r c t i", i=4))
 
-        def quant_query(b):
-            nc.vector.quantize_mx(out=qq[b][:].bitcast(FP8X4), scales=qs[b][:], in_=tile["qi", b])
+        def quantise_query(b):
+            nc.vector.quantize_mx(out=query_codes[b][:].bitcast(FP8X4), scales=query_scales[b][:], in_=staged_query(b))
 
-        def keys(b, lo, hi, pair, eng):
-            first = 0 if b == 0 else lo // H * H
-            dst = ki0[:] if b == 0 else ki[b, first]
-            copy = nc.scalar.copy if eng == "A" else nc.vector.tensor_copy
-            copy(out=dst.rearrange("p (s t) -> p s t", t=4)[:, lo - first:hi - first, 2 * pair:2 * pair + 2],
-                 in_=g[:, 2 * pair * B * N:(2 * pair + 2) * B * N].rearrange("p (t s) -> p s t", t=2)[:, b * N + lo:b * N + hi])
+        def copy_keys(b, lo, hi, pair, copy):
+            first = 0 if b == 0 else lo // HALF * HALF
+            dst = first_keys[:] if b == 0 else key_halves[b, first]
+            two_planes = gathered[:, 2 * pair * B * N:(2 * pair + 2) * B * N].rearrange("r (t s) -> r s t", t=2)
+            copy(out=dst.rearrange("r (s t) -> r s t", t=4)[:, lo - first:hi - first, 2 * pair:2 * pair + 2],
+                 in_=two_planes[:, b * N + lo:b * N + hi])
 
-        def quant_keys(b, lo):
-            nc.vector.quantize_mx(out=kq[b][:, lo:lo + H].bitcast(FP8X4), scales=ks[b][:, lo:lo + H], in_=ki[b, lo])
+        def quantise_keys(b, lo):
+            nc.vector.quantize_mx(out=key_codes[b][:, lo:lo + HALF].bitcast(FP8X4), scales=key_scales[b][:, lo:lo + HALF],
+                                  in_=key_halves[b, lo])
 
-        def scores(b, lo, rows):
-            tile["s", b, lo] = rows
-            nc.tensor.matmul_mx(rows[:, lo:lo + H], lhsT=qq[b][:].bitcast(FP8X4), lhsT_scale=qs[b][:],
-                                rhs=kq[b][:, lo:lo + H].bitcast(FP8X4), rhs_scale=ks[b][:, lo:lo + H], start=True, stop=True)
+        def score(b, lo, rows):
+            banks["scores", b, lo] = rows
+            nc.tensor.matmul_mx(rows[:, lo:lo + HALF], lhsT=query_codes[b][:].bitcast(FP8X4), lhsT_scale=query_scales[b][:],
+                                rhs=key_codes[b][:, lo:lo + HALF].bitcast(FP8X4), rhs_scale=key_scales[b][:, lo:lo + HALF],
+                                start=True, stop=True)
 
-        def scaled(b, lo, hi):
-            nc.vector.tensor_tensor(out=a[:, b * ROW:b * ROW + N].rearrange("q (s m) -> q s m", s=4)[:, :, lo // 4:hi // 4],
-                                    in0=tile["s", b, lo][:, lo:hi].rearrange("q (m s) -> q s m", s=4),
-                                    in1=tsb[b][:].rearrange("q (s m) -> q s m", s=4)[:, :, lo // 4:hi // 4], op=MULT)
+        def scale_scores(b, lo, hi):
+            nc.vector.tensor_tensor(out=scaled[:, b * ROW:b * ROW + N].rearrange("q (s m) -> q s m", s=4)[:, :, lo // 4:hi // 4],
+                                    in0=banks["scores", b, lo][:, lo:hi].rearrange("q (m s) -> q s m", s=4),
+                                    in1=ts_spread[b][:].rearrange("q (s m) -> q s m", s=4)[:, :, lo // 4:hi // 4], op=MULT)
 
         def row_max(b):
-            nc.vector.tensor_reduce(out=nm[b][:], in_=a[:, b * ROW:b * ROW + N + 1], axis=AX, op=MAX, negate=True)
+            nc.vector.tensor_reduce(out=neg_max[b][:], in_=scaled[:, b * ROW:b * ROW + N + 1], axis=AX, op=MAX, negate=True)
 
-        def expo(b):
-            for i, (lo, hi) in enumerate(((0, H), (H, N + 1))):
-                nc.scalar.activation(out=p[b][:, lo:hi], in_=a[:, b * ROW + lo:b * ROW + hi], func=EXP, bias=nm[b][:], scale=1.0,
-                                     accum_out=lsum[b][:, i:i + 1])
-            nc.scalar.activation(out=total[:, b:b + 1], in_=lsum[b][:, 0:1], func=IDENTITY, bias=lsum[b][:, 1:2], scale=1.0)
+        def exponentials(b):
+            for i, (lo, hi) in enumerate(((0, HALF), (HALF, N + 1))):
+                nc.scalar.activation(out=p[b][:, lo:hi], in_=scaled[:, b * ROW + lo:b * ROW + hi], func=EXP,
+                                     bias=neg_max[b][:], scale=1.0, accum_out=part_sum[b][:, i:i + 1])
+            nc.scalar.activation(out=row_sum[:, b:b + 1], in_=part_sum[b][:, 0:1], func=IDENTITY,
+                                 bias=part_sum[b][:, 1:2], scale=1.0)
 
         def turn_p(b):
-            tile["p", b] = bank("pps")
+            banks["p", b] = turn_bank("p_turned")
             for s in range(4):
-                nc.tensor.transpose(tile["p", b][:, s * P:(s + 1) * P], p[b][:, s * P:(s + 1) * P], ident[:])
+                nc.tensor.transpose(banks["p", b][:, s * P:(s + 1) * P], p[b][:, s * P:(s + 1) * P], ident[:])
 
-        def weights(b):
-            nc.vector.tensor_tensor(out=wi[b][:], in0=tile["p", b][:].rearrange("m (s q) -> m q s", s=4),
-                                    in1=ts4[b][:].unsqueeze(1).to_broadcast([P, NQ, 4]), op=MULT)
+        def weigh(b):
+            nc.vector.tensor_tensor(out=w[b][:], in0=banks["p", b][:].rearrange("m (s q) -> m q s", s=4),
+                                    in1=ts_cols[b][:].unsqueeze(1).to_broadcast([P, NQ, 4]), op=MULT)
 
-        def quant_weights(b):
-            nc.vector.quantize_mx(out=wq[b][:].bitcast(FP8X4), scales=ws[b][:], in_=wi[b][:].rearrange("m q s -> m (q s)"))
+        def quantise_w(b):
+            nc.vector.quantize_mx(out=w_codes[b][:].bitcast(FP8X4), scales=w_scales[b][:], in_=w[b][:].rearrange("m q s -> m (q s)"))
 
-        def product(b):
+        def multiply_values(b):
             for h in range(2):
-                cols = slice(h * H, (h + 1) * H)
-                tile["y", b, h] = seq_bank("yps", h)
-                nc.tensor.matmul_mx(tile["y", b, h][:, 0:H], lhsT=wq[b][:].bitcast(FP8X4), lhsT_scale=ws[b][:],
-                                    rhs=vq[b][:, cols].bitcast(FP8X4), rhs_scale=vs[b][:, cols], start=True, stop=True)
+                cols = slice(h * HALF, (h + 1) * HALF)
+                banks["y", b, h] = product_bank("y", h)
+                nc.tensor.matmul_mx(banks["y", b, h][:, 0:HALF], lhsT=w_codes[b][:].bitcast(FP8X4), lhsT_scale=w_scales[b][:],
+                                    rhs=value_codes[b][:, cols].bitcast(FP8X4), rhs_scale=value_scales[b][:, cols],
+                                    start=True, stop=True)
 
         def epilogue(b, h, queue):
-            cols = slice(h * H, (h + 1) * H)
+            cols = slice(h * HALF, (h + 1) * HALF)
             nc.vector.scalar_tensor_tensor(
-                out=o[b][:, cols].rearrange("q (p t) -> q p t", t=4),
-                in0=tile["y", b, h][:, 0:H].rearrange("q (t p) -> q p t", t=4),
-                scalar=rl[:, b:b + 1], in1=chs[:, cols].rearrange("q (p t) -> q p t", t=4), op0=MULT, op1=MULT)
-            queue.dma_start(out=out[b][:, cols], in_=o[b][:, cols])
+                out=result[b][:, cols].rearrange("q (r t) -> q r t", t=4),
+                in0=banks["y", b, h][:, 0:HALF].rearrange("q (t r) -> q r t", t=4),
+                scalar=inv_sum[:, b:b + 1], in1=channels[:, cols].rearrange("q (r t) -> q r t", t=4), op0=MULT, op1=MULT)
+            queue.dma_start(out=out[b][:, cols], in_=result[b][:, cols])
 
-        ts_gather()
-        gather_v(0, 0, B * N)
-        turn(0, (0, 1))
-        values(0, 0)
-        values(0, 1)
-        ts_spread()
-        gather_v(1, 0, H)
-        gather_v(1, N, B * N)
-        gather_v(1, H, N)
-        load_q()
-        keys(1, 0, H, 0, "D")
-        keys(1, H, N, 0, "D")
-        turn(1, (1,))
-        values(1, 1)
-        turn(1, (0,))
-        values(1, 0)
-        keys(0, 0, H, 0, "A")
-        keys(0, H, N, 0, "A")
-        gather_v(2, 0, B * N)
-        turn(2, (0, 1))
-        quant_values(1, 0)
-        quant_values(0, 0)
-        gather_v(3, 0, H)
-        gather_s(3, N, N + H)
-        gather_v(3, H, N)
-        keys(0, 0, Q, 1, "A")
-        keys(0, Q, H, 1, "D")
-        keys(0, H, N, 1, "D")
-        query(0, "A")
-        keys(1, 0, H, 1, "A")
-        turn(3, (0,))
-        quant_keys(0, 0)
-        quant_keys(0, H)
-        quant_query(0)
-        first = seq_bank("sps", 0)
-        scores(0, 0, first)
-        scores(0, H, first)
-        gather_v(3, N + H, B * N)
-        nc.sync.dma_start(out=chs[:], in_=ch)
-        keys(1, H, N, 1, "A")
-        turn(3, (1,))
-        query(1, "D")
-        quant_keys(1, 0)
-        quant_query(1)
-        scores(1, 0, seq_bank("sps", 1))
-        values(2, 0)
-        values(3, 0)
-        values(2, 1)
-        values(3, 1)
-        scaled(0, 0, N)
-        quant_keys(1, H)
-        scores(1, H, seq_bank("sps", 0))
+        gather_ts()
+        gather_on_vector(0, 0, B * N)
+        turn_values(0, (0, 1))
+        copy_values(0, 0)
+        copy_values(0, 1)
+        spread_ts()
+        gather_on_vector(1, 0, HALF)
+        gather_on_vector(1, N, B * N)
+        gather_on_vector(1, HALF, N)
+        load_queries_and_sinks()
+        copy_keys(1, 0, HALF, 0, on_vector)
+        copy_keys(1, HALF, N, 0, on_vector)
+        for b in (1, 0):
+            turn_values(1, (b,))
+            copy_values(1, b)
+        copy_keys(0, 0, HALF, 0, on_scalar)
+        copy_keys(0, HALF, N, 0, on_scalar)
+        gather_on_vector(2, 0, B * N)
+        turn_values(2, (0, 1))
+        quantise_values(1, 0)
+        quantise_values(0, 0)
+
+        gather_on_vector(3, 0, HALF)
+        gather_on_scalar(3, N, N + HALF)
+        gather_on_vector(3, HALF, N)
+        copy_keys(0, 0, QUARTER, 1, on_scalar)
+        copy_keys(0, QUARTER, HALF, 1, on_vector)
+        copy_keys(0, HALF, N, 1, on_vector)
+        copy_query(0, on_scalar)
+        copy_keys(1, 0, HALF, 1, on_scalar)
+        turn_values(3, (0,))
+        quantise_keys(0, 0)
+        quantise_keys(0, HALF)
+        quantise_query(0)
+        first_scores = product_bank("scores", 0)
+        score(0, 0, first_scores)
+        score(0, HALF, first_scores)
+
+        gather_on_vector(3, N + HALF, B * N)
+        nc.sync.dma_start(out=channels[:], in_=ch)
+        copy_keys(1, HALF, N, 1, on_scalar)
+        turn_values(3, (1,))
+        copy_query(1, on_vector)
+        quantise_keys(1, 0)
+        quantise_query(1)
+        score(1, 0, product_bank("scores", 1))
+        for b in range(B):
+            copy_values(2, b)
+            copy_values(3, b)
+
+        scale_scores(0, 0, N)
+        quantise_keys(1, HALF)
+        score(1, HALF, product_bank("scores", 0))
         row_max(0)
-        expo(0)
-        scaled(1, 0, H)
-        scaled(1, H, N)
+        exponentials(0)
+        scale_scores(1, 0, HALF)
+        scale_scores(1, HALF, N)
         row_max(1)
-        quant_values(0, 1)
-        expo(1)
+        quantise_values(0, 1)
+        exponentials(1)
         turn_p(0)
         turn_p(1)
-        quant_values(1, 1)
-        weights(0)
-        nc.vector.reciprocal(out=rl[:], in_=total[:])
-        quant_weights(0)
-        product(0)
-        weights(1)
-        quant_weights(1)
-        product(1)
-        epilogue(0, 0, nc.scalar)
-        epilogue(0, 1, nc.sync)
-        epilogue(1, 0, nc.scalar)
-        epilogue(1, 1, nc.sync)
+        quantise_values(1, 1, [0])
+        weigh(0)
+        quantise_values(1, 1, [1])
+        quantise_w(0)
+        multiply_values(0)
+        nc.vector.reciprocal(out=inv_sum[:], in_=row_sum[:])
+        weigh(1)
+        quantise_w(1)
+        multiply_values(1)
+        for b in range(B):
+            epilogue(b, 0, nc.scalar)
+            epilogue(b, 1, nc.sync)

@@ -8,6 +8,7 @@ P = 128
 HALF = N // 2
 QUARTER = N // 4
 ROW = N + 8
+PARTS = (2, 4)
 FLOPS = 4 * B * N * D * NQ
 
 PLANE = 4 * T + 256
@@ -15,8 +16,12 @@ QUERIES_AT = PLANE + 33 * 128
 LATE_VALUES_AT = QUERIES_AT + 8 * NQ
 VALUE_CODES_AT = 2 * PLANE + 65 * 64
 CHANNELS_AT = 3 * PLANE + 4 * D
-FIRST_KEYS_AT = 4 * PLANE
-FIRST_RESULT_AT = FIRST_KEYS_AT + 12 * N
+KEYS_AT = 4 * PLANE
+RESULT_AT = KEYS_AT + 8 * HALF
+BANK = 2048
+
+PLANE_AT = (0, B * N, 2 * B * N, 3 * B * N + HALF)
+FIRST_KEYS_COL = PLANE_AT[3] + N + HALF
 
 F32 = mybir.dt.float32
 BF16 = mybir.dt.bfloat16
@@ -47,16 +52,13 @@ def tile_attend_x_mla_sink_kernel(tc, qT, cT, ts, sink, ch, offs, out):
         def placed(shape, dtype, name, offset):
             return shared.tile(shape, dtype, name=name, offset=offset, align_bytes=64)
 
-        def turn_bank(name):
-            return psum.tile([P, 512], F32, name=name, tag="turn", bufs=4)
+        def bank(name, index):
+            return psum.tile([P, 512], F32, name=name, offset=index * BANK)
 
-        def product_bank(name, pair):
-            return psum.tile([P, 512], F32, name=name, tag=f"product{pair}", bufs=2)
-
-        offsets = lists.tile([P, B * N // 16], U16, name="offsets")
-        nc.sync.dma_start(offsets[:], offs)
         ts_window = own([P, T], F32, "ts_window")
         nc.sync.dma_start(out=ts_window[P - 1:P, :], in_=ts[0:1, :])
+        offsets = lists.tile([P, B * N // 16], U16, name="offsets")
+        nc.sync.dma_start(offsets[:], offs)
         nc.vector.memset(ts_window[0:P - 1, :], 0.0)
 
         pool_rows = cT.rearrange("(r t) c -> r t c", t=4)
@@ -79,37 +81,33 @@ def tile_attend_x_mla_sink_kernel(tc, qT, cT, ts, sink, ch, offs, out):
         part_sum = [own([P, 2], F32, f"part_sum{b}") for b in range(B)]
         row_sum = own([P, B], F32, "row_sum")
         inv_sum = own([P, B], F32, "inv_sum")
-        gathered = own([P, 4 * B * N + N], BF16, "gathered")
+        gathered = own([P, FIRST_KEYS_COL + 4 * HALF], BF16, "gathered")
         early_values1 = own([P, 2 * N], BF16, "early_values1")
         value_codes = [placed([P, D], U32, f"value_codes{b}", VALUE_CODES_AT + b * 4 * D) for b in range(B)]
         value_scales = [own([P, D], U8, f"value_scales{b}") for b in range(B)]
         late_values = [placed([P, 2 * N], BF16, f"late_values{b}", LATE_VALUES_AT + 4 * N * b) for b in range(B)]
-        staged_values = {(0, 0): gathered[:, 3 * B * N:4 * B * N], (0, 1): early_values1[:],
+        staged_values = {(0, 0): gathered[:, FIRST_KEYS_COL - 2 * N:FIRST_KEYS_COL], (0, 1): early_values1[:],
                          (1, 0): late_values[0][:], (1, 1): late_values[1][:]}
         ts_row = own([P, B * N], F32, "ts_row")
-        ts_cols = [own([P, 4], F32, "ts_cols0"), placed([P, 4], F32, "ts_cols1", FIRST_RESULT_AT)]
-        ts_source = [placed([P, 4], F32, f"ts_source{b}", FIRST_KEYS_AT + 64 * b) for b in range(B)]
+        ts_cols = [gathered[:, FIRST_KEYS_COL + N + 32 * b:FIRST_KEYS_COL + N + 32 * b + 8].bitcast(F32) for b in range(B)]
         ts_spread = [own([P, N], F32, f"ts_spread{b}") for b in range(B)]
         query_codes = [own([P, NQ], U32, f"query_codes{b}") for b in range(B)]
         query_scales = [own([P, NQ], U8, f"query_scales{b}") for b in range(B)]
-        first_keys = placed([P, 4 * N], BF16, "first_keys", FIRST_KEYS_AT)
-        key_halves = {(0, 0): first_keys[:, 0:4 * HALF], (0, HALF): first_keys[:, 4 * HALF:],
+        key_halves = {(0, 0): gathered[:, FIRST_KEYS_COL:], (0, HALF): placed([P, 4 * HALF], BF16, "second_keys", KEYS_AT)[:],
                       (1, 0): scaled[:, 0:N].bitcast(BF16), (1, HALF): own([P, 4 * HALF], BF16, "last_keys")[:]}
+        staged_query = [own([P, 4 * NQ], BF16, "staged_query0"), placed([P, 4 * NQ], BF16, "staged_query1", KEYS_AT)]
         key_codes = [own([P, N], U32, f"key_codes{b}") for b in range(B)]
         key_scales = [own([P, N], U8, f"key_scales{b}") for b in range(B)]
         p = [own([P, N + 1], F32, f"p{b}") for b in range(B)]
-        w = [own([P, NQ, 4], BF16, f"w{b}") for b in range(B)]
+        w = [own([P, N], BF16, f"w{b}") for b in range(B)]
+        w_turned = [own([P, 4 * NQ], BF16, "w_turned0"), placed([P, 4 * NQ], BF16, "w_turned1", RESULT_AT)]
         w_codes = [own([P, NQ], U32, f"w_codes{b}") for b in range(B)]
         w_scales = [own([P, NQ], U8, f"w_scales{b}") for b in range(B)]
-        result = [placed([P, D], F32, "result0", FIRST_RESULT_AT), own([P, D], F32, "result1")]
+        result = [placed([P, D], F32, "result0", RESULT_AT), own([P, D], F32, "result1")]
         banks = {}
 
         def plane_cols(t):
-            return gathered[:, t * B * N:(t + 1) * B * N]
-
-        def staged_query(b):
-            first = 4 * B * N - HALF + b * HALF
-            return gathered[:, first:first + 4 * NQ]
+            return gathered[:, PLANE_AT[t]:PLANE_AT[t] + B * N]
 
         def load_queries_and_sinks():
             for b in range(B):
@@ -119,19 +117,19 @@ def tile_attend_x_mla_sink_kernel(tc, qT, cT, ts, sink, ch, offs, out):
         def gather_ts():
             nc.vector.tensor_copy(ts_row[:], ts_window[:].indirect(offsets[:]))
             for b in range(B):
-                banks["ts", b] = turn_bank("ts_turned")
-                for s in range(4):
-                    nc.tensor.transpose(banks["ts", b][:, s * P:(s + 1) * P], ts_row[:, b * N + s:(b + 1) * N:4], ident[:])
+                banks["ts", b] = bank(f"ts_turned{b}", b)
+                for j in range(4):
+                    nc.tensor.transpose(banks["ts", b][:, j * P:(j + 1) * P], ts_row[:, b * N + j * P:b * N + (j + 1) * P], ident[:])
 
         def spread_ts():
             for b in range(B):
-                nc.scalar.copy(out=ts_source[b][:], in_=banks["ts", b][:, P - 1:512:P])
-                nc.scalar.copy(out=ts_cols[b][:], in_=banks["ts", b][:, P - 1:512:P])
+                nc.scalar.copy(out=ts_cols[b], in_=banks["ts", b][:, P - 1:512:P])
             for b in range(B):
-                rows = turn_bank("ts_rows")
-                for s in range(4):
-                    nc.tensor.transpose(rows[:, s * P:(s + 1) * P], ts_source[b][:, s:s + 1].to_broadcast([P, P]), ident[:])
-                nc.scalar.copy(out=ts_spread[b][:], in_=rows[:])
+                rows = bank(f"ts_rows{b}", (3, 0)[b])
+                for j in range(4):
+                    nc.tensor.transpose(rows[:, j * P:(j + 1) * P], ts_cols[b][:, j:j + 1].to_broadcast([P, P]), ident[:])
+                nc.scalar.copy(out=ts_spread[b][:].rearrange("q (u m e) -> q u m e", u=2, e=2),
+                               in_=rows[:].rearrange("q (m u e) -> q u m e", u=2, e=2))
 
         def gather_on_vector(t, lo, hi):
             nc.vector.tensor_copy(plane_cols(t)[:, lo:hi], planes[t][:].indirect(offsets[:, lo // 16:hi // 16]))
@@ -139,9 +137,9 @@ def tile_attend_x_mla_sink_kernel(tc, qT, cT, ts, sink, ch, offs, out):
         def gather_on_scalar(t, lo, hi):
             nc.scalar.activation(plane_cols(t)[:, lo:hi], planes[t][:].indirect(offsets[:, lo // 16:hi // 16]), COPY)
 
-        def turn_values(t, seqs):
+        def turn_values(t, seqs, index):
             words = plane_cols(t).bitcast(F32)
-            rows = turn_bank("values_turned")
+            rows = bank(f"values_turned{t}_{seqs[0]}", index)
             for b in seqs:
                 banks["values", t, b] = rows
                 for u in range(2):
@@ -149,28 +147,29 @@ def tile_attend_x_mla_sink_kernel(tc, qT, cT, ts, sink, ch, offs, out):
                     nc.tensor.transpose(rows[:, k * P:(k + 1) * P], words[:, b * HALF + u:(b + 1) * HALF:2], ident[:])
 
         def copy_values(t, b):
-            src = banks["values", t, b][:, b * HALF:(b + 1) * HALF].rearrange("m (u h r) -> m h r u", u=2, h=2)
-            dst = staged_values[t // 2, b].bitcast(F32).rearrange("m (h t r u) -> m h t r u", h=2, t=2, u=2)
+            src = banks["values", t, b][:, b * HALF:(b + 1) * HALF].rearrange("m (u g r) -> m g r u", u=2, g=PARTS[b])
+            dst = staged_values[t // 2, b].bitcast(F32).rearrange("m (g t r u) -> m g t r u", g=PARTS[b], t=2, u=2)
             nc.scalar.copy(out=dst[:, :, t % 2], in_=src)
 
-        def quantise_values(b, pair, halves=range(2)):
-            for h in halves:
-                cols = slice(h * HALF + pair * P, h * HALF + (pair + 1) * P)
+        def quantise_values(b, pair, parts):
+            width = D // PARTS[b]
+            for g in parts:
+                cols = slice(g * width + pair * width // 2, g * width + (pair + 1) * width // 2)
                 nc.vector.quantize_mx(out=value_codes[b][:, cols].bitcast(FP8X4), scales=value_scales[b][:, cols],
-                                      in_=staged_values[pair, b][:, h * N:(h + 1) * N])
+                                      in_=staged_values[pair, b][:, g * 2 * width:(g + 1) * 2 * width])
 
         def copy_query(b, copy):
-            dst = staged_query(b).rearrange("r (q t) -> r q t", t=4)
+            dst = staged_query[b][:].rearrange("r (q t) -> r q t", t=4)
             copy(out=dst.rearrange("r (c i) t -> r c t i", i=4), in_=raw_query[b][:].rearrange("r t (c i) -> r c t i", i=4))
 
         def quantise_query(b):
-            nc.vector.quantize_mx(out=query_codes[b][:].bitcast(FP8X4), scales=query_scales[b][:], in_=staged_query(b))
+            nc.vector.quantize_mx(out=query_codes[b][:].bitcast(FP8X4), scales=query_scales[b][:], in_=staged_query[b][:])
 
         def copy_keys(b, lo, hi, pair, copy):
-            first = 0 if b == 0 else lo // HALF * HALF
-            dst = first_keys[:] if b == 0 else key_halves[b, first]
-            two_planes = gathered[:, 2 * pair * B * N:(2 * pair + 2) * B * N].rearrange("r (t s) -> r s t", t=2)
-            copy(out=dst.rearrange("r (s t) -> r s t", t=4)[:, lo - first:hi - first, 2 * pair:2 * pair + 2],
+            first = lo // HALF * HALF
+            start, step = PLANE_AT[2 * pair], PLANE_AT[2 * pair + 1] - PLANE_AT[2 * pair]
+            two_planes = gathered[:, start:start + 2 * step].rearrange("r (t s) -> r s t", t=2)
+            copy(out=key_halves[b, first].rearrange("r (s t) -> r s t", t=4)[:, lo - first:hi - first, 2 * pair:2 * pair + 2],
                  in_=two_planes[:, b * N + lo:b * N + hi])
 
         def quantise_keys(b, lo):
@@ -184,9 +183,11 @@ def tile_attend_x_mla_sink_kernel(tc, qT, cT, ts, sink, ch, offs, out):
                                 start=True, stop=True)
 
         def scale_scores(b, lo, hi):
-            nc.vector.tensor_tensor(out=scaled[:, b * ROW:b * ROW + N].rearrange("q (s m) -> q s m", s=4)[:, :, lo // 4:hi // 4],
-                                    in0=banks["scores", b, lo][:, lo:hi].rearrange("q (m s) -> q s m", s=4),
-                                    in1=ts_spread[b][:].rearrange("q (s m) -> q s m", s=4)[:, :, lo // 4:hi // 4], op=MULT)
+            def dealt(row):
+                return row.rearrange("q (u m e) -> q u m e", u=2, e=2)[:, :, lo // 4:hi // 4]
+            nc.vector.tensor_tensor(out=dealt(scaled[:, b * ROW:b * ROW + N]),
+                                    in0=banks["scores", b, lo][:, lo:hi].rearrange("q (m u e) -> q u m e", u=2, e=2),
+                                    in1=dealt(ts_spread[b][:]), op=MULT)
 
         def row_max(b):
             nc.vector.tensor_reduce(out=neg_max[b][:], in_=scaled[:, b * ROW:b * ROW + N + 1], axis=AX, op=MAX, negate=True)
@@ -195,40 +196,47 @@ def tile_attend_x_mla_sink_kernel(tc, qT, cT, ts, sink, ch, offs, out):
             for i, (lo, hi) in enumerate(((0, HALF), (HALF, N + 1))):
                 nc.scalar.activation(out=p[b][:, lo:hi], in_=scaled[:, b * ROW + lo:b * ROW + hi], func=EXP,
                                      bias=neg_max[b][:], scale=1.0, accum_out=part_sum[b][:, i:i + 1])
+
+        def add_sums(b):
             nc.scalar.activation(out=row_sum[:, b:b + 1], in_=part_sum[b][:, 0:1], func=IDENTITY,
                                  bias=part_sum[b][:, 1:2], scale=1.0)
 
-        def turn_p(b):
-            banks["p", b] = turn_bank("p_turned")
-            for s in range(4):
-                nc.tensor.transpose(banks["p", b][:, s * P:(s + 1) * P], p[b][:, s * P:(s + 1) * P], ident[:])
+        def weigh(b, u):
+            cols = slice(u * HALF, (u + 1) * HALF)
+            nc.vector.tensor_tensor(out=w[b][:, cols], in0=p[b][:, cols], in1=ts_spread[b][:, cols], op=MULT)
 
-        def weigh(b):
-            nc.vector.tensor_tensor(out=w[b][:], in0=banks["p", b][:].rearrange("m (s q) -> m q s", s=4),
-                                    in1=ts_cols[b][:].unsqueeze(1).to_broadcast([P, NQ, 4]), op=MULT)
+        def turn_w(b, index):
+            rows = bank(f"w_rows{b}", index)
+            for u in range(2):
+                nc.tensor.transpose(rows[:, u * P:(u + 1) * P], w[b][:].bitcast(F32)[:, u * P:(u + 1) * P], ident[:])
+            nc.scalar.copy(out=w_turned[b][:].bitcast(F32).rearrange("m (q u) -> m q u", u=2),
+                           in_=rows[:, 0:2 * P].rearrange("m (u q) -> m q u", u=2))
 
         def quantise_w(b):
-            nc.vector.quantize_mx(out=w_codes[b][:].bitcast(FP8X4), scales=w_scales[b][:], in_=w[b][:].rearrange("m q s -> m (q s)"))
+            nc.vector.quantize_mx(out=w_codes[b][:].bitcast(FP8X4), scales=w_scales[b][:], in_=w_turned[b][:])
 
-        def multiply_values(b):
-            for h in range(2):
-                cols = slice(h * HALF, (h + 1) * HALF)
-                banks["y", b, h] = product_bank("y", h)
-                nc.tensor.matmul_mx(banks["y", b, h][:, 0:HALF], lhsT=w_codes[b][:].bitcast(FP8X4), lhsT_scale=w_scales[b][:],
+        def multiply_values(b, indices):
+            width = D // PARTS[b]
+            for g, index in enumerate(indices):
+                cols = slice(g * width, (g + 1) * width)
+                banks["y", b, g] = bank(f"y{b}_{g}", index)
+                nc.tensor.matmul_mx(banks["y", b, g][:, 0:width], lhsT=w_codes[b][:].bitcast(FP8X4), lhsT_scale=w_scales[b][:],
                                     rhs=value_codes[b][:, cols].bitcast(FP8X4), rhs_scale=value_scales[b][:, cols],
                                     start=True, stop=True)
 
-        def epilogue(b, h, queue):
-            cols = slice(h * HALF, (h + 1) * HALF)
-            nc.vector.scalar_tensor_tensor(
-                out=result[b][:, cols].rearrange("q (r t) -> q r t", t=4),
-                in0=banks["y", b, h][:, 0:HALF].rearrange("q (t r) -> q r t", t=4),
-                scalar=inv_sum[:, b:b + 1], in1=channels[:, cols].rearrange("q (r t) -> q r t", t=4), op0=MULT, op1=MULT)
-            queue.dma_start(out=out[b][:, cols], in_=result[b][:, cols])
+        def epilogue(b):
+            width = D // PARTS[b]
+            for g in range(PARTS[b]):
+                cols = slice(g * width, (g + 1) * width)
+                nc.vector.scalar_tensor_tensor(
+                    out=result[b][:, cols].rearrange("q (r t) -> q r t", t=4),
+                    in0=banks["y", b, g][:, 0:width].rearrange("q (t r) -> q r t", t=4),
+                    scalar=inv_sum[:, b:b + 1], in1=channels[:, cols].rearrange("q (r t) -> q r t", t=4), op0=MULT, op1=MULT)
+                (nc.scalar, nc.sync)[g % 2].dma_start(out=out[b][:, cols], in_=result[b][:, cols])
 
         gather_ts()
         gather_on_vector(0, 0, B * N)
-        turn_values(0, (0, 1))
+        turn_values(0, (0, 1), 2)
         copy_values(0, 0)
         copy_values(0, 1)
         spread_ts()
@@ -239,14 +247,14 @@ def tile_attend_x_mla_sink_kernel(tc, qT, cT, ts, sink, ch, offs, out):
         copy_keys(1, 0, HALF, 0, on_vector)
         copy_keys(1, HALF, N, 0, on_vector)
         for b in (1, 0):
-            turn_values(1, (b,))
+            turn_values(1, (b,), (2, 1)[b])
             copy_values(1, b)
         copy_keys(0, 0, HALF, 0, on_scalar)
         copy_keys(0, HALF, N, 0, on_scalar)
         gather_on_vector(2, 0, B * N)
-        turn_values(2, (0, 1))
-        quantise_values(1, 0)
-        quantise_values(0, 0)
+        turn_values(2, (0, 1), 7)
+        quantise_values(1, 0, range(4))
+        quantise_values(0, 0, range(2))
 
         gather_on_vector(3, 0, HALF)
         gather_on_scalar(3, N, N + HALF)
@@ -256,47 +264,49 @@ def tile_attend_x_mla_sink_kernel(tc, qT, cT, ts, sink, ch, offs, out):
         copy_keys(0, HALF, N, 1, on_vector)
         copy_query(0, on_scalar)
         copy_keys(1, 0, HALF, 1, on_scalar)
-        turn_values(3, (0,))
+        turn_values(3, (0,), 2)
         quantise_keys(0, 0)
         quantise_keys(0, HALF)
         quantise_query(0)
-        first_scores = product_bank("scores", 0)
+        first_scores = bank("scores0", 0)
         score(0, 0, first_scores)
         score(0, HALF, first_scores)
 
         gather_on_vector(3, N + HALF, B * N)
         nc.sync.dma_start(out=channels[:], in_=ch)
         copy_keys(1, HALF, N, 1, on_scalar)
-        turn_values(3, (1,))
+        turn_values(3, (1,), 5)
         copy_query(1, on_vector)
         quantise_keys(1, 0)
         quantise_query(1)
-        score(1, 0, product_bank("scores", 1))
+        score(1, 0, bank("scores1a", 1))
         for b in range(B):
             copy_values(2, b)
             copy_values(3, b)
 
         scale_scores(0, 0, N)
         quantise_keys(1, HALF)
-        score(1, HALF, product_bank("scores", 0))
+        score(1, HALF, bank("scores1b", 3))
         row_max(0)
         exponentials(0)
+        add_sums(0)
         scale_scores(1, 0, HALF)
         scale_scores(1, HALF, N)
         row_max(1)
-        quantise_values(0, 1)
         exponentials(1)
-        turn_p(0)
-        turn_p(1)
-        quantise_values(1, 1, [0])
-        weigh(0)
-        quantise_values(1, 1, [1])
+        weigh(0, 0)
+        weigh(0, 1)
+        turn_w(0, 4)
+        weigh(1, 0)
+        weigh(1, 1)
+        turn_w(1, 6)
+        add_sums(1)
+        quantise_values(0, 1, range(2))
         quantise_w(0)
-        multiply_values(0)
+        multiply_values(0, (0, 1))
+        quantise_values(1, 1, range(4))
         nc.vector.reciprocal(out=inv_sum[:], in_=row_sum[:])
-        weigh(1)
         quantise_w(1)
-        multiply_values(1)
+        multiply_values(1, (3, 2, 5, 7))
         for b in range(B):
-            epilogue(b, 0, nc.scalar)
-            epilogue(b, 1, nc.sync)
+            epilogue(b)

@@ -99,8 +99,8 @@ def tile_attend_x_mla_sink_kernel(tc, qT, cT, ts, sink, ch, offs, out):
         key_codes = [own([P, N], U32, f"key_codes{b}") for b in range(B)]
         key_scales = [own([P, N], U8, f"key_scales{b}") for b in range(B)]
         p = [own([P, N + 1], F32, f"p{b}") for b in range(B)]
-        w = [own([P, N], BF16, f"w{b}") for b in range(B)]
-        w_turned = [own([P, 4 * NQ], BF16, "w_turned0"), placed([P, 4 * NQ], BF16, "w_turned1", RESULT_AT)]
+        ts_by_slot = [own([P, 4], F32, "ts_by_slot0"), placed([P, 4], F32, "ts_by_slot1", RESULT_AT)]
+        w_turned = [own([P, 4 * NQ], BF16, "w_turned0"), own([P, 4 * NQ], BF16, "w_turned1")]
         w_codes = [own([P, NQ], U32, f"w_codes{b}") for b in range(B)]
         w_scales = [own([P, NQ], U8, f"w_scales{b}") for b in range(B)]
         result = [placed([P, D], F32, "result0", RESULT_AT), own([P, D], F32, "result1")]
@@ -119,17 +119,17 @@ def tile_attend_x_mla_sink_kernel(tc, qT, cT, ts, sink, ch, offs, out):
             for b in range(B):
                 banks["ts", b] = bank(f"ts_turned{b}", b)
                 for j in range(4):
-                    nc.tensor.transpose(banks["ts", b][:, j * P:(j + 1) * P], ts_row[:, b * N + j * P:b * N + (j + 1) * P], ident[:])
+                    nc.tensor.transpose(banks["ts", b][:, j * P:(j + 1) * P], ts_row[:, b * N + j:(b + 1) * N:4], ident[:])
 
         def spread_ts():
             for b in range(B):
                 nc.scalar.copy(out=ts_cols[b], in_=banks["ts", b][:, P - 1:512:P])
+                nc.scalar.copy(out=ts_by_slot[b][:], in_=banks["ts", b][:, P - 1:512:P])
             for b in range(B):
                 rows = bank(f"ts_rows{b}", (3, 0)[b])
                 for j in range(4):
                     nc.tensor.transpose(rows[:, j * P:(j + 1) * P], ts_cols[b][:, j:j + 1].to_broadcast([P, P]), ident[:])
-                nc.scalar.copy(out=ts_spread[b][:].rearrange("q (u m e) -> q u m e", u=2, e=2),
-                               in_=rows[:].rearrange("q (m u e) -> q u m e", u=2, e=2))
+                nc.scalar.copy(out=ts_spread[b][:], in_=rows[:])
 
         def gather_on_vector(t, lo, hi):
             nc.vector.tensor_copy(plane_cols(t)[:, lo:hi], planes[t][:].indirect(offsets[:, lo // 16:hi // 16]))
@@ -184,9 +184,9 @@ def tile_attend_x_mla_sink_kernel(tc, qT, cT, ts, sink, ch, offs, out):
 
         def scale_scores(b, lo, hi):
             def dealt(row):
-                return row.rearrange("q (u m e) -> q u m e", u=2, e=2)[:, :, lo // 4:hi // 4]
+                return row.rearrange("q (s m) -> q s m", s=4)[:, :, lo // 4:hi // 4]
             nc.vector.tensor_tensor(out=dealt(scaled[:, b * ROW:b * ROW + N]),
-                                    in0=banks["scores", b, lo][:, lo:hi].rearrange("q (m u e) -> q u m e", u=2, e=2),
+                                    in0=banks["scores", b, lo][:, lo:hi].rearrange("q (m s) -> q s m", s=4),
                                     in1=dealt(ts_spread[b][:]), op=MULT)
 
         def row_max(b):
@@ -201,16 +201,15 @@ def tile_attend_x_mla_sink_kernel(tc, qT, cT, ts, sink, ch, offs, out):
             nc.scalar.activation(out=row_sum[:, b:b + 1], in_=part_sum[b][:, 0:1], func=IDENTITY,
                                  bias=part_sum[b][:, 1:2], scale=1.0)
 
-        def weigh(b, u):
-            cols = slice(u * HALF, (u + 1) * HALF)
-            nc.vector.tensor_tensor(out=w[b][:, cols], in0=p[b][:, cols], in1=ts_spread[b][:, cols], op=MULT)
+        def turn_p(b, index):
+            banks["p", b] = bank(f"p_turned{b}", index)
+            for s in range(4):
+                nc.tensor.transpose(banks["p", b][:, s * P:(s + 1) * P], p[b][:, s * P:(s + 1) * P], ident[:])
 
-        def turn_w(b, index):
-            rows = bank(f"w_rows{b}", index)
-            for u in range(2):
-                nc.tensor.transpose(rows[:, u * P:(u + 1) * P], w[b][:].bitcast(F32)[:, u * P:(u + 1) * P], ident[:])
-            nc.scalar.copy(out=w_turned[b][:].bitcast(F32).rearrange("m (q u) -> m q u", u=2),
-                           in_=rows[:, 0:2 * P].rearrange("m (u q) -> m q u", u=2))
+        def weigh(b):
+            nc.vector.tensor_tensor(out=w_turned[b][:].rearrange("m (q s) -> m q s", s=4),
+                                    in0=banks["p", b][:].rearrange("m (s q) -> m q s", s=4),
+                                    in1=ts_by_slot[b][:].unsqueeze(1).to_broadcast([P, NQ, 4]), op=MULT)
 
         def quantise_w(b):
             nc.vector.quantize_mx(out=w_codes[b][:].bitcast(FP8X4), scales=w_scales[b][:], in_=w_turned[b][:])
@@ -293,19 +292,18 @@ def tile_attend_x_mla_sink_kernel(tc, qT, cT, ts, sink, ch, offs, out):
         scale_scores(1, 0, HALF)
         scale_scores(1, HALF, N)
         row_max(1)
-        exponentials(1)
-        weigh(0, 0)
-        weigh(0, 1)
-        turn_w(0, 4)
-        weigh(1, 0)
-        weigh(1, 1)
-        turn_w(1, 6)
-        add_sums(1)
         quantise_values(0, 1, range(2))
+        exponentials(1)
+        add_sums(1)
+        turn_p(0, 4)
+        turn_p(1, 6)
+        quantise_values(1, 1, range(2))
+        weigh(0)
+        quantise_values(1, 1, range(2, 4))
         quantise_w(0)
         multiply_values(0, (0, 1))
-        quantise_values(1, 1, range(4))
         nc.vector.reciprocal(out=inv_sum[:], in_=row_sum[:])
+        weigh(1)
         quantise_w(1)
         multiply_values(1, (3, 2, 5, 7))
         for b in range(B):

@@ -8,7 +8,7 @@ P = 128
 HALF = N // 2
 QUARTER = N // 4
 ROW = N + 8
-PARTS = (2, 4)
+PARTS = (2, 2)
 FLOPS = 4 * B * N * D * NQ
 
 PLANE = 4 * T + 256
@@ -18,6 +18,7 @@ VALUE_CODES_AT = 2 * PLANE + 65 * 64
 CHANNELS_AT = 3 * PLANE + 4 * D
 KEYS_AT = 4 * PLANE
 RESULT_AT = KEYS_AT + 8 * HALF
+LATE_CODES_AT = RESULT_AT + 4 * D
 BANK = 2048
 
 PLANE_AT = (0, B * N, 2 * B * N, 3 * B * N + HALF)
@@ -83,7 +84,7 @@ def tile_attend_x_mla_sink_kernel(tc, qT, cT, ts, sink, ch, offs, out):
         inv_sum = own([P, B], F32, "inv_sum")
         gathered = own([P, FIRST_KEYS_COL + 4 * HALF], BF16, "gathered")
         early_values1 = own([P, 2 * N], BF16, "early_values1")
-        value_codes = [placed([P, D], U32, f"value_codes{b}", VALUE_CODES_AT + b * 4 * D) for b in range(B)]
+        value_codes = [placed([P, D], U32, f"value_codes{b}", (VALUE_CODES_AT, LATE_CODES_AT)[b]) for b in range(B)]
         value_scales = [own([P, D], U8, f"value_scales{b}") for b in range(B)]
         late_values = [placed([P, 2 * N], BF16, f"late_values{b}", LATE_VALUES_AT + 4 * N * b) for b in range(B)]
         staged_values = {(0, 0): gathered[:, FIRST_KEYS_COL - 2 * N:FIRST_KEYS_COL], (0, 1): early_values1[:],
@@ -96,7 +97,7 @@ def tile_attend_x_mla_sink_kernel(tc, qT, cT, ts, sink, ch, offs, out):
         key_halves = {(0, 0): gathered[:, FIRST_KEYS_COL:], (0, HALF): placed([P, 4 * HALF], BF16, "second_keys", KEYS_AT)[:],
                       (1, 0): scaled[:, 0:N].bitcast(BF16), (1, HALF): own([P, 4 * HALF], BF16, "last_keys")[:]}
         staged_query = [own([P, 4 * NQ], BF16, "staged_query0"), placed([P, 4 * NQ], BF16, "staged_query1", KEYS_AT)]
-        key_codes = [own([P, N], U32, f"key_codes{b}") for b in range(B)]
+        key_codes = [own([P, N], U32, "key_codes0"), placed([P, N], U32, "key_codes1", LATE_CODES_AT)]
         key_scales = [own([P, N], U8, f"key_scales{b}") for b in range(B)]
         p = [own([P, N + 1], F32, f"p{b}") for b in range(B)]
         ts_by_slot = [own([P, 4], F32, "ts_by_slot0"), placed([P, 4], F32, "ts_by_slot1", RESULT_AT)]
@@ -245,14 +246,13 @@ def tile_attend_x_mla_sink_kernel(tc, qT, cT, ts, sink, ch, offs, out):
         load_queries_and_sinks()
         copy_keys(1, 0, HALF, 0, on_vector)
         copy_keys(1, HALF, N, 0, on_vector)
-        for b in (1, 0):
+        for b in (0, 1):
             turn_values(1, (b,), (2, 1)[b])
             copy_values(1, b)
         copy_keys(0, 0, HALF, 0, on_scalar)
         copy_keys(0, HALF, N, 0, on_scalar)
         gather_on_vector(2, 0, B * N)
         turn_values(2, (0, 1), 7)
-        quantise_values(1, 0, range(4))
         quantise_values(0, 0, range(2))
 
         gather_on_vector(3, 0, HALF)
@@ -297,14 +297,15 @@ def tile_attend_x_mla_sink_kernel(tc, qT, cT, ts, sink, ch, offs, out):
         add_sums(1)
         turn_p(0, 4)
         turn_p(1, 6)
-        quantise_values(1, 1, range(2))
+        quantise_values(1, 0, range(2))
+        quantise_values(1, 1, [0])
         weigh(0)
-        quantise_values(1, 1, range(2, 4))
+        quantise_values(1, 1, [1])
         quantise_w(0)
         multiply_values(0, (0, 1))
         nc.vector.reciprocal(out=inv_sum[:], in_=row_sum[:])
         weigh(1)
         quantise_w(1)
-        multiply_values(1, (3, 2, 5, 7))
+        multiply_values(1, (3, 2))
         for b in range(B):
             epilogue(b)

@@ -8,7 +8,7 @@ P = 128
 HALF = N // 2
 QUARTER = N // 4
 ROW = N + 8
-PARTS = (2, 2)
+PARTS = (1, 2)
 FLOPS = 4 * B * N * D * NQ
 
 PLANE = 4 * T + 256
@@ -19,6 +19,7 @@ CHANNELS_AT = 3 * PLANE + 4 * D
 KEYS_AT = 4 * PLANE
 RESULT_AT = KEYS_AT + 8 * HALF
 LATE_CODES_AT = RESULT_AT + 4 * D
+LAST_P_AT = LATE_CODES_AT + 4 * D
 BANK = 2048
 
 PLANE_AT = (0, B * N, 2 * B * N, 3 * B * N + HALF)
@@ -79,16 +80,15 @@ def tile_attend_x_mla_sink_kernel(tc, qT, cT, ts, sink, ch, offs, out):
         scaled = placed([P, B * ROW], F32, "scaled", PLANE)
         channels = placed([P, D], F32, "channels", CHANNELS_AT)
         neg_max = [own([P, 1], F32, f"neg_max{b}") for b in range(B)]
-        part_sum = [own([P, 2], F32, f"part_sum{b}") for b in range(B)]
+        part_sum = own([P, 2], F32, "part_sum")
         row_sum = own([P, B], F32, "row_sum")
-        inv_sum = own([P, B], F32, "inv_sum")
+        inv_sum = placed([P, B], F32, "inv_sum", LAST_P_AT)
         gathered = own([P, FIRST_KEYS_COL + 4 * HALF], BF16, "gathered")
-        early_values1 = own([P, 2 * N], BF16, "early_values1")
+        second_values = own([P, 4 * N], BF16, "second_values")
         value_codes = [placed([P, D], U32, f"value_codes{b}", (VALUE_CODES_AT, LATE_CODES_AT)[b]) for b in range(B)]
         value_scales = [own([P, D], U8, f"value_scales{b}") for b in range(B)]
-        late_values = [placed([P, 2 * N], BF16, f"late_values{b}", LATE_VALUES_AT + 4 * N * b) for b in range(B)]
-        staged_values = {(0, 0): gathered[:, FIRST_KEYS_COL - 2 * N:FIRST_KEYS_COL], (0, 1): early_values1[:],
-                         (1, 0): late_values[0][:], (1, 1): late_values[1][:]}
+        late_values = placed([P, 2 * N], BF16, "late_values", LATE_VALUES_AT)
+        first_values = [gathered[:, FIRST_KEYS_COL - 2 * N:FIRST_KEYS_COL], late_values[:]]
         ts_row = own([P, B * N], F32, "ts_row")
         ts_cols = [gathered[:, FIRST_KEYS_COL + N + 32 * b:FIRST_KEYS_COL + N + 32 * b + 8].bitcast(F32) for b in range(B)]
         ts_spread = [own([P, N], F32, f"ts_spread{b}") for b in range(B)]
@@ -99,7 +99,7 @@ def tile_attend_x_mla_sink_kernel(tc, qT, cT, ts, sink, ch, offs, out):
         staged_query = [own([P, 4 * NQ], BF16, "staged_query0"), placed([P, 4 * NQ], BF16, "staged_query1", KEYS_AT)]
         key_codes = [own([P, N], U32, "key_codes0"), placed([P, N], U32, "key_codes1", LATE_CODES_AT)]
         key_scales = [own([P, N], U8, f"key_scales{b}") for b in range(B)]
-        p = [own([P, N + 1], F32, f"p{b}") for b in range(B)]
+        p = [own([P, N + 1], F32, "p0"), placed([P, N + 1], F32, "p1", LAST_P_AT)]
         ts_by_slot = [own([P, 4], F32, "ts_by_slot0"), placed([P, 4], F32, "ts_by_slot1", RESULT_AT)]
         w_turned = [own([P, 4 * NQ], BF16, "w_turned0"), own([P, 4 * NQ], BF16, "w_turned1")]
         w_codes = [own([P, NQ], U32, f"w_codes{b}") for b in range(B)]
@@ -138,26 +138,25 @@ def tile_attend_x_mla_sink_kernel(tc, qT, cT, ts, sink, ch, offs, out):
         def gather_on_scalar(t, lo, hi):
             nc.scalar.activation(plane_cols(t)[:, lo:hi], planes[t][:].indirect(offsets[:, lo // 16:hi // 16]), COPY)
 
-        def turn_values(t, seqs, index):
+        def turn_values(t, b, rows, place):
             words = plane_cols(t).bitcast(F32)
-            rows = bank(f"values_turned{t}_{seqs[0]}", index)
-            for b in seqs:
-                banks["values", t, b] = rows
-                for u in range(2):
-                    k = 2 * b + u
-                    nc.tensor.transpose(rows[:, k * P:(k + 1) * P], words[:, b * HALF + u:(b + 1) * HALF:2], ident[:])
+            for u in range(2):
+                k = 2 * place + u
+                nc.tensor.transpose(rows[:, k * P:(k + 1) * P], words[:, b * HALF + u:(b + 1) * HALF:2], ident[:])
 
-        def copy_values(t, b):
-            src = banks["values", t, b][:, b * HALF:(b + 1) * HALF].rearrange("m (u g r) -> m g r u", u=2, g=PARTS[b])
-            dst = staged_values[t // 2, b].bitcast(F32).rearrange("m (g t r u) -> m g t r u", g=PARTS[b], t=2, u=2)
-            nc.scalar.copy(out=dst[:, :, t % 2], in_=src)
+        def copy_values(b, t, count, rows, place):
+            src = rows[:, place * HALF:(place + count) * HALF]
+            if b == 0:
+                dst = first_values[t // 2].bitcast(F32)[:, t % 2 * HALF:(t % 2 + count) * HALF]
+                nc.scalar.copy(out=dst.rearrange("m (t r u) -> m t r u", t=count, u=2), in_=src.rearrange("m (t u r) -> m t r u", t=count, u=2))
+            else:
+                dst = second_values[:].bitcast(F32).rearrange("m (h t r u) -> m t h r u", h=2, t=4, u=2)[:, t:t + count]
+                nc.scalar.copy(out=dst, in_=src.rearrange("m (t u h r) -> m t h r u", t=count, u=2, h=2))
 
-        def quantise_values(b, pair, parts):
-            width = D // PARTS[b]
-            for g in parts:
-                cols = slice(g * width + pair * width // 2, g * width + (pair + 1) * width // 2)
-                nc.vector.quantize_mx(out=value_codes[b][:, cols].bitcast(FP8X4), scales=value_scales[b][:, cols],
-                                      in_=staged_values[pair, b][:, g * 2 * width:(g + 1) * 2 * width])
+        def quantise_values(b, half):
+            cols = slice(half * HALF, (half + 1) * HALF)
+            staged = first_values[half] if b == 0 else second_values[:, half * 2 * N:(half + 1) * 2 * N]
+            nc.vector.quantize_mx(out=value_codes[b][:, cols].bitcast(FP8X4), scales=value_scales[b][:, cols], in_=staged)
 
         def copy_query(b, copy):
             dst = staged_query[b][:].rearrange("r (q t) -> r q t", t=4)
@@ -196,11 +195,13 @@ def tile_attend_x_mla_sink_kernel(tc, qT, cT, ts, sink, ch, offs, out):
         def exponentials(b):
             for i, (lo, hi) in enumerate(((0, HALF), (HALF, N + 1))):
                 nc.scalar.activation(out=p[b][:, lo:hi], in_=scaled[:, b * ROW + lo:b * ROW + hi], func=EXP,
-                                     bias=neg_max[b][:], scale=1.0, accum_out=part_sum[b][:, i:i + 1])
+                                     bias=neg_max[b][:], scale=1.0, accum_out=part_sum[:, i:i + 1] if b == 0 else None)
 
         def add_sums(b):
-            nc.scalar.activation(out=row_sum[:, b:b + 1], in_=part_sum[b][:, 0:1], func=IDENTITY,
-                                 bias=part_sum[b][:, 1:2], scale=1.0)
+            if b == 0:
+                nc.scalar.activation(out=row_sum[:, 0:1], in_=part_sum[:, 0:1], func=IDENTITY, bias=part_sum[:, 1:2], scale=1.0)
+            else:
+                nc.scalar.activation(out=scaled[:, ROW:ROW + N + 1], in_=p[1][:], func=IDENTITY, accum_out=row_sum[:, 1:2])
 
         def turn_p(b, index):
             banks["p", b] = bank(f"p_turned{b}", index)
@@ -225,20 +226,24 @@ def tile_attend_x_mla_sink_kernel(tc, qT, cT, ts, sink, ch, offs, out):
                                     start=True, stop=True)
 
         def epilogue(b):
-            width = D // PARTS[b]
-            for g in range(PARTS[b]):
-                cols = slice(g * width, (g + 1) * width)
+            for h in range(2):
+                cols = slice(h * HALF, (h + 1) * HALF)
+                if PARTS[b] == 1:
+                    sums = banks["y", b, 0][:].rearrange("q (t r) -> q r t", t=4)[:, h * HALF // 4:(h + 1) * HALF // 4]
+                else:
+                    sums = banks["y", b, h][:, 0:HALF].rearrange("q (t r) -> q r t", t=4)
                 nc.vector.scalar_tensor_tensor(
-                    out=result[b][:, cols].rearrange("q (r t) -> q r t", t=4),
-                    in0=banks["y", b, g][:, 0:width].rearrange("q (t r) -> q r t", t=4),
+                    out=result[b][:, cols].rearrange("q (r t) -> q r t", t=4), in0=sums,
                     scalar=inv_sum[:, b:b + 1], in1=channels[:, cols].rearrange("q (r t) -> q r t", t=4), op0=MULT, op1=MULT)
-                (nc.scalar, nc.sync)[g % 2].dma_start(out=out[b][:, cols], in_=result[b][:, cols])
+                (nc.scalar, nc.sync)[h].dma_start(out=out[b][:, cols], in_=result[b][:, cols])
 
         gather_ts()
         gather_on_vector(0, 0, B * N)
-        turn_values(0, (0, 1), 2)
-        copy_values(0, 0)
-        copy_values(0, 1)
+        rows = bank("plane0_turned", 2)
+        for b in range(B):
+            turn_values(0, b, rows, b)
+        for b in range(B):
+            copy_values(b, 0, 1, rows, b)
         spread_ts()
         gather_on_vector(1, 0, HALF)
         gather_on_vector(1, N, B * N)
@@ -247,13 +252,16 @@ def tile_attend_x_mla_sink_kernel(tc, qT, cT, ts, sink, ch, offs, out):
         copy_keys(1, 0, HALF, 0, on_vector)
         copy_keys(1, HALF, N, 0, on_vector)
         for b in (0, 1):
-            turn_values(1, (b,), (2, 1)[b])
-            copy_values(1, b)
+            rows = bank(f"plane1_turned{b}", (2, 1)[b])
+            turn_values(1, b, rows, 0)
+            copy_values(b, 1, 1, rows, 0)
         copy_keys(0, 0, HALF, 0, on_scalar)
         copy_keys(0, HALF, N, 0, on_scalar)
         gather_on_vector(2, 0, B * N)
-        turn_values(2, (0, 1), 7)
-        quantise_values(0, 0, range(2))
+        late_rows = [bank(f"late_turned{b}", (7, 5)[b]) for b in range(B)]
+        for b in range(B):
+            turn_values(2, b, late_rows[b], 0)
+        quantise_values(0, 0)
 
         gather_on_vector(3, 0, HALF)
         gather_on_scalar(3, N, N + HALF)
@@ -263,7 +271,7 @@ def tile_attend_x_mla_sink_kernel(tc, qT, cT, ts, sink, ch, offs, out):
         copy_keys(0, HALF, N, 1, on_vector)
         copy_query(0, on_scalar)
         copy_keys(1, 0, HALF, 1, on_scalar)
-        turn_values(3, (0,), 2)
+        turn_values(3, 0, late_rows[0], 1)
         quantise_keys(0, 0)
         quantise_keys(0, HALF)
         quantise_query(0)
@@ -274,14 +282,13 @@ def tile_attend_x_mla_sink_kernel(tc, qT, cT, ts, sink, ch, offs, out):
         gather_on_vector(3, N + HALF, B * N)
         nc.sync.dma_start(out=channels[:], in_=ch)
         copy_keys(1, HALF, N, 1, on_scalar)
-        turn_values(3, (1,), 5)
+        turn_values(3, 1, late_rows[1], 1)
         copy_query(1, on_vector)
         quantise_keys(1, 0)
         quantise_query(1)
         score(1, 0, bank("scores1a", 1))
         for b in range(B):
-            copy_values(2, b)
-            copy_values(3, b)
+            copy_values(b, 2, 2, late_rows[b], 0)
 
         scale_scores(0, 0, N)
         quantise_keys(1, HALF)
@@ -292,19 +299,18 @@ def tile_attend_x_mla_sink_kernel(tc, qT, cT, ts, sink, ch, offs, out):
         scale_scores(1, 0, HALF)
         scale_scores(1, HALF, N)
         row_max(1)
-        quantise_values(0, 1, range(2))
+        quantise_values(0, 1)
         exponentials(1)
         add_sums(1)
         turn_p(0, 4)
         turn_p(1, 6)
-        quantise_values(1, 0, range(2))
-        quantise_values(1, 1, [0])
+        quantise_values(1, 0)
         weigh(0)
-        quantise_values(1, 1, [1])
+        quantise_values(1, 1)
         quantise_w(0)
-        multiply_values(0, (0, 1))
-        nc.vector.reciprocal(out=inv_sum[:], in_=row_sum[:])
+        multiply_values(0, (0,))
         weigh(1)
+        nc.vector.reciprocal(out=inv_sum[:], in_=row_sum[:])
         quantise_w(1)
         multiply_values(1, (3, 2))
         for b in range(B):

from contextlib import ExitStack

import concourse.mybir as mybir
from concourse.masks import make_identity

B, N, T, D, NQ = 2, 512, 2048, 512, 128
P = 128
HALF = N // 2
QUARTER = N // 4
ROW = N + 8
PARTS = (1, 2)
FLOPS = 4 * B * N * D * NQ

PLANE = 4 * T + 256
QUERIES_AT = PLANE + 33 * 128
LATE_VALUES_AT = QUERIES_AT + 8 * NQ
VALUE_CODES_AT = 2 * PLANE + 65 * 64
CHANNELS_AT = 3 * PLANE + 4 * D
KEYS_AT = 4 * PLANE
RESULT_AT = KEYS_AT + 8 * HALF
LATE_CODES_AT = RESULT_AT + 4 * D
LAST_P_AT = LATE_CODES_AT + 4 * D
BANK = 2048

PLANE_AT = (0, B * N, 2 * B * N, 3 * B * N + HALF)
FIRST_KEYS_COL = PLANE_AT[3] + N + HALF

F32 = mybir.dt.float32
BF16 = mybir.dt.bfloat16
U32 = mybir.dt.uint32
U16 = mybir.dt.uint16
U8 = mybir.dt.uint8
FP8X4 = mybir.dt.float8_e4m3fn_x4
MULT = mybir.AluOpType.mult
MAX = mybir.AluOpType.max
IDENTITY = mybir.ActivationFunctionType.Identity
COPY = mybir.ActivationFunctionType.Copy
EXP = mybir.ActivationFunctionType.Exp
AX = mybir.AxisListType.X


def tile_attend_x_mla_sink_kernel(tc, qT, cT, ts, sink, ch, offs, out):
    nc = tc.nc
    on_scalar, on_vector = nc.scalar.copy, nc.vector.tensor_copy
    with ExitStack() as ctx:
        lists = ctx.enter_context(tc.tile_pool(name="lists", bufs=1))
        keep = ctx.enter_context(tc.tile_pool(name="keep", bufs=1))
        shared = ctx.enter_context(tc.tile_pool(name="shared", bufs=1))
        psum = ctx.enter_context(tc.psum_pool(name="psum", bufs=1))

        def own(shape, dtype, name):
            return keep.tile(shape, dtype, name=name, align_bytes=64)

        def placed(shape, dtype, name, offset):
            return shared.tile(shape, dtype, name=name, offset=offset, align_bytes=64)

        def bank(name, index):
            return psum.tile([P, 512], F32, name=name, offset=index * BANK)

        ts_window = own([P, T], F32, "ts_window")
        nc.sync.dma_start(out=ts_window[P - 1:P, :], in_=ts[0:1, :])
        offsets = lists.tile([P, B * N // 16], U16, name="offsets")
        nc.sync.dma_start(offsets[:], offs)
        nc.vector.memset(ts_window[0:P - 1, :], 0.0)

        pool_rows = cT.rearrange("(r t) c -> r t c", t=4)
        planes = []
        for t in range(4):
            plane = placed([P, T], F32, f"plane{t}", t * PLANE)
            nc.sync.dma_start(out=plane[:], in_=pool_rows[:, t, :])
            planes.append(plane)

        ident = own([P, P], F32, "ident")
        make_identity(nc, ident[:])
        warm = own([P, 1], F32, "warm")
        nc.gpsimd.memset(warm[:], 0.0)
        nc.scalar.activation(out=warm[:], in_=warm[:], func=EXP)

        raw_query = [placed([P, 4, NQ], F32, f"raw_query{b}", QUERIES_AT + 16 * NQ * b) for b in range(B)]
        scaled = placed([P, B * ROW], F32, "scaled", PLANE)
        channels = placed([P, D], F32, "channels", CHANNELS_AT)
        neg_max = [own([P, 1], F32, f"neg_max{b}") for b in range(B)]
        part_sum = own([P, 2], F32, "part_sum")
        row_sum = own([P, B], F32, "row_sum")
        inv_sum = placed([P, B], F32, "inv_sum", LAST_P_AT)
        gathered = own([P, FIRST_KEYS_COL + 4 * HALF], BF16, "gathered")
        second_values = own([P, 4 * N], BF16, "second_values")
        value_codes = [placed([P, D], U32, f"value_codes{b}", (VALUE_CODES_AT, LATE_CODES_AT)[b]) for b in range(B)]
        value_scales = [own([P, D], U8, f"value_scales{b}") for b in range(B)]
        late_values = placed([P, 2 * N], BF16, "late_values", LATE_VALUES_AT)
        first_values = [gathered[:, FIRST_KEYS_COL - 2 * N:FIRST_KEYS_COL], late_values[:]]
        ts_row = own([P, B * N], F32, "ts_row")
        ts_cols = [gathered[:, FIRST_KEYS_COL + N + 32 * b:FIRST_KEYS_COL + N + 32 * b + 8].bitcast(F32) for b in range(B)]
        ts_spread = [own([P, N], F32, f"ts_spread{b}") for b in range(B)]
        query_codes = [own([P, NQ], U32, f"query_codes{b}") for b in range(B)]
        query_scales = [own([P, NQ], U8, f"query_scales{b}") for b in range(B)]
        key_halves = {(0, 0): gathered[:, FIRST_KEYS_COL:], (0, HALF): placed([P, 4 * HALF], BF16, "second_keys", KEYS_AT)[:],
                      (1, 0): scaled[:, 0:N].bitcast(BF16), (1, HALF): own([P, 4 * HALF], BF16, "last_keys")[:]}
        staged_query = [own([P, 4 * NQ], BF16, "staged_query0"), placed([P, 4 * NQ], BF16, "staged_query1", KEYS_AT)]
        key_codes = [own([P, N], U32, "key_codes0"), placed([P, N], U32, "key_codes1", LATE_CODES_AT)]
        key_scales = [own([P, N], U8, f"key_scales{b}") for b in range(B)]
        p = [own([P, N + 1], F32, "p0"), placed([P, N + 1], F32, "p1", LAST_P_AT)]
        ts_by_slot = [own([P, 4], F32, "ts_by_slot0"), placed([P, 4], F32, "ts_by_slot1", RESULT_AT)]
        w_turned = [own([P, 4 * NQ], BF16, "w_turned0"), own([P, 4 * NQ], BF16, "w_turned1")]
        w_codes = [own([P, NQ], U32, f"w_codes{b}") for b in range(B)]
        w_scales = [own([P, NQ], U8, f"w_scales{b}") for b in range(B)]
        result = [placed([P, D], F32, "result0", RESULT_AT), own([P, D], F32, "result1")]
        banks = {}

        def plane_cols(t):
            return gathered[:, PLANE_AT[t]:PLANE_AT[t] + B * N]

        def load_queries_and_sinks():
            for b in range(B):
                nc.sync.dma_start(out=raw_query[b][:], in_=qT[b].rearrange("(r t) q -> r t q", t=4))
            nc.sync.dma_start(out=scaled[:].rearrange("q (b c) -> q b c", b=B)[:, :, N:N + 1], in_=sink.rearrange("b q o -> q b o"))

        def gather_ts():
            nc.vector.tensor_copy(ts_row[:], ts_window[:].indirect(offsets[:]))
            for b in range(B):
                banks["ts", b] = bank(f"ts_turned{b}", b)
                for j in range(4):
                    nc.tensor.transpose(banks["ts", b][:, j * P:(j + 1) * P], ts_row[:, b * N + j:(b + 1) * N:4], ident[:])

        def spread_ts():
            for b in range(B):
                nc.scalar.copy(out=ts_cols[b], in_=banks["ts", b][:, P - 1:512:P])
                nc.scalar.copy(out=ts_by_slot[b][:], in_=banks["ts", b][:, P - 1:512:P])
            for b in range(B):
                rows = bank(f"ts_rows{b}", (3, 0)[b])
                for j in range(4):
                    nc.tensor.transpose(rows[:, j * P:(j + 1) * P], ts_cols[b][:, j:j + 1].to_broadcast([P, P]), ident[:])
                nc.scalar.copy(out=ts_spread[b][:], in_=rows[:])

        def gather_on_vector(t, lo, hi):
            nc.vector.tensor_copy(plane_cols(t)[:, lo:hi], planes[t][:].indirect(offsets[:, lo // 16:hi // 16]))

        def gather_on_scalar(t, lo, hi):
            nc.scalar.activation(plane_cols(t)[:, lo:hi], planes[t][:].indirect(offsets[:, lo // 16:hi // 16]), COPY)

        def turn_values(t, b, rows, place):
            words = plane_cols(t).bitcast(F32)
            for u in range(2):
                k = 2 * place + u
                nc.tensor.transpose(rows[:, k * P:(k + 1) * P], words[:, b * HALF + u:(b + 1) * HALF:2], ident[:])

        def copy_values(b, t, count, rows, place):
            src = rows[:, place * HALF:(place + count) * HALF]
            if b == 0:
                dst = first_values[t // 2].bitcast(F32)[:, t % 2 * HALF:(t % 2 + count) * HALF]
                nc.scalar.copy(out=dst.rearrange("m (t r u) -> m t r u", t=count, u=2), in_=src.rearrange("m (t u r) -> m t r u", t=count, u=2))
            else:
                dst = second_values[:].bitcast(F32).rearrange("m (h t r u) -> m t h r u", h=2, t=4, u=2)[:, t:t + count]
                nc.scalar.copy(out=dst, in_=src.rearrange("m (t u h r) -> m t h r u", t=count, u=2, h=2))

        def quantise_values(b, half):
            cols = slice(half * HALF, (half + 1) * HALF)
            staged = first_values[half] if b == 0 else second_values[:, half * 2 * N:(half + 1) * 2 * N]
            nc.vector.quantize_mx(out=value_codes[b][:, cols].bitcast(FP8X4), scales=value_scales[b][:, cols], in_=staged)

        def copy_query(b, copy):
            dst = staged_query[b][:].rearrange("r (q t) -> r q t", t=4)
            copy(out=dst.rearrange("r (c i) t -> r c t i", i=4), in_=raw_query[b][:].rearrange("r t (c i) -> r c t i", i=4))

        def quantise_query(b):
            nc.vector.quantize_mx(out=query_codes[b][:].bitcast(FP8X4), scales=query_scales[b][:], in_=staged_query[b][:])

        def copy_keys(b, lo, hi, pair, copy):
            first = lo // HALF * HALF
            start, step = PLANE_AT[2 * pair], PLANE_AT[2 * pair + 1] - PLANE_AT[2 * pair]
            two_planes = gathered[:, start:start + 2 * step].rearrange("r (t s) -> r s t", t=2)
            copy(out=key_halves[b, first].rearrange("r (s t) -> r s t", t=4)[:, lo - first:hi - first, 2 * pair:2 * pair + 2],
                 in_=two_planes[:, b * N + lo:b * N + hi])

        def quantise_keys(b, lo):
            nc.vector.quantize_mx(out=key_codes[b][:, lo:lo + HALF].bitcast(FP8X4), scales=key_scales[b][:, lo:lo + HALF],
                                  in_=key_halves[b, lo])

        def score(b, lo, rows):
            banks["scores", b, lo] = rows
            nc.tensor.matmul_mx(rows[:, lo:lo + HALF], lhsT=query_codes[b][:].bitcast(FP8X4), lhsT_scale=query_scales[b][:],
                                rhs=key_codes[b][:, lo:lo + HALF].bitcast(FP8X4), rhs_scale=key_scales[b][:, lo:lo + HALF],
                                start=True, stop=True)

        def scale_scores(b, lo, hi):
            def dealt(row):
                return row.rearrange("q (s m) -> q s m", s=4)[:, :, lo // 4:hi // 4]
            nc.vector.tensor_tensor(out=dealt(scaled[:, b * ROW:b * ROW + N]),
                                    in0=banks["scores", b, lo][:, lo:hi].rearrange("q (m s) -> q s m", s=4),
                                    in1=dealt(ts_spread[b][:]), op=MULT)

        def row_max(b):
            nc.vector.tensor_reduce(out=neg_max[b][:], in_=scaled[:, b * ROW:b * ROW + N + 1], axis=AX, op=MAX, negate=True)

        def exponentials(b):
            for i, (lo, hi) in enumerate(((0, HALF), (HALF, N + 1))):
                nc.scalar.activation(out=p[b][:, lo:hi], in_=scaled[:, b * ROW + lo:b * ROW + hi], func=EXP,
                                     bias=neg_max[b][:], scale=1.0, accum_out=part_sum[:, i:i + 1] if b == 0 else None)

        def add_sums(b):
            if b == 0:
                nc.scalar.activation(out=row_sum[:, 0:1], in_=part_sum[:, 0:1], func=IDENTITY, bias=part_sum[:, 1:2], scale=1.0)
            else:
                nc.scalar.activation(out=scaled[:, ROW:ROW + N + 1], in_=p[1][:], func=IDENTITY, accum_out=row_sum[:, 1:2])

        def turn_p(b, index):
            banks["p", b] = bank(f"p_turned{b}", index)
            for s in range(4):
                nc.tensor.transpose(banks["p", b][:, s * P:(s + 1) * P], p[b][:, s * P:(s + 1) * P], ident[:])

        def weigh(b):
            nc.vector.tensor_tensor(out=w_turned[b][:].rearrange("m (q s) -> m q s", s=4),
                                    in0=banks["p", b][:].rearrange("m (s q) -> m q s", s=4),
                                    in1=ts_by_slot[b][:].unsqueeze(1).to_broadcast([P, NQ, 4]), op=MULT)

        def quantise_w(b):
            nc.vector.quantize_mx(out=w_codes[b][:].bitcast(FP8X4), scales=w_scales[b][:], in_=w_turned[b][:])

        def multiply_values(b, indices):
            width = D // PARTS[b]
            for g, index in enumerate(indices):
                cols = slice(g * width, (g + 1) * width)
                banks["y", b, g] = bank(f"y{b}_{g}", index)
                nc.tensor.matmul_mx(banks["y", b, g][:, 0:width], lhsT=w_codes[b][:].bitcast(FP8X4), lhsT_scale=w_scales[b][:],
                                    rhs=value_codes[b][:, cols].bitcast(FP8X4), rhs_scale=value_scales[b][:, cols],
                                    start=True, stop=True)

        def epilogue(b):
            for h in range(2):
                cols = slice(h * HALF, (h + 1) * HALF)
                if PARTS[b] == 1:
                    sums = banks["y", b, 0][:].rearrange("q (t r) -> q r t", t=4)[:, h * HALF // 4:(h + 1) * HALF // 4]
                else:
                    sums = banks["y", b, h][:, 0:HALF].rearrange("q (t r) -> q r t", t=4)
                nc.vector.scalar_tensor_tensor(
                    out=result[b][:, cols].rearrange("q (r t) -> q r t", t=4), in0=sums,
                    scalar=inv_sum[:, b:b + 1], in1=channels[:, cols].rearrange("q (r t) -> q r t", t=4), op0=MULT, op1=MULT)
                (nc.scalar, nc.sync)[h].dma_start(out=out[b][:, cols], in_=result[b][:, cols])

        gather_ts()
        gather_on_vector(0, 0, B * N)
        rows = bank("plane0_turned", 2)
        for b in range(B):
            turn_values(0, b, rows, b)
        for b in range(B):
            copy_values(b, 0, 1, rows, b)
        spread_ts()
        gather_on_vector(1, 0, HALF)
        gather_on_vector(1, N, B * N)
        gather_on_vector(1, HALF, N)
        load_queries_and_sinks()
        copy_keys(1, 0, HALF, 0, on_vector)
        copy_keys(1, HALF, N, 0, on_vector)
        for b in (0, 1):
            rows = bank(f"plane1_turned{b}", (2, 1)[b])
            turn_values(1, b, rows, 0)
            copy_values(b, 1, 1, rows, 0)
        copy_keys(0, 0, HALF, 0, on_scalar)
        copy_keys(0, HALF, N, 0, on_scalar)
        gather_on_vector(2, 0, B * N)
        late_rows = [bank(f"late_turned{b}", (7, 5)[b]) for b in range(B)]
        for b in range(B):
            turn_values(2, b, late_rows[b], 0)
        quantise_values(0, 0)

        gather_on_vector(3, 0, HALF)
        gather_on_scalar(3, N, N + HALF)
        gather_on_vector(3, HALF, N)
        copy_keys(0, 0, QUARTER, 1, on_scalar)
        copy_keys(0, QUARTER, HALF, 1, on_vector)
        copy_keys(0, HALF, N, 1, on_vector)
        copy_query(0, on_scalar)
        copy_keys(1, 0, HALF, 1, on_scalar)
        turn_values(3, 0, late_rows[0], 1)
        quantise_keys(0, 0)
        quantise_keys(0, HALF)
        quantise_query(0)
        first_scores = bank("scores0", 0)
        score(0, 0, first_scores)
        score(0, HALF, first_scores)

        gather_on_vector(3, N + HALF, B * N)
        nc.sync.dma_start(out=channels[:], in_=ch)
        copy_keys(1, HALF, N, 1, on_scalar)
        turn_values(3, 1, late_rows[1], 1)
        copy_query(1, on_vector)
        quantise_keys(1, 0)
        quantise_query(1)
        score(1, 0, bank("scores1a", 1))
        for b in range(B):
            copy_values(b, 2, 2, late_rows[b], 0)

        scale_scores(0, 0, N)
        quantise_keys(1, HALF)
        score(1, HALF, bank("scores1b", 3))
        row_max(0)
        exponentials(0)
        add_sums(0)
        scale_scores(1, 0, HALF)
        scale_scores(1, HALF, N)
        row_max(1)
        quantise_values(0, 1)
        exponentials(1)
        add_sums(1)
        turn_p(0, 4)
        turn_p(1, 6)
        quantise_values(1, 0)
        weigh(0)
        quantise_values(1, 1)
        quantise_w(0)
        multiply_values(0, (0,))
        weigh(1)
        nc.vector.reciprocal(out=inv_sum[:], in_=row_sum[:])
        quantise_w(1)
        multiply_values(1, (3, 2))
        for b in range(B):
            epilogue(b)
